import numpy as np
import ml_dtypes


def mxq(x, axis, fmt="e4m3"):
    dtype, down = {"e4m3": (ml_dtypes.float8_e4m3fn, 7), "e5m2": (ml_dtypes.float8_e5m2, 14)}[fmt]
    v = np.moveaxis(np.asarray(x, np.float32).astype(ml_dtypes.bfloat16).astype(np.float64), axis, -1)
    blocks = v.reshape(v.shape[:-1] + (-1, 32))
    amax = np.abs(blocks).max(-1, keepdims=True)
    byte = np.maximum(np.where(amax > 0, np.frexp(amax)[1] - 1 + 127, 0) - down, 1)
    scale = np.exp2(byte - 127.0)
    codes = (blocks / scale).astype(np.float32).astype(dtype).astype(np.float64)
    return np.moveaxis((codes * scale).reshape(v.shape), -1, axis)


WIDE = False


def mx_kscale(k):
    if not WIDE:
        return np.ones(k)
    levels = np.array([10, -10, 5, -5, 0])
    if k % 512:
        return np.exp2(np.random.permutation(np.resize(levels, k // 32))).repeat(32)
    a = np.empty((k // 512, 16))
    for p in range(k // 512):
        a[p, :8] = np.random.permutation(np.resize(levels, 8))
        for g in range(8):
            far = levels[np.abs(levels - a[p, g]) >= 10]
            a[p, g + 8] = far[np.random.randint(len(far))]
    return np.exp2(a.ravel()).repeat(32)


def f64(x):
    return np.asarray(x).astype(np.float64)


def striped(idx):
    return np.tile(idx.reshape(-1, 16).T, (8, 1)).astype(np.uint16)


def unstriped(offs):
    return offs[:16].T.reshape(-1).astype(np.int64)


E2M1 = np.array([0.0, 0.5, 1.0, 1.5, 2.0, 3.0, 4.0, 6.0, -0.0, -0.5, -1.0, -1.5, -2.0, -3.0, -4.0, -6.0])


def pack_weight(w, fmt):
    k, n = w.shape
    w = f64(np.asarray(w, np.float32).astype(ml_dtypes.bfloat16)).reshape(k // 32, 32, n)
    amax = np.abs(w).max(1)
    if fmt == "e4m3":
        byte = np.frexp(amax)[1] - 1 + 127 - 7
    else:
        mant, ex = np.frexp(amax / 6.0)
        byte = np.where(mant > 0.5, ex, ex - 1) + 127
    byte = np.clip(np.where(amax > 0, byte, 1), 1, 254)
    scaled = (w * np.exp2(127.0 - byte)[:, None, :]).reshape(k, n).astype(np.float32)
    by_word = np.ascontiguousarray(scaled.reshape(k // 512, 128, 4, n).transpose(0, 1, 3, 2))
    if fmt == "e4m3":
        words = by_word.astype(ml_dtypes.float8_e4m3fn).view(np.uint8)
    else:
        c = by_word.astype(ml_dtypes.float4_e2m1fn).view(np.uint8) & 0xF
        words = (c[..., 0::2] | (c[..., 1::2] << 4)).reshape(k // 512, 128, 2 * n)
    return np.ascontiguousarray(words), np.ascontiguousarray(byte.astype(np.uint8).reshape(k // 512, 16, n))


def unpack_weight(words, scales, fmt):
    g, _, n = scales.shape
    words = np.ascontiguousarray(words).reshape(g, 128, n, -1)
    if fmt == "e4m3":
        vals = words.view(ml_dtypes.float8_e4m3fn).astype(np.float64)
    else:
        nib = np.empty((g, 128, n, 4), np.uint8)
        nib[..., 0::2] = words & 0xF
        nib[..., 1::2] = words >> 4
        vals = E2M1[nib]
    vals = vals * np.repeat(np.exp2(scales.astype(np.float64) - 127.0), 8, axis=1)[..., None]
    return vals.transpose(0, 1, 3, 2).reshape(g * 512, n)


def gelu(v):
    return 0.5 * v * (1.0 + np.tanh(np.sqrt(2.0 / np.pi) * (v + 0.044715 * v**3)))


G, K, M, T, S = 2, 512, 1024, 1024, 256


def setup_inputs():
    n = np.random.standard_normal
    s = mx_kscale(K)[:, None]
    p_w4 = pack_weight(n((K, M)) / np.sqrt(K) / s, "e2m1")
    p_w8 = pack_weight(n((K, M)) / np.sqrt(K) / s, "e4m3")
    return {
        "xT": (n((K, T)) * s).astype(np.float32),
        "c": (n((K, S)) * s).astype(np.float32),
        "w4_words": p_w4[0],
        "w4_scales": p_w4[1],
        "w8_words": p_w8[0],
        "w8_scales": p_w8[1],
        "b": (0.3 * n(1024)).astype(np.float32),
        "offs": striped(np.concatenate([np.random.permutation(T)[:S] for _ in range(G)])),
    }


def reference(xT, c, w4_words, w4_scales, w8_words, w8_scales, b, offs):
    idx = unstriped(offs).reshape(G, S)
    xm_ = mxq(np.max([f64(xT)[:, idx[g]] for g in range(G)], axis=0), 0, "e4m3")
    c_ = mxq(f64(c), 0, "e4m3")
    w4_ = unpack_weight(w4_words, w4_scales, "e2m1")
    w8_ = unpack_weight(w8_words, w8_scales, "e4m3")
    y = w4_.T @ xm_ + w8_.T @ c_
    return gelu(y + f64(b)[:, None])

@@ -1,0 +1,157 @@
+from contextlib import ExitStack
+
+import concourse.mybir as mybir
+
+G, K, M, T, S = 2, 512, 1024, 1024, 256
+FLOPS = 2 * 2 * K * M * S
+
+F32 = mybir.dt.float32
+BF16 = mybir.dt.bfloat16
+I32 = mybir.dt.int32
+U32 = mybir.dt.uint32
+U16 = mybir.dt.uint16
+U8 = mybir.dt.uint8
+FP8X4 = mybir.dt.float8_e4m3fn_x4
+FP4X4 = mybir.dt.float4_e2m1fn_x4
+GELU = mybir.ActivationFunctionType.Gelu_apprx_tanh
+
+P = 128
+PACK = 4
+N = 128
+HALVES = S // N
+TILES = M // P
+CHUNKS = 2
+TILES_PER_CHUNK = TILES // CHUNKS
+CHUNK = M // CHUNKS
+LIST_ROWS = 16
+
+
+def tile_list_sage_gelu_kernel(
+    tc, xT, c, w4_words, w4_scales, w8_words, w8_scales, b, offs, out
+):
+    nc = tc.nc
+    with ExitStack() as ctx:
+        pool = ctx.enter_context(tc.tile_pool(name="held", bufs=1))
+        psum = ctx.enter_context(tc.psum_pool(name="psum", bufs=1))
+
+        offsets = pool.tile([P, G * S // LIST_ROWS], U16, name="offsets")
+        x_rows = [pool.tile([P, T], F32, name="x_rows%d" % i, align_bytes=64) for i in range(PACK)]
+        c_raw = pool.tile([P, PACK, S], F32, name="c_raw", align_bytes=64)
+        w8 = [pool.tile([P, CHUNK], U32, name="w8_%d" % a, align_bytes=64) for a in range(CHUNKS)]
+        w4 = [pool.tile([P, 2 * CHUNK], U8, name="w4_%d" % a, align_bytes=64) for a in range(CHUNKS)]
+        w_scales = pool.tile([P, 2, M], U8, name="w_scales", align_bytes=64)
+        picked = pool.tile([P, PACK, G * S], F32, name="picked", align_bytes=64)
+        bias_rows = pool.tile([P, 32], F32, name="bias_rows", align_bytes=64)
+        bias = pool.tile([P, 32], F32, name="bias", align_bytes=64)
+        warm = pool.tile([P, 2], F32, name="warm", align_bytes=64)
+        banks = [psum.tile([P, 512], F32, name="bank%d" % i) for i in range(8)]
+
+        nc.vector.memset(bias_rows[:], 0.0)
+        nc.vector.memset(warm[:, 0:1], 0.0)
+        nc.vector.memset(w_scales[:].rearrange("p a n -> p (a n)").bitcast(U32), 0)
+        nc.scalar.dma_start(bias_rows[0:P:4, :], b.rearrange("(m q r) -> q m r", q=4, r=32))
+        nc.scalar.activation(warm[:, 1:2], warm[:, 0:1], GELU)
+
+        def load_scales(which, quadrant):
+            src = (w8_scales, w4_scales)[which]
+            nc.sync.dma_start(
+                w_scales[32 * quadrant : 32 * quadrant + 4, which, :].bitcast(I32),
+                src[0, 4 * quadrant : 4 * quadrant + 4, :].bitcast(I32),
+            )
+
+        def load_w8(a):
+            src = w8_words[0].rearrange("p n t -> p (n t)")
+            nc.sync.dma_start(w8[a][:].bitcast(I32), src[:, 4 * CHUNK * a : 4 * CHUNK * (a + 1)].bitcast(I32))
+
+        def load_w4(a):
+            nc.sync.dma_start(w4[a][:].bitcast(I32), w4_words[0][:, 2 * CHUNK * a : 2 * CHUNK * (a + 1)].bitcast(I32))
+
+        nc.sync.dma_start(offsets[:], offs)
+        x_view = xT.rearrange("(p i) t -> p i t", i=PACK)
+        for i in range(PACK):
+            nc.sync.dma_start(x_rows[i][:], x_view[:, i, :])
+        for quadrant in range(3):
+            load_scales(0, quadrant)
+        nc.sync.dma_start(c_raw[:], c.rearrange("(p i) j -> p i j", i=PACK))
+        load_scales(0, 3)
+        load_w8(0)
+        for quadrant in range(4):
+            load_scales(1, quadrant)
+        load_w4(0)
+        load_w8(1)
+        load_w4(1)
+
+        nc.vector.transpose(bias[:], bias_rows[:])
+
+        for i in range(PACK - 1):
+            nc.vector.tensor_copy(picked[:, i, :], x_rows[i][:].indirect(offsets[:]))
+
+        out_view = out.rearrange("(m p) j -> p m j", p=P)
+        cols = N // LIST_ROWS
+        for h in range(HALVES):
+            c_bf = pool.tile([P, N, PACK], BF16, name="c_bf%d" % h, align_bytes=64)
+            c_codes = pool.tile([P, N], U32, name="c_codes%d" % h, align_bytes=64)
+            c_scale = pool.tile([P, N], U8, name="c_scale%d" % h, align_bytes=64)
+            x_bf = pool.tile([P, N, PACK], BF16, name="x_bf%d" % h, align_bytes=64)
+            x_codes = pool.tile([P, N], U32, name="x_codes%d" % h, align_bytes=64)
+            x_scale = pool.tile([P, N], U8, name="x_scale%d" % h, align_bytes=64)
+
+            nc.scalar.copy(
+                c_bf[:].rearrange("p (u v) i -> p u i v", v=4),
+                c_raw[:, :, h * N : (h + 1) * N].rearrange("p i (u v) -> p u i v", v=4),
+            )
+            for g in range(G):
+                first = g * S + h * N
+                nc.vector.tensor_copy(
+                    picked[:, PACK - 1, first : first + N],
+                    x_rows[PACK - 1][:].indirect(offsets[:, first // LIST_ROWS : first // LIST_ROWS + cols]),
+                )
+            nc.vector.tensor_max(
+                x_bf[:].rearrange("p (u v) i -> p u i v", v=4),
+                picked[:, :, h * N : (h + 1) * N].rearrange("p i (u v) -> p u i v", v=4),
+                picked[:, :, S + h * N : S + (h + 1) * N].rearrange("p i (u v) -> p u i v", v=4),
+            )
+            nc.vector.quantize_mx(
+                out=c_codes[:].bitcast(FP8X4), scales=c_scale[:], in_=c_bf[:].rearrange("p j i -> p (j i)")
+            )
+            nc.vector.quantize_mx(
+                out=x_codes[:].bitcast(FP8X4), scales=x_scale[:], in_=x_bf[:].rearrange("p j i -> p (j i)")
+            )
+
+            for a in range(CHUNKS):
+                res = pool.tile([P, TILES_PER_CHUNK, N], F32, name="res%d_%d" % (h, a), align_bytes=64)
+                for pair in range(TILES_PER_CHUNK // 2):
+                    bank = banks[4 * h + 2 * a + pair]
+                    for e in range(2):
+                        local = 2 * pair + e
+                        m = a * TILES_PER_CHUNK + local
+                        nc.tensor.matmul_mx(
+                            out=bank[:, e * N : (e + 1) * N],
+                            lhsT=w8[a][:, local * P : (local + 1) * P].bitcast(FP8X4),
+                            lhsT_scale=w_scales[:, 0, m * P : (m + 1) * P],
+                            rhs=c_codes[:].bitcast(FP8X4),
+                            rhs_scale=c_scale[:],
+                            start=(e == 0),
+                            stop=False,
+                        )
+                    for e in range(2):
+                        local = 2 * pair + e
+                        m = a * TILES_PER_CHUNK + local
+                        nc.tensor.matmul_mx(
+                            out=bank[:, e * N : (e + 1) * N],
+                            lhsT=w4[a][:, 2 * local * P : 2 * (local + 1) * P].bitcast(FP4X4),
+                            lhsT_scale=w_scales[:, 1, m * P : (m + 1) * P],
+                            rhs=x_codes[:].bitcast(FP8X4),
+                            rhs_scale=x_scale[:],
+                            start=False,
+                            stop=(e == 1),
+                        )
+                    for e in range(2):
+                        local = 2 * pair + e
+                        m = a * TILES_PER_CHUNK + local
+                        nc.scalar.activation(
+                            res[:, local, :], bank[:, e * N : (e + 1) * N], GELU, bias=bias[:, 4 * m : 4 * m + 1]
+                        )
+                nc.sync.dma_start(
+                    out_view[:, a * TILES_PER_CHUNK : (a + 1) * TILES_PER_CHUNK, h * N : (h + 1) * N], res[:]
+                )

@@ -42,15 +42,17 @@ def tile_list_sage_gelu_kernel(
         w_scales = pool.tile([P, 2, M], U8, name="w_scales", align_bytes=64)
         picked = pool.tile([P, PACK, G * S], F32, name="picked", align_bytes=64)
         bias_rows = pool.tile([P, 32], F32, name="bias_rows", align_bytes=64)
-        bias = pool.tile([P, 32], F32, name="bias", align_bytes=64)
+        bias_all = pool.tile([P, 32], F32, name="bias_all", align_bytes=64)
+        bias = pool.tile([P, TILES], F32, name="bias", align_bytes=64)
+        zeros = pool.tile([P, P], F32, name="zeros", align_bytes=64)
+        staged = pool.tile([P, 3, N, PACK], BF16, name="staged", align_bytes=64)
         warm = pool.tile([P, 2], F32, name="warm", align_bytes=64)
         banks = [psum.tile([P, 512], F32, name="bank%d" % i) for i in range(8)]
 
-        nc.vector.memset(bias_rows[:], 0.0)
-        nc.vector.memset(warm[:, 0:1], 0.0)
+        nc.scalar.dma_start(bias_rows[:], b.rearrange("(a r) -> a r", r=32).unsqueeze(0).broadcast_to([4, 32, 32]))
+        nc.vector.memset(zeros[:], 0.0)
         nc.vector.memset(w_scales[:].rearrange("p a n -> p (a n)").bitcast(U32), 0)
-        nc.scalar.dma_start(bias_rows[0:P:4, :], b.rearrange("(m q r) -> q m r", q=4, r=32))
-        nc.scalar.activation(warm[:, 1:2], warm[:, 0:1], GELU)
+        nc.scalar.activation(warm[:, 0:1], zeros[:, 0:1], GELU)
 
         def load_scales(which, quadrant):
             src = (w8_scales, w4_scales)[which]
@@ -66,40 +68,59 @@ def tile_list_sage_gelu_kernel(
         def load_w4(a):
             nc.sync.dma_start(w4[a][:].bitcast(I32), w4_words[0][:, 2 * CHUNK * a : 2 * CHUNK * (a + 1)].bitcast(I32))
 
-        nc.sync.dma_start(offsets[:], offs)
         x_view = xT.rearrange("(p i) t -> p i t", i=PACK)
-        for i in range(PACK):
-            nc.sync.dma_start(x_rows[i][:], x_view[:, i, :])
-        for quadrant in range(3):
+        nc.sync.dma_start(offsets[:], offs)
+        nc.sync.dma_start(x_rows[0][:], x_view[:, 0, :])
+        nc.sync.dma_start(x_rows[1][:], x_view[:, 1, :])
+        for quadrant in range(4):
             load_scales(0, quadrant)
-        nc.sync.dma_start(c_raw[:], c.rearrange("(p i) j -> p i j", i=PACK))
-        load_scales(0, 3)
-        load_w8(0)
+        nc.sync.dma_start(x_rows[2][:], x_view[:, 2, :])
+        nc.sync.dma_start(x_rows[3][:], x_view[:, 3, :])
         for quadrant in range(4):
             load_scales(1, quadrant)
-        load_w4(0)
-        load_w8(1)
-        load_w4(1)
+        nc.sync.dma_start(c_raw[:], c.rearrange("(p i) j -> p i j", i=PACK))
+        for a in range(CHUNKS):
+            load_w4(a)
+            load_w8(a)
 
-        nc.vector.transpose(bias[:], bias_rows[:])
+        nc.vector.transpose(bias_all[:], bias_rows[:])
+        for quadrant in range(4):
+            rows = slice(32 * quadrant, 32 * (quadrant + 1))
+            nc.scalar.copy(bias[rows, :], bias_all[rows, quadrant:32:4])
+
+        c_flat = c_raw[:].rearrange("p i j -> p (i j)")
+        for source in (x_rows[2][:], x_rows[3][:], c_flat):
+            for block in range(8):
+                nc.tensor.transpose(
+                    banks[4 + block % 4][:, 256 + (block // 4) * P : 256 + (block // 4 + 1) * P],
+                    source[:, block * P : (block + 1) * P],
+                    zeros[:],
+                )
 
         for i in range(PACK - 1):
             nc.vector.tensor_copy(picked[:, i, :], x_rows[i][:].indirect(offsets[:]))
 
         out_view = out.rearrange("(m p) j -> p m j", p=P)
         cols = N // LIST_ROWS
+
+        def quantize(codes, scale, values):
+            nc.vector.quantize_mx(out=codes.bitcast(FP8X4), scales=scale, in_=values.rearrange("p j i -> p (j i)"))
+
+        c_mx = []
         for h in range(HALVES):
-            c_bf = pool.tile([P, N, PACK], BF16, name="c_bf%d" % h, align_bytes=64)
             c_codes = pool.tile([P, N], U32, name="c_codes%d" % h, align_bytes=64)
             c_scale = pool.tile([P, N], U8, name="c_scale%d" % h, align_bytes=64)
-            x_bf = pool.tile([P, N, PACK], BF16, name="x_bf%d" % h, align_bytes=64)
-            x_codes = pool.tile([P, N], U32, name="x_codes%d" % h, align_bytes=64)
-            x_scale = pool.tile([P, N], U8, name="x_scale%d" % h, align_bytes=64)
-
+            c_mx.append((c_codes[:], c_scale[:]))
             nc.scalar.copy(
-                c_bf[:].rearrange("p (u v) i -> p u i v", v=4),
+                staged[:, 1 + h].rearrange("p (u v) i -> p u i v", v=4),
                 c_raw[:, :, h * N : (h + 1) * N].rearrange("p i (u v) -> p u i v", v=4),
             )
+
+        for h in range(HALVES):
+            x_bf = staged[:, h]
+            c_codes, c_scale = c_mx[h]
+            x_codes = pool.tile([P, N], U32, name="x_codes%d" % h, align_bytes=64)[:]
+            x_scale = pool.tile([P, N], U8, name="x_scale%d" % h, align_bytes=64)[:]
             for g in range(G):
                 first = g * S + h * N
                 nc.vector.tensor_copy(
@@ -107,51 +128,50 @@ def tile_list_sage_gelu_kernel(
                     x_rows[PACK - 1][:].indirect(offsets[:, first // LIST_ROWS : first // LIST_ROWS + cols]),
                 )
             nc.vector.tensor_max(
-                x_bf[:].rearrange("p (u v) i -> p u i v", v=4),
+                x_bf.rearrange("p (u v) i -> p u i v", v=4),
                 picked[:, :, h * N : (h + 1) * N].rearrange("p i (u v) -> p u i v", v=4),
                 picked[:, :, S + h * N : S + (h + 1) * N].rearrange("p i (u v) -> p u i v", v=4),
             )
-            nc.vector.quantize_mx(
-                out=c_codes[:].bitcast(FP8X4), scales=c_scale[:], in_=c_bf[:].rearrange("p j i -> p (j i)")
-            )
-            nc.vector.quantize_mx(
-                out=x_codes[:].bitcast(FP8X4), scales=x_scale[:], in_=x_bf[:].rearrange("p j i -> p (j i)")
-            )
+            quantize(x_codes, x_scale, x_bf)
+            if h == 0:
+                for hc in range(HALVES):
+                    quantize(c_mx[hc][0], c_mx[hc][1], staged[:, 1 + hc])
 
             for a in range(CHUNKS):
                 res = pool.tile([P, TILES_PER_CHUNK, N], F32, name="res%d_%d" % (h, a), align_bytes=64)
                 for pair in range(TILES_PER_CHUNK // 2):
                     bank = banks[4 * h + 2 * a + pair]
-                    for e in range(2):
-                        local = 2 * pair + e
-                        m = a * TILES_PER_CHUNK + local
-                        nc.tensor.matmul_mx(
-                            out=bank[:, e * N : (e + 1) * N],
-                            lhsT=w8[a][:, local * P : (local + 1) * P].bitcast(FP8X4),
-                            lhsT_scale=w_scales[:, 0, m * P : (m + 1) * P],
-                            rhs=c_codes[:].bitcast(FP8X4),
-                            rhs_scale=c_scale[:],
-                            start=(e == 0),
-                            stop=False,
-                        )
-                    for e in range(2):
-                        local = 2 * pair + e
-                        m = a * TILES_PER_CHUNK + local
-                        nc.tensor.matmul_mx(
-                            out=bank[:, e * N : (e + 1) * N],
-                            lhsT=w4[a][:, 2 * local * P : 2 * (local + 1) * P].bitcast(FP4X4),
-                            lhsT_scale=w_scales[:, 1, m * P : (m + 1) * P],
-                            rhs=x_codes[:].bitcast(FP8X4),
-                            rhs_scale=x_scale[:],
-                            start=False,
-                            stop=(e == 1),
-                        )
+                    for step in range(2):
+                        for e in range(2):
+                            local = 2 * pair + e
+                            m = a * TILES_PER_CHUNK + local
+                            if step == h:
+                                lhsT = w4[a][:, 2 * local * P : 2 * (local + 1) * P].bitcast(FP4X4)
+                                plane, rhs, rhs_scale = 1, x_codes, x_scale
+                            else:
+                                lhsT = w8[a][:, local * P : (local + 1) * P].bitcast(FP8X4)
+                                plane, rhs, rhs_scale = 0, c_codes, c_scale
+                            nc.tensor.matmul_mx(
+                                out=bank[:, e * N : (e + 1) * N],
+                                lhsT=lhsT,
+                                lhsT_scale=w_scales[:, plane, m * P : (m + 1) * P],
+                                rhs=rhs.bitcast(FP8X4),
+                                rhs_scale=rhs_scale,
+                                start=(step == 0 and e == 0),
+                                stop=(step == 1 and e == 1),
+                            )
                     for e in range(2):
                         local = 2 * pair + e
                         m = a * TILES_PER_CHUNK + local
                         nc.scalar.activation(
-                            res[:, local, :], bank[:, e * N : (e + 1) * N], GELU, bias=bias[:, 4 * m : 4 * m + 1]
+                            res[:, local, :], bank[:, e * N : (e + 1) * N], GELU, bias=bias[:, m : m + 1]
                         )
-                nc.sync.dma_start(
-                    out_view[:, a * TILES_PER_CHUNK : (a + 1) * TILES_PER_CHUNK, h * N : (h + 1) * N], res[:]
-                )
+                    if (h, a) == (HALVES - 1, CHUNKS - 1):
+                        first = a * TILES_PER_CHUNK + 2 * pair
+                        nc.sync.dma_start(
+                            out_view[:, first : first + 2, h * N : (h + 1) * N], res[:, 2 * pair : 2 * pair + 2, :]
+                        )
+                if (h, a) != (HALVES - 1, CHUNKS - 1):
+                    nc.sync.dma_start(
+                        out_view[:, a * TILES_PER_CHUNK : (a + 1) * TILES_PER_CHUNK, h * N : (h + 1) * N], res[:]
+                    )

@@ -24,6 +24,7 @@ CHUNKS = 2
 TILES_PER_CHUNK = TILES // CHUNKS
 CHUNK = M // CHUNKS
 LIST_ROWS = 16
+W8_PLANE_ROW = 4
 
 
 def tile_list_sage_gelu_kernel(
@@ -38,58 +39,42 @@ def tile_list_sage_gelu_kernel(
         x_rows = [pool.tile([P, T], F32, name="x_rows%d" % i, align_bytes=64) for i in range(PACK)]
         c_raw = pool.tile([P, PACK, S], F32, name="c_raw", align_bytes=64)
         w8 = [pool.tile([P, CHUNK], U32, name="w8_%d" % a, align_bytes=64) for a in range(CHUNKS)]
-        w4 = [pool.tile([P, 2 * CHUNK], U8, name="w4_%d" % a, align_bytes=64) for a in range(CHUNKS)]
-        w_scales = pool.tile([P, 2, M], U8, name="w_scales", align_bytes=64)
+        w4 = pool.tile([P, 2 * M], U8, name="w4", align_bytes=64)
+        w4_plane = pool.tile([P, M], U8, name="w4_plane", align_bytes=64)
+        w8_plane = pool.tile([P, M], U8, name="w8_plane", align_bytes=64)
         picked = pool.tile([P, PACK, G * S], F32, name="picked", align_bytes=64)
         bias_rows = pool.tile([P, 32], F32, name="bias_rows", align_bytes=64)
-        bias_all = pool.tile([P, 32], F32, name="bias_all", align_bytes=64)
-        bias = pool.tile([P, TILES], F32, name="bias", align_bytes=64)
         zeros = pool.tile([P, P], F32, name="zeros", align_bytes=64)
         staged = pool.tile([P, 3, N, PACK], BF16, name="staged", align_bytes=64)
         warm = pool.tile([P, 2], F32, name="warm", align_bytes=64)
         banks = [psum.tile([P, 512], F32, name="bank%d" % i) for i in range(8)]
 
-        nc.scalar.dma_start(bias_rows[:], b.rearrange("(a r) -> a r", r=32).unsqueeze(0).broadcast_to([4, 32, 32]))
+        nc.vector.memset(bias_rows[:], 0.0)
+        nc.vector.memset(w8_plane[:].bitcast(U32), 0)
+        nc.gpsimd.dma_start(bias_rows[0:P:4, :], b.rearrange("(m q r) -> q m r", q=4, r=32))
+        nc.vector.memset(w4_plane[:].bitcast(U32), 0)
         nc.vector.memset(zeros[:], 0.0)
-        nc.vector.memset(w_scales[:].rearrange("p a n -> p (a n)").bitcast(U32), 0)
         nc.scalar.activation(warm[:, 0:1], zeros[:, 0:1], GELU)
 
-        def load_scales(which, quadrant):
-            src = (w8_scales, w4_scales)[which]
-            nc.sync.dma_start(
-                w_scales[32 * quadrant : 32 * quadrant + 4, which, :].bitcast(I32),
-                src[0, 4 * quadrant : 4 * quadrant + 4, :].bitcast(I32),
-            )
+        def load_scales(engine, plane, first, src):
+            rows = src[0].rearrange("(q r) n -> r q n", r=4)
+            for r in range(4):
+                engine.dma_start(plane[first + r : P : 32, :].bitcast(I32), rows[r].bitcast(I32))
 
-        def load_w8(a):
-            src = w8_words[0].rearrange("p n t -> p (n t)")
-            nc.sync.dma_start(w8[a][:].bitcast(I32), src[:, 4 * CHUNK * a : 4 * CHUNK * (a + 1)].bitcast(I32))
-
-        def load_w4(a):
-            nc.sync.dma_start(w4[a][:].bitcast(I32), w4_words[0][:, 2 * CHUNK * a : 2 * CHUNK * (a + 1)].bitcast(I32))
+        load_scales(nc.gpsimd, w8_plane, W8_PLANE_ROW, w8_scales)
 
         x_view = xT.rearrange("(p i) t -> p i t", i=PACK)
         nc.sync.dma_start(offsets[:], offs)
-        nc.sync.dma_start(x_rows[0][:], x_view[:, 0, :])
-        nc.sync.dma_start(x_rows[1][:], x_view[:, 1, :])
-        for quadrant in range(4):
-            load_scales(0, quadrant)
-        nc.sync.dma_start(x_rows[2][:], x_view[:, 2, :])
-        nc.sync.dma_start(x_rows[3][:], x_view[:, 3, :])
-        for quadrant in range(4):
-            load_scales(1, quadrant)
+        for i in range(PACK):
+            nc.sync.dma_start(x_rows[i][:], x_view[:, i, :])
         nc.sync.dma_start(c_raw[:], c.rearrange("(p i) j -> p i j", i=PACK))
+        load_scales(nc.sync, w4_plane, 0, w4_scales)
+        nc.sync.dma_start(w4[:].bitcast(I32), w4_words[0].bitcast(I32))
+        w8_bytes = w8_words[0].rearrange("p n t -> p (n t)")
         for a in range(CHUNKS):
-            load_w4(a)
-            load_w8(a)
+            nc.sync.dma_start(w8[a][:].bitcast(I32), w8_bytes[:, 4 * CHUNK * a : 4 * CHUNK * (a + 1)].bitcast(I32))
 
-        nc.vector.transpose(bias_all[:], bias_rows[:])
-        for quadrant in range(4):
-            rows = slice(32 * quadrant, 32 * (quadrant + 1))
-            nc.scalar.copy(bias[rows, :], bias_all[rows, quadrant:32:4])
-
-        c_flat = c_raw[:].rearrange("p i j -> p (i j)")
-        for source in (x_rows[2][:], x_rows[3][:], c_flat):
+        for source in (x_rows[2], x_rows[3]):
             for block in range(8):
                 nc.tensor.transpose(
                     banks[4 + block % 4][:, 256 + (block // 4) * P : 256 + (block // 4 + 1) * P],
@@ -106,6 +91,7 @@ def tile_list_sage_gelu_kernel(
         def quantize(codes, scale, values):
             nc.vector.quantize_mx(out=codes.bitcast(FP8X4), scales=scale, in_=values.rearrange("p j i -> p (j i)"))
 
+        bias = picked[:, 0, 0:32]
         c_mx = []
         for h in range(HALVES):
             c_codes = pool.tile([P, N], U32, name="c_codes%d" % h, align_bytes=64)
@@ -132,6 +118,8 @@ def tile_list_sage_gelu_kernel(
                 picked[:, :, h * N : (h + 1) * N].rearrange("p i (u v) -> p u i v", v=4),
                 picked[:, :, S + h * N : S + (h + 1) * N].rearrange("p i (u v) -> p u i v", v=4),
             )
+            if h == 0:
+                nc.vector.transpose(bias, bias_rows[:])
             quantize(x_codes, x_scale, x_bf)
             if h == 0:
                 for hc in range(HALVES):
@@ -146,15 +134,15 @@ def tile_list_sage_gelu_kernel(
                             local = 2 * pair + e
                             m = a * TILES_PER_CHUNK + local
                             if step == h:
-                                lhsT = w4[a][:, 2 * local * P : 2 * (local + 1) * P].bitcast(FP4X4)
-                                plane, rhs, rhs_scale = 1, x_codes, x_scale
+                                lhsT = w4[:, 2 * m * P : 2 * (m + 1) * P].bitcast(FP4X4)
+                                plane, rhs, rhs_scale = w4_plane[:, m * P : (m + 1) * P], x_codes, x_scale
                             else:
                                 lhsT = w8[a][:, local * P : (local + 1) * P].bitcast(FP8X4)
-                                plane, rhs, rhs_scale = 0, c_codes, c_scale
+                                plane, rhs, rhs_scale = w8_plane[W8_PLANE_ROW:P, m * P : (m + 1) * P], c_codes, c_scale
                             nc.tensor.matmul_mx(
                                 out=bank[:, e * N : (e + 1) * N],
                                 lhsT=lhsT,
-                                lhsT_scale=w_scales[:, plane, m * P : (m + 1) * P],
+                                lhsT_scale=plane,
                                 rhs=rhs.bitcast(FP8X4),
                                 rhs_scale=rhs_scale,
                                 start=(step == 0 and e == 0),
@@ -164,7 +152,7 @@ def tile_list_sage_gelu_kernel(
                         local = 2 * pair + e
                         m = a * TILES_PER_CHUNK + local
                         nc.scalar.activation(
-                            res[:, local, :], bank[:, e * N : (e + 1) * N], GELU, bias=bias[:, m : m + 1]
+                            res[:, local, :], bank[:, e * N : (e + 1) * N], GELU, bias=bias[:, 4 * m : 4 * m + 1]
                         )
                     if (h, a) == (HALVES - 1, CHUNKS - 1):
                         first = a * TILES_PER_CHUNK + 2 * pair

@@ -44,7 +44,6 @@ def tile_list_sage_gelu_kernel(
         w8_plane = pool.tile([P, M], U8, name="w8_plane", align_bytes=64)
         picked = pool.tile([P, PACK, G * S], F32, name="picked", align_bytes=64)
         bias_rows = pool.tile([P, 32], F32, name="bias_rows", align_bytes=64)
-        zeros = pool.tile([P, P], F32, name="zeros", align_bytes=64)
         staged = pool.tile([P, 3, N, PACK], BF16, name="staged", align_bytes=64)
         warm = pool.tile([P, 2], F32, name="warm", align_bytes=64)
         banks = [psum.tile([P, 512], F32, name="bank%d" % i) for i in range(8)]
@@ -53,8 +52,8 @@ def tile_list_sage_gelu_kernel(
         nc.vector.memset(w8_plane[:].bitcast(U32), 0)
         nc.gpsimd.dma_start(bias_rows[0:P:4, :], b.rearrange("(m q r) -> q m r", q=4, r=32))
         nc.vector.memset(w4_plane[:].bitcast(U32), 0)
-        nc.vector.memset(zeros[:], 0.0)
-        nc.scalar.activation(warm[:, 0:1], zeros[:, 0:1], GELU)
+        nc.vector.memset(warm[:, 0:1], 0.0)
+        nc.scalar.activation(warm[:, 1:2], warm[:, 0:1], GELU)
 
         def load_scales(engine, plane, first, src):
             rows = src[0].rearrange("(q r) n -> r q n", r=4)
@@ -64,23 +63,16 @@ def tile_list_sage_gelu_kernel(
         load_scales(nc.gpsimd, w8_plane, W8_PLANE_ROW, w8_scales)
 
         x_view = xT.rearrange("(p i) t -> p i t", i=PACK)
-        nc.sync.dma_start(offsets[:], offs)
         for i in range(PACK):
             nc.sync.dma_start(x_rows[i][:], x_view[:, i, :])
+            if i == 0:
+                nc.sync.dma_start(offsets[:], offs)
         nc.sync.dma_start(c_raw[:], c.rearrange("(p i) j -> p i j", i=PACK))
         load_scales(nc.sync, w4_plane, 0, w4_scales)
         nc.sync.dma_start(w4[:].bitcast(I32), w4_words[0].bitcast(I32))
         w8_bytes = w8_words[0].rearrange("p n t -> p (n t)")
         for a in range(CHUNKS):
             nc.sync.dma_start(w8[a][:].bitcast(I32), w8_bytes[:, 4 * CHUNK * a : 4 * CHUNK * (a + 1)].bitcast(I32))
-
-        for source in (x_rows[2], x_rows[3]):
-            for block in range(8):
-                nc.tensor.transpose(
-                    banks[4 + block % 4][:, 256 + (block // 4) * P : 256 + (block // 4 + 1) * P],
-                    source[:, block * P : (block + 1) * P],
-                    zeros[:],
-                )
 
         for i in range(PACK - 1):
             nc.vector.tensor_copy(picked[:, i, :], x_rows[i][:].indirect(offsets[:]))
@@ -98,8 +90,8 @@ def tile_list_sage_gelu_kernel(
             c_scale = pool.tile([P, N], U8, name="c_scale%d" % h, align_bytes=64)
             c_mx.append((c_codes[:], c_scale[:]))
             nc.scalar.copy(
-                staged[:, 1 + h].rearrange("p (u v) i -> p u i v", v=4),
-                c_raw[:, :, h * N : (h + 1) * N].rearrange("p i (u v) -> p u i v", v=4),
+                staged[:, 1 + h],
+                c_raw[:, :, h * N : (h + 1) * N].rearrange("p i j -> p j i"),
             )
 
         for h in range(HALVES):
@@ -114,9 +106,9 @@ def tile_list_sage_gelu_kernel(
                     x_rows[PACK - 1][:].indirect(offsets[:, first // LIST_ROWS : first // LIST_ROWS + cols]),
                 )
             nc.vector.tensor_max(
-                x_bf.rearrange("p (u v) i -> p u i v", v=4),
-                picked[:, :, h * N : (h + 1) * N].rearrange("p i (u v) -> p u i v", v=4),
-                picked[:, :, S + h * N : S + (h + 1) * N].rearrange("p i (u v) -> p u i v", v=4),
+                x_bf,
+                picked[:, :, h * N : (h + 1) * N].rearrange("p i j -> p j i"),
+                picked[:, :, S + h * N : S + (h + 1) * N].rearrange("p i j -> p j i"),
             )
             if h == 0:
                 nc.vector.transpose(bias, bias_rows[:])

@@ -1,6 +1,7 @@
 from contextlib import ExitStack
 
 import concourse.mybir as mybir
+from concourse.masks import make_identity
 
 G, K, M, T, S = 2, 512, 1024, 1024, 256
 FLOPS = 2 * 2 * K * M * S
@@ -17,14 +18,15 @@ GELU = mybir.ActivationFunctionType.Gelu_apprx_tanh
 
 P = 128
 PACK = 4
+PAIR = 2
 N = 128
 HALVES = S // N
 TILES = M // P
-CHUNKS = 2
-TILES_PER_CHUNK = TILES // CHUNKS
-CHUNK = M // CHUNKS
 LIST_ROWS = 16
 W8_PLANE_ROW = 4
+PIECE = T // 2
+VECTOR_SHARE = 352
+STORES = (2, 2, 2, 1, 1)
 
 
 def tile_list_sage_gelu_kernel(
@@ -35,123 +37,132 @@ def tile_list_sage_gelu_kernel(
         pool = ctx.enter_context(tc.tile_pool(name="held", bufs=1))
         psum = ctx.enter_context(tc.psum_pool(name="psum", bufs=1))
 
-        offsets = pool.tile([P, G * S // LIST_ROWS], U16, name="offsets")
-        x_rows = [pool.tile([P, T], F32, name="x_rows%d" % i, align_bytes=64) for i in range(PACK)]
-        c_raw = pool.tile([P, PACK, S], F32, name="c_raw", align_bytes=64)
-        w8 = [pool.tile([P, CHUNK], U32, name="w8_%d" % a, align_bytes=64) for a in range(CHUNKS)]
-        w4 = pool.tile([P, 2 * M], U8, name="w4", align_bytes=64)
-        w4_plane = pool.tile([P, M], U8, name="w4_plane", align_bytes=64)
-        w8_plane = pool.tile([P, M], U8, name="w8_plane", align_bytes=64)
-        picked = pool.tile([P, PACK, G * S], F32, name="picked", align_bytes=64)
-        bias_rows = pool.tile([P, 32], F32, name="bias_rows", align_bytes=64)
-        staged = pool.tile([P, 3, N, PACK], BF16, name="staged", align_bytes=64)
-        warm = pool.tile([P, 2], F32, name="warm", align_bytes=64)
-        banks = [psum.tile([P, 512], F32, name="bank%d" % i) for i in range(8)]
+        def held(shape, dtype, name):
+            return pool.tile(shape, dtype, name=name, align_bytes=64)
 
-        nc.vector.memset(bias_rows[:], 0.0)
-        nc.vector.memset(w8_plane[:].bitcast(U32), 0)
-        nc.gpsimd.dma_start(bias_rows[0:P:4, :], b.rearrange("(m q r) -> q m r", q=4, r=32))
-        nc.vector.memset(w4_plane[:].bitcast(U32), 0)
+        offsets = pool.tile([P, G * S // LIST_ROWS], U16, name="offsets")
+        x_raw = [
+            [held([P, PAIR, PIECE], F32, "x_raw%d_%d" % (u, a)) for a in range(T // PIECE)] for u in range(PACK // PAIR)
+        ]
+        pairs = [held([P, T * PAIR], BF16, "pairs%d" % u) for u in range(PACK // PAIR)]
+        c_raw = held([P, PACK, S], F32, "c_raw")
+        w8 = held([P, M], U32, "w8")
+        w4 = held([P, 2 * M], U8, "w4")
+        w4_plane = held([P, M], U8, "w4_plane")
+        w8_plane = held([P, M], U8, "w8_plane")
+        picked = held([P, PACK // PAIR * G * S], U32, "picked")
+        bias_rows = held([P, P], F32, "bias_rows")
+        identity = held([P, P], F32, "identity")
+        bias = held([P, TILES], F32, "bias")
+        woven = held([P, 2 * S * PACK], BF16, "woven")
+        codes = held([P, 2 * S], U32, "codes")
+        scales = held([P, 2 * S], U8, "scales")
+        warm = held([P, 2], F32, "warm")
+        banks = [psum.tile([P, 512], F32, name="bank%d" % i) for i in range(TILES)]
+
         nc.vector.memset(warm[:, 0:1], 0.0)
         nc.scalar.activation(warm[:, 1:2], warm[:, 0:1], GELU)
+        nc.vector.memset(w4_plane[:].bitcast(U32), 0)
+        nc.vector.memset(w8_plane[:].bitcast(U32), 0)
+        nc.gpsimd.memset(bias_rows[:], 0.0)
+        nc.gpsimd.dma_start(bias_rows[0:TILES, :], b.rearrange("(m p) -> m p", p=P))
+        make_identity(nc, identity[:])
 
         def load_scales(engine, plane, first, src):
             rows = src[0].rearrange("(q r) n -> r q n", r=4)
             for r in range(4):
                 engine.dma_start(plane[first + r : P : 32, :].bitcast(I32), rows[r].bitcast(I32))
 
-        load_scales(nc.gpsimd, w8_plane, W8_PLANE_ROW, w8_scales)
+        load_scales(nc.gpsimd, w4_plane, 0, w4_scales)
 
         x_view = xT.rearrange("(p i) t -> p i t", i=PACK)
-        for i in range(PACK):
-            nc.sync.dma_start(x_rows[i][:], x_view[:, i, :])
-            if i == 0:
-                nc.sync.dma_start(offsets[:], offs)
+        for u in range(PACK // PAIR):
+            for a in range(T // PIECE):
+                nc.sync.dma_start(x_raw[u][a][:], x_view[:, u * PAIR : (u + 1) * PAIR, a * PIECE : (a + 1) * PIECE])
+                if (u, a) == (0, 0):
+                    nc.sync.dma_start(offsets[:], offs)
         nc.sync.dma_start(c_raw[:], c.rearrange("(p i) j -> p i j", i=PACK))
-        load_scales(nc.sync, w4_plane, 0, w4_scales)
+        nc.sync.dma_start(w8[:].bitcast(I32), w8_words[0].rearrange("p n t -> p (n t)").bitcast(I32))
         nc.sync.dma_start(w4[:].bitcast(I32), w4_words[0].bitcast(I32))
-        w8_bytes = w8_words[0].rearrange("p n t -> p (n t)")
-        for a in range(CHUNKS):
-            nc.sync.dma_start(w8[a][:].bitcast(I32), w8_bytes[:, 4 * CHUNK * a : 4 * CHUNK * (a + 1)].bitcast(I32))
+        load_scales(nc.scalar, w8_plane, W8_PLANE_ROW, w8_scales)
 
-        for i in range(PACK - 1):
-            nc.vector.tensor_copy(picked[:, i, :], x_rows[i][:].indirect(offsets[:]))
+        bias_psum = banks[TILES - 1][:, S : S + P]
+        nc.tensor.transpose(bias_psum, bias_rows[:], identity[:])
+        nc.scalar.copy(bias[:], bias_psum[:, 0:TILES])
 
-        out_view = out.rearrange("(m p) j -> p m j", p=P)
-        cols = N // LIST_ROWS
+        def pair_up(copy, u, first, source):
+            count = source.shape[2]
+            copy(
+                pairs[u][:, PAIR * first : PAIR * (first + count)].rearrange("p (t e) -> p t e", e=PAIR),
+                source.rearrange("p e t -> p t e"),
+            )
 
-        def quantize(codes, scale, values):
-            nc.vector.quantize_mx(out=codes.bitcast(FP8X4), scales=scale, in_=values.rearrange("p j i -> p (j i)"))
+        def gather(u):
+            nc.vector.tensor_copy(
+                picked[:, u * G * S : (u + 1) * G * S], pairs[u][:].bitcast(U32).indirect(offsets[:])
+            )
 
-        bias = picked[:, 0, 0:32]
-        c_mx = []
+        x_column = [0, N + S]
+        c_column = N
+
+        def maximum(h):
+            both = picked[:].bitcast(BF16).rearrange("p (u g j e) -> p g j u e", u=PACK // PAIR, g=G, e=PAIR)
+            first = x_column[h] * PACK
+            nc.vector.tensor_max(
+                woven[:, first : first + N * PACK].rearrange("p (j u e) -> p j u e", u=PACK // PAIR, e=PAIR),
+                both[:, 0, h * N : (h + 1) * N],
+                both[:, 1, h * N : (h + 1) * N],
+            )
+
+        for a in range(T // PIECE):
+            pair_up(nc.vector.tensor_copy, 0, a * PIECE, x_raw[0][a][:])
+        pair_up(nc.scalar.copy, 1, 0, x_raw[1][0][:])
+        gather(0)
+        pair_up(nc.vector.tensor_copy, 1, PIECE, x_raw[1][1][:, :, 0:VECTOR_SHARE])
+        pair_up(nc.scalar.copy, 1, PIECE + VECTOR_SHARE, x_raw[1][1][:, :, VECTOR_SHARE:PIECE])
         for h in range(HALVES):
-            c_codes = pool.tile([P, N], U32, name="c_codes%d" % h, align_bytes=64)
-            c_scale = pool.tile([P, N], U8, name="c_scale%d" % h, align_bytes=64)
-            c_mx.append((c_codes[:], c_scale[:]))
+            first = (c_column + h * N) * PACK
             nc.scalar.copy(
-                staged[:, 1 + h],
+                woven[:, first : first + N * PACK].rearrange("p (j i) -> p j i", i=PACK),
                 c_raw[:, :, h * N : (h + 1) * N].rearrange("p i j -> p j i"),
             )
-
+        gather(1)
         for h in range(HALVES):
-            x_bf = staged[:, h]
-            c_codes, c_scale = c_mx[h]
-            x_codes = pool.tile([P, N], U32, name="x_codes%d" % h, align_bytes=64)[:]
-            x_scale = pool.tile([P, N], U8, name="x_scale%d" % h, align_bytes=64)[:]
-            for g in range(G):
-                first = g * S + h * N
-                nc.vector.tensor_copy(
-                    picked[:, PACK - 1, first : first + N],
-                    x_rows[PACK - 1][:].indirect(offsets[:, first // LIST_ROWS : first // LIST_ROWS + cols]),
-                )
-            nc.vector.tensor_max(
-                x_bf,
-                picked[:, :, h * N : (h + 1) * N].rearrange("p i j -> p j i"),
-                picked[:, :, S + h * N : S + (h + 1) * N].rearrange("p i j -> p j i"),
+            maximum(h)
+        for h in range(HALVES):
+            nc.vector.quantize_mx(
+                out=codes[:, h * S : (h + 1) * S].bitcast(FP8X4),
+                scales=scales[:, h * S : (h + 1) * S],
+                in_=woven[:, h * S * PACK : (h + 1) * S * PACK],
             )
-            if h == 0:
-                nc.vector.transpose(bias, bias_rows[:])
-            quantize(x_codes, x_scale, x_bf)
-            if h == 0:
-                for hc in range(HALVES):
-                    quantize(c_mx[hc][0], c_mx[hc][1], staged[:, 1 + hc])
 
-            for a in range(CHUNKS):
-                res = pool.tile([P, TILES_PER_CHUNK, N], F32, name="res%d_%d" % (h, a), align_bytes=64)
-                for pair in range(TILES_PER_CHUNK // 2):
-                    bank = banks[4 * h + 2 * a + pair]
-                    for step in range(2):
-                        for e in range(2):
-                            local = 2 * pair + e
-                            m = a * TILES_PER_CHUNK + local
-                            if step == h:
-                                lhsT = w4[:, 2 * m * P : 2 * (m + 1) * P].bitcast(FP4X4)
-                                plane, rhs, rhs_scale = w4_plane[:, m * P : (m + 1) * P], x_codes, x_scale
-                            else:
-                                lhsT = w8[a][:, local * P : (local + 1) * P].bitcast(FP8X4)
-                                plane, rhs, rhs_scale = w8_plane[W8_PLANE_ROW:P, m * P : (m + 1) * P], c_codes, c_scale
-                            nc.tensor.matmul_mx(
-                                out=bank[:, e * N : (e + 1) * N],
-                                lhsT=lhsT,
-                                lhsT_scale=plane,
-                                rhs=rhs.bitcast(FP8X4),
-                                rhs_scale=rhs_scale,
-                                start=(step == 0 and e == 0),
-                                stop=(step == 1 and e == 1),
-                            )
-                    for e in range(2):
-                        local = 2 * pair + e
-                        m = a * TILES_PER_CHUNK + local
-                        nc.scalar.activation(
-                            res[:, local, :], bank[:, e * N : (e + 1) * N], GELU, bias=bias[:, 4 * m : 4 * m + 1]
-                        )
-                    if (h, a) == (HALVES - 1, CHUNKS - 1):
-                        first = a * TILES_PER_CHUNK + 2 * pair
-                        nc.sync.dma_start(
-                            out_view[:, first : first + 2, h * N : (h + 1) * N], res[:, 2 * pair : 2 * pair + 2, :]
-                        )
-                if (h, a) != (HALVES - 1, CHUNKS - 1):
-                    nc.sync.dma_start(
-                        out_view[:, a * TILES_PER_CHUNK : (a + 1) * TILES_PER_CHUNK, h * N : (h + 1) * N], res[:]
-                    )
+        def neighbour_pass(m, h):
+            nc.tensor.matmul_mx(
+                out=banks[m][:, h * N : (h + 1) * N],
+                lhsT=w4[:, 2 * m * P : 2 * (m + 1) * P].bitcast(FP4X4),
+                lhsT_scale=w4_plane[:, m * P : (m + 1) * P],
+                rhs=codes[:, x_column[h] : x_column[h] + N].bitcast(FP8X4),
+                rhs_scale=scales[:, x_column[h] : x_column[h] + N],
+                start=(h == 0),
+                stop=False,
+            )
+
+        out_view = out.rearrange("(m p) j -> p m j", p=P)
+        first = 0
+        for number, count in enumerate(STORES):
+            res = held([P, count, S], F32, "res%d" % number)
+            for m in range(first, first + count):
+                for h in range(HALVES):
+                    neighbour_pass(m, h)
+                nc.tensor.matmul_mx(
+                    out=banks[m][:, 0:S],
+                    lhsT=w8[:, m * P : (m + 1) * P].bitcast(FP8X4),
+                    lhsT_scale=w8_plane[W8_PLANE_ROW:P, m * P : (m + 1) * P],
+                    rhs=codes[:, c_column : c_column + S].bitcast(FP8X4),
+                    rhs_scale=scales[:, c_column : c_column + S],
+                    start=False,
+                    stop=True,
+                )
+                nc.scalar.activation(res[:, m - first, :], banks[m][:, 0:S], GELU, bias=bias[:, m : m + 1])
+            nc.sync.dma_start(out_view[:, first : first + count, :], res[:])
+            first += count

@@ -26,7 +26,9 @@ LIST_ROWS = 16
 W8_PLANE_ROW = 4
 PIECE = T // 2
 VECTOR_SHARE = 352
-STORES = (2, 2, 2, 1, 1)
+STORES = ((4, 4), (2, 2, 2, 1, 1))
+PICKED = 7
+WOVEN = N * PACK // PAIR
 
 
 def tile_list_sage_gelu_kernel(
@@ -50,11 +52,10 @@ def tile_list_sage_gelu_kernel(
         w4 = held([P, 2 * M], U8, "w4")
         w4_plane = held([P, M], U8, "w4_plane")
         w8_plane = held([P, M], U8, "w8_plane")
-        picked = held([P, PACK // PAIR * G * S], U32, "picked")
+        work = held([P, PICKED * N + 2 * HALVES * WOVEN], U32, "work")
         bias_rows = held([P, P], F32, "bias_rows")
         identity = held([P, P], F32, "identity")
         bias = held([P, TILES], F32, "bias")
-        woven = held([P, 2 * S * PACK], BF16, "woven")
         codes = held([P, 2 * S], U32, "codes")
         scales = held([P, 2 * S], U8, "scales")
         warm = held([P, 2], F32, "warm")
@@ -97,27 +98,43 @@ def tile_list_sage_gelu_kernel(
                 source.rearrange("p e t -> p t e"),
             )
 
-        def gather(u):
+        woven = work[:, PICKED * N :].bitcast(BF16)
+        blocks = work[:, 0 : (PICKED + 1) * N].bitcast(BF16).rearrange("p (k j e) -> p k j e", j=N, e=PAIR)
+
+        def gather_high(h, g):
+            first = (g * S + h * N) // LIST_ROWS
+            place = (G * HALVES + G * h + g) * N
             nc.vector.tensor_copy(
-                picked[:, u * G * S : (u + 1) * G * S], pairs[u][:].bitcast(U32).indirect(offsets[:])
+                work[:, place : place + N],
+                pairs[1][:].bitcast(U32).indirect(offsets[:, first : first + N // LIST_ROWS]),
             )
 
         x_column = [0, N + S]
         c_column = N
 
         def maximum(h):
-            both = picked[:].bitcast(BF16).rearrange("p (u g j e) -> p g j u e", u=PACK // PAIR, g=G, e=PAIR)
+            sides = []
+            for g in range(G):
+                low, high = HALVES * g + h, G * HALVES + G * h + g
+                sides.append(blocks[:, low : high + 1 : high - low].rearrange("p u j e -> p j u e"))
             first = x_column[h] * PACK
             nc.vector.tensor_max(
                 woven[:, first : first + N * PACK].rearrange("p (j u e) -> p j u e", u=PACK // PAIR, e=PAIR),
-                both[:, 0, h * N : (h + 1) * N],
-                both[:, 1, h * N : (h + 1) * N],
+                sides[0],
+                sides[1],
+            )
+
+        def quantize(h):
+            nc.vector.quantize_mx(
+                out=codes[:, h * S : (h + 1) * S].bitcast(FP8X4),
+                scales=scales[:, h * S : (h + 1) * S],
+                in_=woven[:, h * S * PACK : (h + 1) * S * PACK],
             )
 
         for a in range(T // PIECE):
             pair_up(nc.vector.tensor_copy, 0, a * PIECE, x_raw[0][a][:])
         pair_up(nc.scalar.copy, 1, 0, x_raw[1][0][:])
-        gather(0)
+        nc.vector.tensor_copy(work[:, 0 : G * S], pairs[0][:].bitcast(U32).indirect(offsets[:]))
         pair_up(nc.vector.tensor_copy, 1, PIECE, x_raw[1][1][:, :, 0:VECTOR_SHARE])
         pair_up(nc.scalar.copy, 1, PIECE + VECTOR_SHARE, x_raw[1][1][:, :, VECTOR_SHARE:PIECE])
         for h in range(HALVES):
@@ -126,43 +143,42 @@ def tile_list_sage_gelu_kernel(
                 woven[:, first : first + N * PACK].rearrange("p (j i) -> p j i", i=PACK),
                 c_raw[:, :, h * N : (h + 1) * N].rearrange("p i j -> p j i"),
             )
-        gather(1)
-        for h in range(HALVES):
-            maximum(h)
-        for h in range(HALVES):
-            nc.vector.quantize_mx(
-                out=codes[:, h * S : (h + 1) * S].bitcast(FP8X4),
-                scales=scales[:, h * S : (h + 1) * S],
-                in_=woven[:, h * S * PACK : (h + 1) * S * PACK],
-            )
-
-        def neighbour_pass(m, h):
-            nc.tensor.matmul_mx(
-                out=banks[m][:, h * N : (h + 1) * N],
-                lhsT=w4[:, 2 * m * P : 2 * (m + 1) * P].bitcast(FP4X4),
-                lhsT_scale=w4_plane[:, m * P : (m + 1) * P],
-                rhs=codes[:, x_column[h] : x_column[h] + N].bitcast(FP8X4),
-                rhs_scale=scales[:, x_column[h] : x_column[h] + N],
-                start=(h == 0),
-                stop=False,
-            )
+        gather_high(0, 0)
+        gather_high(0, 1)
+        gather_high(1, 0)
+        maximum(0)
+        quantize(0)
+        gather_high(1, 1)
+        maximum(1)
+        quantize(1)
 
         out_view = out.rearrange("(m p) j -> p m j", p=P)
-        first = 0
-        for number, count in enumerate(STORES):
-            res = held([P, count, S], F32, "res%d" % number)
-            for m in range(first, first + count):
-                for h in range(HALVES):
-                    neighbour_pass(m, h)
-                nc.tensor.matmul_mx(
-                    out=banks[m][:, 0:S],
-                    lhsT=w8[:, m * P : (m + 1) * P].bitcast(FP8X4),
-                    lhsT_scale=w8_plane[W8_PLANE_ROW:P, m * P : (m + 1) * P],
-                    rhs=codes[:, c_column : c_column + S].bitcast(FP8X4),
-                    rhs_scale=scales[:, c_column : c_column + S],
-                    start=False,
-                    stop=True,
-                )
-                nc.scalar.activation(res[:, m - first, :], banks[m][:, 0:S], GELU, bias=bias[:, m : m + 1])
-            nc.sync.dma_start(out_view[:, first : first + count, :], res[:])
-            first += count
+        for h in range(HALVES):
+            x_cols = slice(x_column[h], x_column[h] + N)
+            c_cols = slice(c_column + h * N, c_column + (h + 1) * N)
+            first = 0
+            for number, count in enumerate(STORES[h]):
+                res = held([P, count, N], F32, "res%d_%d" % (h, number))
+                for m in range(first, first + count):
+                    sums = banks[m][:, h * N : (h + 1) * N]
+                    nc.tensor.matmul_mx(
+                        out=sums,
+                        lhsT=w4[:, 2 * m * P : 2 * (m + 1) * P].bitcast(FP4X4),
+                        lhsT_scale=w4_plane[:, m * P : (m + 1) * P],
+                        rhs=codes[:, x_cols].bitcast(FP8X4),
+                        rhs_scale=scales[:, x_cols],
+                        start=True,
+                        stop=False,
+                    )
+                    nc.tensor.matmul_mx(
+                        out=sums,
+                        lhsT=w8[:, m * P : (m + 1) * P].bitcast(FP8X4),
+                        lhsT_scale=w8_plane[W8_PLANE_ROW:P, m * P : (m + 1) * P],
+                        rhs=codes[:, c_cols].bitcast(FP8X4),
+                        rhs_scale=scales[:, c_cols],
+                        start=False,
+                        stop=True,
+                    )
+                    nc.scalar.activation(res[:, m - first, :], sums, GELU, bias=bias[:, m : m + 1])
+                nc.sync.dma_start(out_view[:, first : first + count, h * N : (h + 1) * N], res[:])
+                first += count

@@ -25,6 +25,8 @@ TILES = M // P
 LIST_ROWS = 16
 W8_PLANE_ROW = 4
 PIECE = T // 2
+CHUNKS = 2
+CHUNK = M // CHUNKS
 VECTOR_SHARE = 352
 STORES = ((4, 4), (2, 2, 2, 1, 1))
 PICKED = 7
@@ -48,7 +50,7 @@ def tile_list_sage_gelu_kernel(
         ]
         pairs = [held([P, T * PAIR], BF16, "pairs%d" % u) for u in range(PACK // PAIR)]
         c_raw = held([P, PACK, S], F32, "c_raw")
-        w8 = held([P, M], U32, "w8")
+        w8 = [held([P, CHUNK], U32, "w8_%d" % a) for a in range(CHUNKS)]
         w4 = held([P, 2 * M], U8, "w4")
         w4_plane = held([P, M], U8, "w4_plane")
         w8_plane = held([P, M], U8, "w8_plane")
@@ -74,18 +76,20 @@ def tile_list_sage_gelu_kernel(
             for r in range(4):
                 engine.dma_start(plane[first + r : P : 32, :].bitcast(I32), rows[r].bitcast(I32))
 
-        load_scales(nc.gpsimd, w4_plane, 0, w4_scales)
-
         x_view = xT.rearrange("(p i) t -> p i t", i=PACK)
         for u in range(PACK // PAIR):
             for a in range(T // PIECE):
                 nc.sync.dma_start(x_raw[u][a][:], x_view[:, u * PAIR : (u + 1) * PAIR, a * PIECE : (a + 1) * PIECE])
-                if (u, a) == (0, 0):
-                    nc.sync.dma_start(offsets[:], offs)
+            if u == 0:
+                nc.sync.dma_start(offsets[:], offs)
+        load_scales(nc.sync, w4_plane, 0, w4_scales)
         nc.sync.dma_start(c_raw[:], c.rearrange("(p i) j -> p i j", i=PACK))
-        nc.sync.dma_start(w8[:].bitcast(I32), w8_words[0].rearrange("p n t -> p (n t)").bitcast(I32))
         nc.sync.dma_start(w4[:].bitcast(I32), w4_words[0].bitcast(I32))
-        load_scales(nc.scalar, w8_plane, W8_PLANE_ROW, w8_scales)
+        w8_bytes = w8_words[0].rearrange("p n t -> p (n t)")
+        for a in range(CHUNKS):
+            nc.sync.dma_start(w8[a][:].bitcast(I32), w8_bytes[:, 4 * CHUNK * a : 4 * CHUNK * (a + 1)].bitcast(I32))
+            if a == 0:
+                load_scales(nc.sync, w8_plane, W8_PLANE_ROW, w8_scales)
 
         bias_psum = banks[TILES - 1][:, S : S + P]
         nc.tensor.transpose(bias_psum, bias_rows[:], identity[:])
@@ -172,7 +176,7 @@ def tile_list_sage_gelu_kernel(
                     )
                     nc.tensor.matmul_mx(
                         out=sums,
-                        lhsT=w8[:, m * P : (m + 1) * P].bitcast(FP8X4),
+                        lhsT=w8[m * P // CHUNK][:, m * P % CHUNK : m * P % CHUNK + P].bitcast(FP8X4),
                         lhsT_scale=w8_plane[W8_PLANE_ROW:P, m * P : (m + 1) * P],
                         rhs=codes[:, c_cols].bitcast(FP8X4),
                         rhs_scale=scales[:, c_cols],

@@ -28,9 +28,9 @@ PIECE = T // 2
 CHUNKS = 2
 CHUNK = M // CHUNKS
 VECTOR_SHARE = 352
-STORES = ((4, 4), (2, 2, 2, 1, 1))
-PICKED = 7
+STORES = ((1, 1, 2, 2, 2), (2, 2, 2, 1, 1))
 WOVEN = N * PACK // PAIR
+SHARED = 16
 
 
 def tile_list_sage_gelu_kernel(
@@ -49,17 +49,21 @@ def tile_list_sage_gelu_kernel(
             [held([P, PAIR, PIECE], F32, "x_raw%d_%d" % (u, a)) for a in range(T // PIECE)] for u in range(PACK // PAIR)
         ]
         pairs = [held([P, T * PAIR], BF16, "pairs%d" % u) for u in range(PACK // PAIR)]
-        c_raw = held([P, PACK, S], F32, "c_raw")
+        staged = held([P, PACK * S + HALVES * (WOVEN - SHARED)], F32, "staged")
+        c_raw = staged[:, WOVEN - SHARED : WOVEN - SHARED + PACK * S].rearrange("p (i j) -> p i j", i=PACK)
+        x_first = [0, WOVEN + PACK * S - 2 * SHARED]
+        x_woven = [staged[:, first : first + WOVEN].bitcast(BF16) for first in x_first]
+        c_woven = [held([P, N * PACK], BF16, "c_woven%d" % h)[:] for h in range(HALVES)]
         w8 = [held([P, CHUNK], U32, "w8_%d" % a) for a in range(CHUNKS)]
         w4 = held([P, 2 * M], U8, "w4")
         w4_plane = held([P, M], U8, "w4_plane")
         w8_plane = held([P, M], U8, "w8_plane")
-        work = held([P, PICKED * N + 2 * HALVES * WOVEN], U32, "work")
+        picked = held([P, PACK // PAIR * G * S], U32, "picked")
         bias_rows = held([P, P], F32, "bias_rows")
         identity = held([P, P], F32, "identity")
         bias = held([P, TILES], F32, "bias")
-        codes = held([P, 2 * S], U32, "codes")
-        scales = held([P, 2 * S], U8, "scales")
+        x_mx = [(held([P, N], U32, "x_codes%d" % h)[:], held([P, N], U8, "x_scale%d" % h)[:]) for h in range(HALVES)]
+        c_mx = [(held([P, N], U32, "c_codes%d" % h)[:], held([P, N], U8, "c_scale%d" % h)[:]) for h in range(HALVES)]
         warm = held([P, 2], F32, "warm")
         banks = [psum.tile([P, 512], F32, name="bank%d" % i) for i in range(TILES)]
 
@@ -83,7 +87,7 @@ def tile_list_sage_gelu_kernel(
             if u == 0:
                 nc.sync.dma_start(offsets[:], offs)
         load_scales(nc.sync, w4_plane, 0, w4_scales)
-        nc.sync.dma_start(c_raw[:], c.rearrange("(p i) j -> p i j", i=PACK))
+        nc.sync.dma_start(c_raw, c.rearrange("(p i) j -> p i j", i=PACK))
         nc.sync.dma_start(w4[:].bitcast(I32), w4_words[0].bitcast(I32))
         w8_bytes = w8_words[0].rearrange("p n t -> p (n t)")
         for a in range(CHUNKS):
@@ -102,64 +106,41 @@ def tile_list_sage_gelu_kernel(
                 source.rearrange("p e t -> p t e"),
             )
 
-        woven = work[:, PICKED * N :].bitcast(BF16)
-        blocks = work[:, 0 : (PICKED + 1) * N].bitcast(BF16).rearrange("p (k j e) -> p k j e", j=N, e=PAIR)
-
-        def gather_high(h, g):
-            first = (g * S + h * N) // LIST_ROWS
-            place = (G * HALVES + G * h + g) * N
+        def gather(u):
             nc.vector.tensor_copy(
-                work[:, place : place + N],
-                pairs[1][:].bitcast(U32).indirect(offsets[:, first : first + N // LIST_ROWS]),
+                picked[:, u * G * S : (u + 1) * G * S], pairs[u][:].bitcast(U32).indirect(offsets[:])
             )
-
-        x_column = [0, N + S]
-        c_column = N
 
         def maximum(h):
-            sides = []
-            for g in range(G):
-                low, high = HALVES * g + h, G * HALVES + G * h + g
-                sides.append(blocks[:, low : high + 1 : high - low].rearrange("p u j e -> p j u e"))
-            first = x_column[h] * PACK
+            both = picked[:].bitcast(BF16).rearrange("p (u g j e) -> p g j u e", u=PACK // PAIR, g=G, e=PAIR)
             nc.vector.tensor_max(
-                woven[:, first : first + N * PACK].rearrange("p (j u e) -> p j u e", u=PACK // PAIR, e=PAIR),
-                sides[0],
-                sides[1],
+                x_woven[h].rearrange("p (j u e) -> p j u e", u=PACK // PAIR, e=PAIR),
+                both[:, 0, h * N : (h + 1) * N],
+                both[:, 1, h * N : (h + 1) * N],
             )
 
-        def quantize(h):
-            nc.vector.quantize_mx(
-                out=codes[:, h * S : (h + 1) * S].bitcast(FP8X4),
-                scales=scales[:, h * S : (h + 1) * S],
-                in_=woven[:, h * S * PACK : (h + 1) * S * PACK],
-            )
+        def quantize(mx, values):
+            nc.vector.quantize_mx(out=mx[0].bitcast(FP8X4), scales=mx[1], in_=values)
 
         for a in range(T // PIECE):
             pair_up(nc.vector.tensor_copy, 0, a * PIECE, x_raw[0][a][:])
         pair_up(nc.scalar.copy, 1, 0, x_raw[1][0][:])
-        nc.vector.tensor_copy(work[:, 0 : G * S], pairs[0][:].bitcast(U32).indirect(offsets[:]))
+        gather(0)
         pair_up(nc.vector.tensor_copy, 1, PIECE, x_raw[1][1][:, :, 0:VECTOR_SHARE])
         pair_up(nc.scalar.copy, 1, PIECE + VECTOR_SHARE, x_raw[1][1][:, :, VECTOR_SHARE:PIECE])
         for h in range(HALVES):
-            first = (c_column + h * N) * PACK
             nc.scalar.copy(
-                woven[:, first : first + N * PACK].rearrange("p (j i) -> p j i", i=PACK),
+                c_woven[h].rearrange("p (j i) -> p j i", i=PACK),
                 c_raw[:, :, h * N : (h + 1) * N].rearrange("p i j -> p j i"),
             )
-        gather_high(0, 0)
-        gather_high(0, 1)
-        gather_high(1, 0)
-        maximum(0)
-        quantize(0)
-        gather_high(1, 1)
-        maximum(1)
-        quantize(1)
+        gather(1)
+        for h in range(HALVES):
+            maximum(h)
+            quantize(c_mx[h], c_woven[h])
+            quantize(x_mx[h], x_woven[h])
 
         out_view = out.rearrange("(m p) j -> p m j", p=P)
         for h in range(HALVES):
-            x_cols = slice(x_column[h], x_column[h] + N)
-            c_cols = slice(c_column + h * N, c_column + (h + 1) * N)
             first = 0
             for number, count in enumerate(STORES[h]):
                 res = held([P, count, N], F32, "res%d_%d" % (h, number))
@@ -169,8 +150,8 @@ def tile_list_sage_gelu_kernel(
                         out=sums,
                         lhsT=w4[:, 2 * m * P : 2 * (m + 1) * P].bitcast(FP4X4),
                         lhsT_scale=w4_plane[:, m * P : (m + 1) * P],
-                        rhs=codes[:, x_cols].bitcast(FP8X4),
-                        rhs_scale=scales[:, x_cols],
+                        rhs=x_mx[h][0].bitcast(FP8X4),
+                        rhs_scale=x_mx[h][1],
                         start=True,
                         stop=False,
                     )
@@ -178,8 +159,8 @@ def tile_list_sage_gelu_kernel(
                         out=sums,
                         lhsT=w8[m * P // CHUNK][:, m * P % CHUNK : m * P % CHUNK + P].bitcast(FP8X4),
                         lhsT_scale=w8_plane[W8_PLANE_ROW:P, m * P : (m + 1) * P],
-                        rhs=codes[:, c_cols].bitcast(FP8X4),
-                        rhs_scale=scales[:, c_cols],
+                        rhs=c_mx[h][0].bitcast(FP8X4),
+                        rhs_scale=c_mx[h][1],
                         start=False,
                         stop=True,
                     )

@@ -28,9 +28,11 @@ PIECE = T // 2
 CHUNKS = 2
 CHUNK = M // CHUNKS
 VECTOR_SHARE = 352
-STORES = ((1, 1, 2, 2, 2), (2, 2, 2, 1, 1))
-WOVEN = N * PACK // PAIR
-SHARED = 16
+STORES = ((4, 4), (2, 2, 2, 1, 1))
+HIGH_BLOCK = ((4, 5), (9, 11))
+WOVEN_BLOCK = 6
+C_BLOCK = 7
+BLOCKS = C_BLOCK + PACK * HALVES
 
 
 def tile_list_sage_gelu_kernel(
@@ -49,16 +51,17 @@ def tile_list_sage_gelu_kernel(
             [held([P, PAIR, PIECE], F32, "x_raw%d_%d" % (u, a)) for a in range(T // PIECE)] for u in range(PACK // PAIR)
         ]
         pairs = [held([P, T * PAIR], BF16, "pairs%d" % u) for u in range(PACK // PAIR)]
-        staged = held([P, PACK * S + HALVES * (WOVEN - SHARED)], F32, "staged")
-        c_raw = staged[:, WOVEN - SHARED : WOVEN - SHARED + PACK * S].rearrange("p (i j) -> p i j", i=PACK)
-        x_first = [0, WOVEN + PACK * S - 2 * SHARED]
-        x_woven = [staged[:, first : first + WOVEN].bitcast(BF16) for first in x_first]
+        staged = held([P, BLOCKS * N], U32, "staged")
+        c_raw = staged[:, C_BLOCK * N :].bitcast(F32).rearrange("p (i j) -> p i j", i=PACK)
+        x_woven = [
+            staged[:, WOVEN_BLOCK * N : (WOVEN_BLOCK + 2) * N].bitcast(BF16),
+            held([P, N * PACK], BF16, "x_woven1")[:],
+        ]
         c_woven = [held([P, N * PACK], BF16, "c_woven%d" % h)[:] for h in range(HALVES)]
         w8 = [held([P, CHUNK], U32, "w8_%d" % a) for a in range(CHUNKS)]
         w4 = held([P, 2 * M], U8, "w4")
         w4_plane = held([P, M], U8, "w4_plane")
         w8_plane = held([P, M], U8, "w8_plane")
-        picked = held([P, PACK // PAIR * G * S], U32, "picked")
         bias_rows = held([P, P], F32, "bias_rows")
         identity = held([P, P], F32, "identity")
         bias = held([P, TILES], F32, "bias")
@@ -69,8 +72,8 @@ def tile_list_sage_gelu_kernel(
 
         nc.vector.memset(warm[:, 0:1], 0.0)
         nc.scalar.activation(warm[:, 1:2], warm[:, 0:1], GELU)
-        nc.vector.memset(w4_plane[:].bitcast(U32), 0)
         nc.vector.memset(w8_plane[:].bitcast(U32), 0)
+        nc.vector.memset(w4_plane[:].bitcast(U32), 0)
         nc.gpsimd.memset(bias_rows[:], 0.0)
         nc.gpsimd.dma_start(bias_rows[0:TILES, :], b.rearrange("(m p) -> m p", p=P))
         make_identity(nc, identity[:])
@@ -80,20 +83,20 @@ def tile_list_sage_gelu_kernel(
             for r in range(4):
                 engine.dma_start(plane[first + r : P : 32, :].bitcast(I32), rows[r].bitcast(I32))
 
+        load_scales(nc.gpsimd, w4_plane, 0, w4_scales)
+
         x_view = xT.rearrange("(p i) t -> p i t", i=PACK)
         for u in range(PACK // PAIR):
             for a in range(T // PIECE):
                 nc.sync.dma_start(x_raw[u][a][:], x_view[:, u * PAIR : (u + 1) * PAIR, a * PIECE : (a + 1) * PIECE])
             if u == 0:
                 nc.sync.dma_start(offsets[:], offs)
-        load_scales(nc.sync, w4_plane, 0, w4_scales)
         nc.sync.dma_start(c_raw, c.rearrange("(p i) j -> p i j", i=PACK))
-        nc.sync.dma_start(w4[:].bitcast(I32), w4_words[0].bitcast(I32))
+        load_scales(nc.sync, w8_plane, W8_PLANE_ROW, w8_scales)
         w8_bytes = w8_words[0].rearrange("p n t -> p (n t)")
         for a in range(CHUNKS):
             nc.sync.dma_start(w8[a][:].bitcast(I32), w8_bytes[:, 4 * CHUNK * a : 4 * CHUNK * (a + 1)].bitcast(I32))
-            if a == 0:
-                load_scales(nc.sync, w8_plane, W8_PLANE_ROW, w8_scales)
+        nc.sync.dma_start(w4[:].bitcast(I32), w4_words[0].bitcast(I32))
 
         bias_psum = banks[TILES - 1][:, S : S + P]
         nc.tensor.transpose(bias_psum, bias_rows[:], identity[:])
@@ -106,17 +109,23 @@ def tile_list_sage_gelu_kernel(
                 source.rearrange("p e t -> p t e"),
             )
 
-        def gather(u):
+        blocks = staged[:].bitcast(BF16).rearrange("p (k j e) -> p k j e", j=N, e=PAIR)
+
+        def gather_high(h, g):
+            first = (g * S + h * N) // LIST_ROWS
+            place = HIGH_BLOCK[h][g] * N
             nc.vector.tensor_copy(
-                picked[:, u * G * S : (u + 1) * G * S], pairs[u][:].bitcast(U32).indirect(offsets[:])
+                staged[:, place : place + N],
+                pairs[1][:].bitcast(U32).indirect(offsets[:, first : first + N // LIST_ROWS]),
             )
 
         def maximum(h):
-            both = picked[:].bitcast(BF16).rearrange("p (u g j e) -> p g j u e", u=PACK // PAIR, g=G, e=PAIR)
+            sides = []
+            for g in range(G):
+                low, high = HALVES * g + h, HIGH_BLOCK[h][g]
+                sides.append(blocks[:, low : high + 1 : high - low].rearrange("p u j e -> p j u e"))
             nc.vector.tensor_max(
-                x_woven[h].rearrange("p (j u e) -> p j u e", u=PACK // PAIR, e=PAIR),
-                both[:, 0, h * N : (h + 1) * N],
-                both[:, 1, h * N : (h + 1) * N],
+                x_woven[h].rearrange("p (j u e) -> p j u e", u=PACK // PAIR, e=PAIR), sides[0], sides[1]
             )
 
         def quantize(mx, values):
@@ -125,7 +134,7 @@ def tile_list_sage_gelu_kernel(
         for a in range(T // PIECE):
             pair_up(nc.vector.tensor_copy, 0, a * PIECE, x_raw[0][a][:])
         pair_up(nc.scalar.copy, 1, 0, x_raw[1][0][:])
-        gather(0)
+        nc.vector.tensor_copy(staged[:, 0 : G * S], pairs[0][:].bitcast(U32).indirect(offsets[:]))
         pair_up(nc.vector.tensor_copy, 1, PIECE, x_raw[1][1][:, :, 0:VECTOR_SHARE])
         pair_up(nc.scalar.copy, 1, PIECE + VECTOR_SHARE, x_raw[1][1][:, :, VECTOR_SHARE:PIECE])
         for h in range(HALVES):
@@ -133,11 +142,16 @@ def tile_list_sage_gelu_kernel(
                 c_woven[h].rearrange("p (j i) -> p j i", i=PACK),
                 c_raw[:, :, h * N : (h + 1) * N].rearrange("p i j -> p j i"),
             )
-        gather(1)
-        for h in range(HALVES):
-            maximum(h)
-            quantize(c_mx[h], c_woven[h])
-            quantize(x_mx[h], x_woven[h])
+        gather_high(0, 0)
+        gather_high(0, 1)
+        quantize(c_mx[0], c_woven[0])
+        maximum(0)
+        gather_high(1, 0)
+        quantize(x_mx[0], x_woven[0])
+        gather_high(1, 1)
+        quantize(c_mx[1], c_woven[1])
+        maximum(1)
+        quantize(x_mx[1], x_woven[1])
 
         out_view = out.rearrange("(m p) j -> p m j", p=P)
         for h in range(HALVES):
@@ -148,19 +162,19 @@ def tile_list_sage_gelu_kernel(
                     sums = banks[m][:, h * N : (h + 1) * N]
                     nc.tensor.matmul_mx(
                         out=sums,
-                        lhsT=w4[:, 2 * m * P : 2 * (m + 1) * P].bitcast(FP4X4),
-                        lhsT_scale=w4_plane[:, m * P : (m + 1) * P],
-                        rhs=x_mx[h][0].bitcast(FP8X4),
-                        rhs_scale=x_mx[h][1],
+                        lhsT=w8[m * P // CHUNK][:, m * P % CHUNK : m * P % CHUNK + P].bitcast(FP8X4),
+                        lhsT_scale=w8_plane[W8_PLANE_ROW:P, m * P : (m + 1) * P],
+                        rhs=c_mx[h][0].bitcast(FP8X4),
+                        rhs_scale=c_mx[h][1],
                         start=True,
                         stop=False,
                     )
                     nc.tensor.matmul_mx(
                         out=sums,
-                        lhsT=w8[m * P // CHUNK][:, m * P % CHUNK : m * P % CHUNK + P].bitcast(FP8X4),
-                        lhsT_scale=w8_plane[W8_PLANE_ROW:P, m * P : (m + 1) * P],
-                        rhs=c_mx[h][0].bitcast(FP8X4),
-                        rhs_scale=c_mx[h][1],
+                        lhsT=w4[:, 2 * m * P : 2 * (m + 1) * P].bitcast(FP4X4),
+                        lhsT_scale=w4_plane[:, m * P : (m + 1) * P],
+                        rhs=x_mx[h][0].bitcast(FP8X4),
+                        rhs_scale=x_mx[h][1],
                         start=False,
                         stop=True,
                     )

@@ -24,14 +24,14 @@ HALVES = S // N
 TILES = M // P
 LIST_ROWS = 16
 W8_PLANE_ROW = 4
-PIECE = T // 2
 CHUNKS = 2
 CHUNK = M // CHUNKS
-VECTOR_SHARE = 352
-STORES = ((4, 4), (2, 2, 2, 1, 1))
-HIGH_BLOCK = ((4, 5), (9, 11))
-WOVEN_BLOCK = 6
-C_BLOCK = 7
+PIECES = ((T // 2, T // 2), (768, T - 768))
+VECTOR_SHARES = ((T // 2, 352), (400, 144))
+EARLY = 6
+EARLY_STORES = ((2, 2, 2), (2, 2, 1, 1))
+HIGH_BLOCK = ((4, 5), (6, 8))
+C_BLOCK = 6
 BLOCKS = C_BLOCK + PACK * HALVES
 
 
@@ -48,15 +48,13 @@ def tile_list_sage_gelu_kernel(
 
         offsets = pool.tile([P, G * S // LIST_ROWS], U16, name="offsets")
         x_raw = [
-            [held([P, PAIR, PIECE], F32, "x_raw%d_%d" % (u, a)) for a in range(T // PIECE)] for u in range(PACK // PAIR)
+            [held([P, PAIR, width], F32, "x_raw%d_%d" % (u, a)) for a, width in enumerate(PIECES[u])]
+            for u in range(PACK // PAIR)
         ]
         pairs = [held([P, T * PAIR], BF16, "pairs%d" % u) for u in range(PACK // PAIR)]
         staged = held([P, BLOCKS * N], U32, "staged")
         c_raw = staged[:, C_BLOCK * N :].bitcast(F32).rearrange("p (i j) -> p i j", i=PACK)
-        x_woven = [
-            staged[:, WOVEN_BLOCK * N : (WOVEN_BLOCK + 2) * N].bitcast(BF16),
-            held([P, N * PACK], BF16, "x_woven1")[:],
-        ]
+        x_woven = [held([P, N * PACK], BF16, "x_woven%d" % h)[:] for h in range(HALVES)]
         c_woven = [held([P, N * PACK], BF16, "c_woven%d" % h)[:] for h in range(HALVES)]
         w8 = [held([P, CHUNK], U32, "w8_%d" % a) for a in range(CHUNKS)]
         w4 = held([P, 2 * M], U8, "w4")
@@ -87,16 +85,17 @@ def tile_list_sage_gelu_kernel(
 
         x_view = xT.rearrange("(p i) t -> p i t", i=PACK)
         for u in range(PACK // PAIR):
-            for a in range(T // PIECE):
-                nc.sync.dma_start(x_raw[u][a][:], x_view[:, u * PAIR : (u + 1) * PAIR, a * PIECE : (a + 1) * PIECE])
+            for a, width in enumerate(PIECES[u]):
+                first = sum(PIECES[u][:a])
+                nc.sync.dma_start(x_raw[u][a][:], x_view[:, u * PAIR : (u + 1) * PAIR, first : first + width])
             if u == 0:
                 nc.sync.dma_start(offsets[:], offs)
         nc.sync.dma_start(c_raw, c.rearrange("(p i) j -> p i j", i=PACK))
         load_scales(nc.sync, w8_plane, W8_PLANE_ROW, w8_scales)
+        nc.sync.dma_start(w4[:].bitcast(I32), w4_words[0].bitcast(I32))
         w8_bytes = w8_words[0].rearrange("p n t -> p (n t)")
         for a in range(CHUNKS):
             nc.sync.dma_start(w8[a][:].bitcast(I32), w8_bytes[:, 4 * CHUNK * a : 4 * CHUNK * (a + 1)].bitcast(I32))
-        nc.sync.dma_start(w4[:].bitcast(I32), w4_words[0].bitcast(I32))
 
         bias_psum = banks[TILES - 1][:, S : S + P]
         nc.tensor.transpose(bias_psum, bias_rows[:], identity[:])
@@ -131,12 +130,16 @@ def tile_list_sage_gelu_kernel(
         def quantize(mx, values):
             nc.vector.quantize_mx(out=mx[0].bitcast(FP8X4), scales=mx[1], in_=values)
 
-        for a in range(T // PIECE):
-            pair_up(nc.vector.tensor_copy, 0, a * PIECE, x_raw[0][a][:])
-        pair_up(nc.scalar.copy, 1, 0, x_raw[1][0][:])
+        def pair_up_pieces(u):
+            for a, width in enumerate(PIECES[u]):
+                first, share = sum(PIECES[u][:a]), VECTOR_SHARES[u][a]
+                pair_up(nc.vector.tensor_copy, u, first, x_raw[u][a][:, :, 0:share])
+                if share < width:
+                    pair_up(nc.scalar.copy, u, first + share, x_raw[u][a][:, :, share:width])
+
+        pair_up_pieces(0)
         nc.vector.tensor_copy(staged[:, 0 : G * S], pairs[0][:].bitcast(U32).indirect(offsets[:]))
-        pair_up(nc.vector.tensor_copy, 1, PIECE, x_raw[1][1][:, :, 0:VECTOR_SHARE])
-        pair_up(nc.scalar.copy, 1, PIECE + VECTOR_SHARE, x_raw[1][1][:, :, VECTOR_SHARE:PIECE])
+        pair_up_pieces(1)
         for h in range(HALVES):
             nc.scalar.copy(
                 c_woven[h].rearrange("p (j i) -> p j i", i=PACK),
@@ -144,40 +147,54 @@ def tile_list_sage_gelu_kernel(
             )
         gather_high(0, 0)
         gather_high(0, 1)
-        quantize(c_mx[0], c_woven[0])
         maximum(0)
-        gather_high(1, 0)
         quantize(x_mx[0], x_woven[0])
+        quantize(c_mx[0], c_woven[0])
+        gather_high(1, 0)
         gather_high(1, 1)
         quantize(c_mx[1], c_woven[1])
         maximum(1)
         quantize(x_mx[1], x_woven[1])
 
+        def passes(m, h, start, stop):
+            sums = banks[m][:, h * N : (h + 1) * N]
+            nc.tensor.matmul_mx(
+                out=sums,
+                lhsT=w4[:, 2 * m * P : 2 * (m + 1) * P].bitcast(FP4X4),
+                lhsT_scale=w4_plane[:, m * P : (m + 1) * P],
+                rhs=x_mx[h][0].bitcast(FP8X4),
+                rhs_scale=x_mx[h][1],
+                start=start,
+                stop=False,
+            )
+            nc.tensor.matmul_mx(
+                out=sums,
+                lhsT=w8[m * P // CHUNK][:, m * P % CHUNK : m * P % CHUNK + P].bitcast(FP8X4),
+                lhsT_scale=w8_plane[W8_PLANE_ROW:P, m * P : (m + 1) * P],
+                rhs=c_mx[h][0].bitcast(FP8X4),
+                rhs_scale=c_mx[h][1],
+                start=False,
+                stop=stop,
+            )
+
         out_view = out.rearrange("(m p) j -> p m j", p=P)
-        for h in range(HALVES):
+
+        def half_tiles(h):
+            cols = slice(h * N, (h + 1) * N)
             first = 0
-            for number, count in enumerate(STORES[h]):
-                res = held([P, count, N], F32, "res%d_%d" % (h, number))
+            for count in EARLY_STORES[h]:
+                res = held([P, count, N], F32, "res%d_%d" % (first, h))
                 for m in range(first, first + count):
-                    sums = banks[m][:, h * N : (h + 1) * N]
-                    nc.tensor.matmul_mx(
-                        out=sums,
-                        lhsT=w8[m * P // CHUNK][:, m * P % CHUNK : m * P % CHUNK + P].bitcast(FP8X4),
-                        lhsT_scale=w8_plane[W8_PLANE_ROW:P, m * P : (m + 1) * P],
-                        rhs=c_mx[h][0].bitcast(FP8X4),
-                        rhs_scale=c_mx[h][1],
-                        start=True,
-                        stop=False,
-                    )
-                    nc.tensor.matmul_mx(
-                        out=sums,
-                        lhsT=w4[:, 2 * m * P : 2 * (m + 1) * P].bitcast(FP4X4),
-                        lhsT_scale=w4_plane[:, m * P : (m + 1) * P],
-                        rhs=x_mx[h][0].bitcast(FP8X4),
-                        rhs_scale=x_mx[h][1],
-                        start=False,
-                        stop=True,
-                    )
-                    nc.scalar.activation(res[:, m - first, :], sums, GELU, bias=bias[:, m : m + 1])
-                nc.sync.dma_start(out_view[:, first : first + count, h * N : (h + 1) * N], res[:])
+                    passes(m, h, True, True)
+                    nc.scalar.activation(res[:, m - first, :], banks[m][:, cols], GELU, bias=bias[:, m : m + 1])
+                nc.sync.dma_start(out_view[:, first : first + count, cols], res[:])
                 first += count
+
+        half_tiles(0)
+        for m in range(EARLY, TILES):
+            res = held([P, S], F32, "res%d" % m)
+            for h in range(HALVES):
+                passes(m, h, h == 0, h == HALVES - 1)
+            nc.scalar.activation(res[:], banks[m][:, 0:S], GELU, bias=bias[:, m : m + 1])
+            nc.sync.dma_start(out_view[:, m, :], res[:])
+        half_tiles(1)

@@ -26,13 +26,14 @@ LIST_ROWS = 16
 W8_PLANE_ROW = 4
 CHUNKS = 2
 CHUNK = M // CHUNKS
-PIECES = ((T // 2, T // 2), (768, T - 768))
-VECTOR_SHARES = ((T // 2, 352), (400, 144))
-EARLY = 6
-EARLY_STORES = ((2, 2, 2), (2, 2, 1, 1))
-HIGH_BLOCK = ((4, 5), (6, 8))
-C_BLOCK = 6
-BLOCKS = C_BLOCK + PACK * HALVES
+PIECES = (640, T - 640)
+VECTOR_SHARES = ((416, 256), (416, 256))
+EARLY = 4
+AHEAD = 3
+TOGETHER = 2
+LOW_BLOCK = 0
+HIGH_BLOCK = ((4, 5), (6, 5))
+BLOCKS = 7
 
 
 def tile_list_sage_gelu_kernel(
@@ -47,24 +48,24 @@ def tile_list_sage_gelu_kernel(
             return pool.tile(shape, dtype, name=name, align_bytes=64)
 
         offsets = pool.tile([P, G * S // LIST_ROWS], U16, name="offsets")
-        x_raw = [
-            [held([P, PAIR, width], F32, "x_raw%d_%d" % (u, a)) for a, width in enumerate(PIECES[u])]
-            for u in range(PACK // PAIR)
-        ]
+        x_raw = [held([P, PAIR * T], F32, "x_raw%d" % u) for u in range(PACK // PAIR)]
         pairs = [held([P, T * PAIR], BF16, "pairs%d" % u) for u in range(PACK // PAIR)]
         staged = held([P, BLOCKS * N], U32, "staged")
-        c_raw = staged[:, C_BLOCK * N :].bitcast(F32).rearrange("p (i j) -> p i j", i=PACK)
-        x_woven = [held([P, N * PACK], BF16, "x_woven%d" % h)[:] for h in range(HALVES)]
+        c_room = held([P, N + PACK * S], F32, "c_room")
+        c_raw = c_room[:, N:].rearrange("p (i j) -> p i j", i=PACK)
+        x_woven = [held([P, N * PACK], BF16, "x_woven0")[:], c_room[:, 0 : 2 * N].bitcast(BF16)]
         c_woven = [held([P, N * PACK], BF16, "c_woven%d" % h)[:] for h in range(HALVES)]
         w8 = [held([P, CHUNK], U32, "w8_%d" % a) for a in range(CHUNKS)]
-        w4 = held([P, 2 * M], U8, "w4")
+        w4 = [held([P, 2 * CHUNK], U8, "w4_%d" % a) for a in range(CHUNKS)]
         w4_plane = held([P, M], U8, "w4_plane")
         w8_plane = held([P, M], U8, "w8_plane")
         bias_rows = held([P, P], F32, "bias_rows")
         identity = held([P, P], F32, "identity")
-        bias = held([P, TILES], F32, "bias")
+        bias = x_raw[1][:, PAIR * T - TILES :]
         x_mx = [(held([P, N], U32, "x_codes%d" % h)[:], held([P, N], U8, "x_scale%d" % h)[:]) for h in range(HALVES)]
-        c_mx = [(held([P, N], U32, "c_codes%d" % h)[:], held([P, N], U8, "c_scale%d" % h)[:]) for h in range(HALVES)]
+        c_codes = held([P, S], U32, "c_codes")
+        c_scale = held([P, S], U8, "c_scale")
+        c_mx = [(c_codes[:, h * N : (h + 1) * N], c_scale[:, h * N : (h + 1) * N]) for h in range(HALVES)]
         warm = held([P, 2], F32, "warm")
         banks = [psum.tile([P, 512], F32, name="bank%d" % i) for i in range(TILES)]
 
@@ -81,31 +82,36 @@ def tile_list_sage_gelu_kernel(
             for r in range(4):
                 engine.dma_start(plane[first + r : P : 32, :].bitcast(I32), rows[r].bitcast(I32))
 
-        load_scales(nc.gpsimd, w4_plane, 0, w4_scales)
-
-        x_view = xT.rearrange("(p i) t -> p i t", i=PACK)
+        x_view = xT.rearrange("(p i) t -> p (i t)", i=PACK)
         for u in range(PACK // PAIR):
-            for a, width in enumerate(PIECES[u]):
-                first = sum(PIECES[u][:a])
-                nc.sync.dma_start(x_raw[u][a][:], x_view[:, u * PAIR : (u + 1) * PAIR, first : first + width])
+            cut = T + PIECES[0]
+            nc.sync.dma_start(x_raw[u][:, 0:cut], x_view[:, u * PAIR * T : u * PAIR * T + cut])
+            nc.sync.dma_start(x_raw[u][:, cut:], x_view[:, u * PAIR * T + cut : (u + 1) * PAIR * T])
             if u == 0:
                 nc.sync.dma_start(offsets[:], offs)
+                load_scales(nc.sync, w4_plane, 0, w4_scales)
         nc.sync.dma_start(c_raw, c.rearrange("(p i) j -> p i j", i=PACK))
         load_scales(nc.sync, w8_plane, W8_PLANE_ROW, w8_scales)
-        nc.sync.dma_start(w4[:].bitcast(I32), w4_words[0].bitcast(I32))
         w8_bytes = w8_words[0].rearrange("p n t -> p (n t)")
-        for a in range(CHUNKS):
+
+        def load_w4(a):
+            nc.sync.dma_start(w4[a][:].bitcast(I32), w4_words[0][:, 2 * CHUNK * a : 2 * CHUNK * (a + 1)].bitcast(I32))
+
+        def load_w8(a):
             nc.sync.dma_start(w8[a][:].bitcast(I32), w8_bytes[:, 4 * CHUNK * a : 4 * CHUNK * (a + 1)].bitcast(I32))
+
+        load_w4(0)
+        load_w8(0)
+        load_w8(1)
+        load_w4(1)
 
         bias_psum = banks[TILES - 1][:, S : S + P]
         nc.tensor.transpose(bias_psum, bias_rows[:], identity[:])
-        nc.scalar.copy(bias[:], bias_psum[:, 0:TILES])
 
-        def pair_up(copy, u, first, source):
-            count = source.shape[2]
+        def pair_up(copy, u, first, count):
             copy(
                 pairs[u][:, PAIR * first : PAIR * (first + count)].rearrange("p (t e) -> p t e", e=PAIR),
-                source.rearrange("p e t -> p t e"),
+                x_raw[u][:].rearrange("p (e t) -> p t e", e=PAIR)[:, first : first + count, :],
             )
 
         blocks = staged[:].bitcast(BF16).rearrange("p (k j e) -> p k j e", j=N, e=PAIR)
@@ -121,7 +127,7 @@ def tile_list_sage_gelu_kernel(
         def maximum(h):
             sides = []
             for g in range(G):
-                low, high = HALVES * g + h, HIGH_BLOCK[h][g]
+                low, high = LOW_BLOCK + HALVES * g + h, HIGH_BLOCK[h][g]
                 sides.append(blocks[:, low : high + 1 : high - low].rearrange("p u j e -> p j u e"))
             nc.vector.tensor_max(
                 x_woven[h].rearrange("p (j u e) -> p j u e", u=PACK // PAIR, e=PAIR), sides[0], sides[1]
@@ -131,70 +137,81 @@ def tile_list_sage_gelu_kernel(
             nc.vector.quantize_mx(out=mx[0].bitcast(FP8X4), scales=mx[1], in_=values)
 
         def pair_up_pieces(u):
-            for a, width in enumerate(PIECES[u]):
-                first, share = sum(PIECES[u][:a]), VECTOR_SHARES[u][a]
-                pair_up(nc.vector.tensor_copy, u, first, x_raw[u][a][:, :, 0:share])
-                if share < width:
-                    pair_up(nc.scalar.copy, u, first + share, x_raw[u][a][:, :, share:width])
+            for a, width in enumerate(PIECES):
+                first, share = sum(PIECES[:a]), VECTOR_SHARES[u][a]
+                pair_up(nc.vector.tensor_copy, u, first, share)
+                pair_up(nc.scalar.copy, u, first + share, width - share)
 
         pair_up_pieces(0)
-        nc.vector.tensor_copy(staged[:, 0 : G * S], pairs[0][:].bitcast(U32).indirect(offsets[:]))
+        nc.vector.tensor_copy(staged[:, LOW_BLOCK * N : LOW_BLOCK * N + G * S], pairs[0][:].bitcast(U32).indirect(offsets[:]))
         pair_up_pieces(1)
-        for h in range(HALVES):
+        nc.scalar.copy(bias, bias_psum[:, 0:TILES])
+
+        def weave(h):
             nc.scalar.copy(
                 c_woven[h].rearrange("p (j i) -> p j i", i=PACK),
                 c_raw[:, :, h * N : (h + 1) * N].rearrange("p i j -> p j i"),
             )
+
+        weave(0)
+        weave(1)
         gather_high(0, 0)
         gather_high(0, 1)
         maximum(0)
-        quantize(x_mx[0], x_woven[0])
-        quantize(c_mx[0], c_woven[0])
         gather_high(1, 0)
+        quantize(x_mx[0], x_woven[0])
         gather_high(1, 1)
-        quantize(c_mx[1], c_woven[1])
+        quantize(c_mx[0], c_woven[0])
         maximum(1)
+        quantize(c_mx[1], c_woven[1])
         quantize(x_mx[1], x_woven[1])
 
-        def passes(m, h, start, stop):
-            sums = banks[m][:, h * N : (h + 1) * N]
+        def w4_pass(m, h, sums, start, stop):
+            first = m * P % CHUNK
             nc.tensor.matmul_mx(
                 out=sums,
-                lhsT=w4[:, 2 * m * P : 2 * (m + 1) * P].bitcast(FP4X4),
+                lhsT=w4[m * P // CHUNK][:, 2 * first : 2 * (first + P)].bitcast(FP4X4),
                 lhsT_scale=w4_plane[:, m * P : (m + 1) * P],
                 rhs=x_mx[h][0].bitcast(FP8X4),
                 rhs_scale=x_mx[h][1],
                 start=start,
-                stop=False,
+                stop=stop,
             )
+
+        def w8_pass(m, cols, sums, start, stop):
+            first = m * P % CHUNK
             nc.tensor.matmul_mx(
                 out=sums,
-                lhsT=w8[m * P // CHUNK][:, m * P % CHUNK : m * P % CHUNK + P].bitcast(FP8X4),
+                lhsT=w8[m * P // CHUNK][:, first : first + P].bitcast(FP8X4),
                 lhsT_scale=w8_plane[W8_PLANE_ROW:P, m * P : (m + 1) * P],
-                rhs=c_mx[h][0].bitcast(FP8X4),
-                rhs_scale=c_mx[h][1],
-                start=False,
+                rhs=c_codes[:, cols].bitcast(FP8X4),
+                rhs_scale=c_scale[:, cols],
+                start=start,
                 stop=stop,
             )
 
         out_view = out.rearrange("(m p) j -> p m j", p=P)
 
-        def half_tiles(h):
-            cols = slice(h * N, (h + 1) * N)
-            first = 0
-            for count in EARLY_STORES[h]:
-                res = held([P, count, N], F32, "res%d_%d" % (first, h))
-                for m in range(first, first + count):
-                    passes(m, h, True, True)
-                    nc.scalar.activation(res[:, m - first, :], banks[m][:, cols], GELU, bias=bias[:, m : m + 1])
-                nc.sync.dma_start(out_view[:, first : first + count, cols], res[:])
-                first += count
+        def gelu(res, m, cols):
+            nc.scalar.activation(res, banks[m][:, cols], GELU, bias=bias[:, m : m + 1])
 
-        half_tiles(0)
+        halves = [slice(h * N, (h + 1) * N) for h in range(HALVES)]
+        for m in range(AHEAD):
+            w4_pass(m, 0, banks[m][:, halves[0]], True, False)
+        for h in range(HALVES):
+            for first in range(0, EARLY, TOGETHER):
+                res = held([P, TOGETHER, N], F32, "res%d_%d" % (first, h))
+                for m in range(first, first + TOGETHER):
+                    opened = h == 0 and m < AHEAD
+                    w8_pass(m, halves[h], banks[m][:, halves[h]], not opened, opened)
+                    if not opened:
+                        w4_pass(m, h, banks[m][:, halves[h]], False, True)
+                    gelu(res[:, m - first, :], m, halves[h])
+                nc.sync.dma_start(out_view[:, first : first + TOGETHER, halves[h]], res[:])
         for m in range(EARLY, TILES):
             res = held([P, S], F32, "res%d" % m)
+            w8_pass(m, slice(0, S), banks[m][:, 0:S], True, False)
             for h in range(HALVES):
-                passes(m, h, h == 0, h == HALVES - 1)
-            nc.scalar.activation(res[:], banks[m][:, 0:S], GELU, bias=bias[:, m : m + 1])
+                w4_pass(m, h, banks[m][:, halves[h]], False, h == HALVES - 1)
+            gelu(res[:], m, slice(0, S))
             nc.sync.dma_start(out_view[:, m, :], res[:])
-        half_tiles(1)

@@ -26,8 +26,8 @@ LIST_ROWS = 16
 W8_PLANE_ROW = 4
 CHUNKS = 2
 CHUNK = M // CHUNKS
-PIECES = (640, T - 640)
-VECTOR_SHARES = ((416, 256), (416, 256))
+PIECES = ((640, 384), (512, 320, 192))
+VECTOR_SHARES = ((416, 256), (336, 128, 192))
 EARLY = 4
 AHEAD = 3
 TOGETHER = 2
@@ -61,7 +61,7 @@ def tile_list_sage_gelu_kernel(
         w8_plane = held([P, M], U8, "w8_plane")
         bias_rows = held([P, P], F32, "bias_rows")
         identity = held([P, P], F32, "identity")
-        bias = x_raw[1][:, PAIR * T - TILES :]
+        bias = held([P, TILES], F32, "bias")[:]
         x_mx = [(held([P, N], U32, "x_codes%d" % h)[:], held([P, N], U8, "x_scale%d" % h)[:]) for h in range(HALVES)]
         c_codes = held([P, S], U32, "c_codes")
         c_scale = held([P, S], U8, "c_scale")
@@ -74,7 +74,6 @@ def tile_list_sage_gelu_kernel(
         nc.vector.memset(w8_plane[:].bitcast(U32), 0)
         nc.vector.memset(w4_plane[:].bitcast(U32), 0)
         nc.gpsimd.memset(bias_rows[:], 0.0)
-        nc.gpsimd.dma_start(bias_rows[0:TILES, :], b.rearrange("(m p) -> m p", p=P))
         make_identity(nc, identity[:])
 
         def load_scales(engine, plane, first, src):
@@ -82,16 +81,19 @@ def tile_list_sage_gelu_kernel(
             for r in range(4):
                 engine.dma_start(plane[first + r : P : 32, :].bitcast(I32), rows[r].bitcast(I32))
 
+        load_scales(nc.gpsimd, w8_plane, W8_PLANE_ROW, w8_scales)
+
         x_view = xT.rearrange("(p i) t -> p (i t)", i=PACK)
         for u in range(PACK // PAIR):
-            cut = T + PIECES[0]
-            nc.sync.dma_start(x_raw[u][:, 0:cut], x_view[:, u * PAIR * T : u * PAIR * T + cut])
-            nc.sync.dma_start(x_raw[u][:, cut:], x_view[:, u * PAIR * T + cut : (u + 1) * PAIR * T])
+            for a, width in enumerate(PIECES[u]):
+                last = T + sum(PIECES[u][: a + 1])
+                first = last - width if a > 0 else 0
+                nc.sync.dma_start(x_raw[u][:, first:last], x_view[:, u * PAIR * T + first : u * PAIR * T + last])
             if u == 0:
                 nc.sync.dma_start(offsets[:], offs)
-                load_scales(nc.sync, w4_plane, 0, w4_scales)
+                nc.sync.dma_start(bias_rows[0:TILES, :], b.rearrange("(m p) -> m p", p=P))
         nc.sync.dma_start(c_raw, c.rearrange("(p i) j -> p i j", i=PACK))
-        load_scales(nc.sync, w8_plane, W8_PLANE_ROW, w8_scales)
+        load_scales(nc.sync, w4_plane, 0, w4_scales)
         w8_bytes = w8_words[0].rearrange("p n t -> p (n t)")
 
         def load_w4(a):
@@ -137,10 +139,11 @@ def tile_list_sage_gelu_kernel(
             nc.vector.quantize_mx(out=mx[0].bitcast(FP8X4), scales=mx[1], in_=values)
 
         def pair_up_pieces(u):
-            for a, width in enumerate(PIECES):
-                first, share = sum(PIECES[:a]), VECTOR_SHARES[u][a]
+            for a, width in enumerate(PIECES[u]):
+                first, share = sum(PIECES[u][:a]), VECTOR_SHARES[u][a]
                 pair_up(nc.vector.tensor_copy, u, first, share)
-                pair_up(nc.scalar.copy, u, first + share, width - share)
+                if share < width:
+                    pair_up(nc.scalar.copy, u, first + share, width - share)
 
         pair_up_pieces(0)
         nc.vector.tensor_copy(staged[:, LOW_BLOCK * N : LOW_BLOCK * N + G * S], pairs[0][:].bitcast(U32).indirect(offsets[:]))

@@ -1,7 +1,6 @@
 from contextlib import ExitStack
 
 import concourse.mybir as mybir
-from concourse.masks import make_identity
 
 G, K, M, T, S = 2, 512, 1024, 1024, 256
 FLOPS = 2 * 2 * K * M * S
@@ -29,7 +28,11 @@ CHUNK = M // CHUNKS
 PIECES = ((640, 384), (512, 320, 192))
 VECTOR_SHARES = ((416, 256), (336, 128, 192))
 EARLY = 4
-AHEAD = 3
+AHEAD = 4
+SQUARE = 32
+WIDE = 512
+WARM_PASSES = 2
+BIAS_STEP = SQUARE // TILES
 TOGETHER = 2
 LOW_BLOCK = 0
 HIGH_BLOCK = ((4, 5), (6, 5))
@@ -59,22 +62,22 @@ def tile_list_sage_gelu_kernel(
         w4 = [held([P, 2 * CHUNK], U8, "w4_%d" % a) for a in range(CHUNKS)]
         w4_plane = held([P, M], U8, "w4_plane")
         w8_plane = held([P, M], U8, "w8_plane")
-        bias_rows = held([P, P], F32, "bias_rows")
-        identity = held([P, P], F32, "identity")
-        bias = held([P, TILES], F32, "bias")[:]
+        bias_rows = held([P, SQUARE], F32, "bias_rows")
+        bias = held([P, SQUARE], F32, "bias")
         x_mx = [(held([P, N], U32, "x_codes%d" % h)[:], held([P, N], U8, "x_scale%d" % h)[:]) for h in range(HALVES)]
         c_codes = held([P, S], U32, "c_codes")
         c_scale = held([P, S], U8, "c_scale")
         c_mx = [(c_codes[:, h * N : (h + 1) * N], c_scale[:, h * N : (h + 1) * N]) for h in range(HALVES)]
-        warm = held([P, 2], F32, "warm")
+        warm = held([P, 1], F32, "warm")
+        idle = held([P, 5 * WIDE], U8, "idle")
+        idle_codes, idle_scale = idle[:, 0 : 4 * WIDE].bitcast(U32), idle[:, 4 * WIDE :]
         banks = [psum.tile([P, 512], F32, name="bank%d" % i) for i in range(TILES)]
 
-        nc.vector.memset(warm[:, 0:1], 0.0)
-        nc.scalar.activation(warm[:, 1:2], warm[:, 0:1], GELU)
+        nc.vector.memset(bias_rows[:], 0.0)
         nc.vector.memset(w8_plane[:].bitcast(U32), 0)
         nc.vector.memset(w4_plane[:].bitcast(U32), 0)
-        nc.gpsimd.memset(bias_rows[:], 0.0)
-        make_identity(nc, identity[:])
+        nc.vector.memset(idle[:].bitcast(U32), 0)
+        nc.scalar.activation(warm[:], idle_codes[:, WIDE - 1 : WIDE].bitcast(F32), GELU)
 
         def load_scales(engine, plane, first, src):
             rows = src[0].rearrange("(q r) n -> r q n", r=4)
@@ -91,7 +94,9 @@ def tile_list_sage_gelu_kernel(
                 nc.sync.dma_start(x_raw[u][:, first:last], x_view[:, u * PAIR * T + first : u * PAIR * T + last])
             if u == 0:
                 nc.sync.dma_start(offsets[:], offs)
-                nc.sync.dma_start(bias_rows[0:TILES, :], b.rearrange("(m p) -> m p", p=P))
+                nc.sync.dma_start(
+                    bias_rows[0:P:BIAS_STEP, :], b.rearrange("(m q a) -> q m a", m=TILES, a=SQUARE)
+                )
         nc.sync.dma_start(c_raw, c.rearrange("(p i) j -> p i j", i=PACK))
         load_scales(nc.sync, w4_plane, 0, w4_scales)
         w8_bytes = w8_words[0].rearrange("p n t -> p (n t)")
@@ -107,8 +112,6 @@ def tile_list_sage_gelu_kernel(
         load_w8(1)
         load_w4(1)
 
-        bias_psum = banks[TILES - 1][:, S : S + P]
-        nc.tensor.transpose(bias_psum, bias_rows[:], identity[:])
 
         def pair_up(copy, u, first, count):
             copy(
@@ -147,8 +150,20 @@ def tile_list_sage_gelu_kernel(
 
         pair_up_pieces(0)
         nc.vector.tensor_copy(staged[:, LOW_BLOCK * N : LOW_BLOCK * N + G * S], pairs[0][:].bitcast(U32).indirect(offsets[:]))
+        nc.vector.transpose(bias[:], bias_rows[:])
         pair_up_pieces(1)
-        nc.scalar.copy(bias, bias_psum[:, 0:TILES])
+        late = PAIR * (PIECES[1][0] + VECTOR_SHARES[1][1])
+        quantize((idle_codes[:, 0:SQUARE], idle_scale[:, 0:SQUARE]), pairs[1][:, late : late + PACK * SQUARE])
+        for a in range(WARM_PASSES):
+            nc.tensor.matmul_mx(
+                out=banks[TILES - 1][0:SQUARE, :],
+                lhsT=idle_codes[:, 0:SQUARE].bitcast(FP8X4),
+                lhsT_scale=idle_scale[:, 0:SQUARE],
+                rhs=idle_codes.bitcast(FP8X4),
+                rhs_scale=idle_scale,
+                start=True,
+                stop=True,
+            )
 
         def weave(h):
             nc.scalar.copy(
@@ -196,7 +211,7 @@ def tile_list_sage_gelu_kernel(
         out_view = out.rearrange("(m p) j -> p m j", p=P)
 
         def gelu(res, m, cols):
-            nc.scalar.activation(res, banks[m][:, cols], GELU, bias=bias[:, m : m + 1])
+            nc.scalar.activation(res, banks[m][:, cols], GELU, bias=bias[:, BIAS_STEP * m : BIAS_STEP * m + 1])
 
         halves = [slice(h * N, (h + 1) * N) for h in range(HALVES)]
         for m in range(AHEAD):

@@ -21,22 +21,22 @@ PAIR = 2
 N = 128
 HALVES = S // N
 TILES = M // P
+BANK = 512
 LIST_ROWS = 16
+QUADRANT = 32
+SCALE_ROWS = 4
 W8_PLANE_ROW = 4
 CHUNKS = 2
 CHUNK = M // CHUNKS
 PIECES = ((640, 384), (512, 320, 192))
 VECTOR_SHARES = ((416, 256), (336, 128, 192))
 EARLY = 4
-AHEAD = 4
-SQUARE = 32
-WIDE = 512
-WARM_PASSES = 2
-BIAS_STEP = SQUARE // TILES
 TOGETHER = 2
-LOW_BLOCK = 0
+BIAS_STEP = QUADRANT // TILES
 HIGH_BLOCK = ((4, 5), (6, 5))
 BLOCKS = 7
+WARM_PASSES = 3
+WARM_ROWS = 32
 
 
 def tile_list_sage_gelu_kernel(
@@ -62,41 +62,42 @@ def tile_list_sage_gelu_kernel(
         w4 = [held([P, 2 * CHUNK], U8, "w4_%d" % a) for a in range(CHUNKS)]
         w4_plane = held([P, M], U8, "w4_plane")
         w8_plane = held([P, M], U8, "w8_plane")
-        bias_rows = held([P, SQUARE], F32, "bias_rows")
-        bias = held([P, SQUARE], F32, "bias")
+        bias_rows = held([P, QUADRANT], F32, "bias_rows")
+        bias = held([P, QUADRANT], F32, "bias")
         x_mx = [(held([P, N], U32, "x_codes%d" % h)[:], held([P, N], U8, "x_scale%d" % h)[:]) for h in range(HALVES)]
         c_codes = held([P, S], U32, "c_codes")
         c_scale = held([P, S], U8, "c_scale")
         c_mx = [(c_codes[:, h * N : (h + 1) * N], c_scale[:, h * N : (h + 1) * N]) for h in range(HALVES)]
         warm = held([P, 1], F32, "warm")
-        idle = held([P, 5 * WIDE], U8, "idle")
-        idle_codes, idle_scale = idle[:, 0 : 4 * WIDE].bitcast(U32), idle[:, 4 * WIDE :]
-        banks = [psum.tile([P, 512], F32, name="bank%d" % i) for i in range(TILES)]
+        idle = held([P, (PACK + 1) * BANK], U8, "idle")
+        idle_codes, idle_scale = idle[:, 0 : PACK * BANK].bitcast(U32), idle[:, PACK * BANK :]
+        banks = [psum.tile([P, BANK], F32, name="bank%d" % m) for m in range(TILES)]
 
         nc.vector.memset(bias_rows[:], 0.0)
         nc.vector.memset(w8_plane[:].bitcast(U32), 0)
         nc.vector.memset(w4_plane[:].bitcast(U32), 0)
         nc.vector.memset(idle[:].bitcast(U32), 0)
-        nc.scalar.activation(warm[:], idle_codes[:, WIDE - 1 : WIDE].bitcast(F32), GELU)
+        nc.scalar.activation(warm[:], idle_codes[:, BANK - 1 : BANK].bitcast(F32), GELU)
 
-        def load_scales(engine, plane, first, src):
-            rows = src[0].rearrange("(q r) n -> r q n", r=4)
-            for r in range(4):
-                engine.dma_start(plane[first + r : P : 32, :].bitcast(I32), rows[r].bitcast(I32))
+        def load_scales(engine, plane, first_row, src):
+            rows = src[0].rearrange("(q r) n -> r q n", r=SCALE_ROWS)
+            for r in range(SCALE_ROWS):
+                engine.dma_start(plane[first_row + r : P : QUADRANT, :].bitcast(I32), rows[r].bitcast(I32))
 
         load_scales(nc.gpsimd, w8_plane, W8_PLANE_ROW, w8_scales)
 
         x_view = xT.rearrange("(p i) t -> p (i t)", i=PACK)
-        for u in range(PACK // PAIR):
+
+        def load_pair(u):
             for a, width in enumerate(PIECES[u]):
                 last = T + sum(PIECES[u][: a + 1])
                 first = last - width if a > 0 else 0
                 nc.sync.dma_start(x_raw[u][:, first:last], x_view[:, u * PAIR * T + first : u * PAIR * T + last])
-            if u == 0:
-                nc.sync.dma_start(offsets[:], offs)
-                nc.sync.dma_start(
-                    bias_rows[0:P:BIAS_STEP, :], b.rearrange("(m q a) -> q m a", m=TILES, a=SQUARE)
-                )
+
+        load_pair(0)
+        nc.sync.dma_start(offsets[:], offs)
+        nc.sync.dma_start(bias_rows[0:P:BIAS_STEP, :], b.rearrange("(m q a) -> q m a", m=TILES, a=QUADRANT))
+        load_pair(1)
         nc.sync.dma_start(c_raw, c.rearrange("(p i) j -> p i j", i=PACK))
         load_scales(nc.sync, w4_plane, 0, w4_scales)
         w8_bytes = w8_words[0].rearrange("p n t -> p (n t)")
@@ -112,14 +113,18 @@ def tile_list_sage_gelu_kernel(
         load_w8(1)
         load_w4(1)
 
-
         def pair_up(copy, u, first, count):
             copy(
                 pairs[u][:, PAIR * first : PAIR * (first + count)].rearrange("p (t e) -> p t e", e=PAIR),
                 x_raw[u][:].rearrange("p (e t) -> p t e", e=PAIR)[:, first : first + count, :],
             )
 
-        blocks = staged[:].bitcast(BF16).rearrange("p (k j e) -> p k j e", j=N, e=PAIR)
+        def pair_up_pieces(u):
+            for a, width in enumerate(PIECES[u]):
+                first, share = sum(PIECES[u][:a]), VECTOR_SHARES[u][a]
+                pair_up(nc.vector.tensor_copy, u, first, share)
+                if share < width:
+                    pair_up(nc.scalar.copy, u, first + share, width - share)
 
         def gather_high(h, g):
             first = (g * S + h * N) // LIST_ROWS
@@ -129,46 +134,45 @@ def tile_list_sage_gelu_kernel(
                 pairs[1][:].bitcast(U32).indirect(offsets[:, first : first + N // LIST_ROWS]),
             )
 
+        blocks = staged[:].bitcast(BF16).rearrange("p (k j e) -> p k j e", j=N, e=PAIR)
+
         def maximum(h):
             sides = []
             for g in range(G):
-                low, high = LOW_BLOCK + HALVES * g + h, HIGH_BLOCK[h][g]
+                low, high = HALVES * g + h, HIGH_BLOCK[h][g]
                 sides.append(blocks[:, low : high + 1 : high - low].rearrange("p u j e -> p j u e"))
             nc.vector.tensor_max(
                 x_woven[h].rearrange("p (j u e) -> p j u e", u=PACK // PAIR, e=PAIR), sides[0], sides[1]
-            )
-
-        def quantize(mx, values):
-            nc.vector.quantize_mx(out=mx[0].bitcast(FP8X4), scales=mx[1], in_=values)
-
-        def pair_up_pieces(u):
-            for a, width in enumerate(PIECES[u]):
-                first, share = sum(PIECES[u][:a]), VECTOR_SHARES[u][a]
-                pair_up(nc.vector.tensor_copy, u, first, share)
-                if share < width:
-                    pair_up(nc.scalar.copy, u, first + share, width - share)
-
-        pair_up_pieces(0)
-        nc.vector.tensor_copy(staged[:, LOW_BLOCK * N : LOW_BLOCK * N + G * S], pairs[0][:].bitcast(U32).indirect(offsets[:]))
-        nc.vector.transpose(bias[:], bias_rows[:])
-        pair_up_pieces(1)
-        late = PAIR * (PIECES[1][0] + VECTOR_SHARES[1][1])
-        quantize((idle_codes[:, 0:SQUARE], idle_scale[:, 0:SQUARE]), pairs[1][:, late : late + PACK * SQUARE])
-        for a in range(WARM_PASSES):
-            nc.tensor.matmul_mx(
-                out=banks[TILES - 1][0:SQUARE, :],
-                lhsT=idle_codes[:, 0:SQUARE].bitcast(FP8X4),
-                lhsT_scale=idle_scale[:, 0:SQUARE],
-                rhs=idle_codes.bitcast(FP8X4),
-                rhs_scale=idle_scale,
-                start=True,
-                stop=True,
             )
 
         def weave(h):
             nc.scalar.copy(
                 c_woven[h].rearrange("p (j i) -> p j i", i=PACK),
                 c_raw[:, :, h * N : (h + 1) * N].rearrange("p i j -> p j i"),
+            )
+
+        def quantize(mx, values):
+            nc.vector.quantize_mx(out=mx[0].bitcast(FP8X4), scales=mx[1], in_=values)
+
+        pair_up_pieces(0)
+        nc.vector.tensor_copy(staged[:, 0 : G * S], pairs[0][:].bitcast(U32).indirect(offsets[:]))
+        nc.vector.transpose(bias[:], bias_rows[:])
+        pair_up_pieces(1)
+
+        last_of_scalar = PAIR * (PIECES[1][0] + VECTOR_SHARES[1][1])
+        quantize(
+            (idle_codes[:, 0:WARM_ROWS], idle_scale[:, 0:WARM_ROWS]),
+            pairs[1][:, last_of_scalar : last_of_scalar + PACK * WARM_ROWS],
+        )
+        for warm_pass in range(WARM_PASSES):
+            nc.tensor.matmul_mx(
+                out=banks[TILES - 1][0:WARM_ROWS, :],
+                lhsT=idle_codes[:, 0:WARM_ROWS].bitcast(FP8X4),
+                lhsT_scale=idle_scale[:, 0:WARM_ROWS],
+                rhs=idle_codes.bitcast(FP8X4),
+                rhs_scale=idle_scale,
+                start=True,
+                stop=True,
             )
 
         weave(0)
@@ -184,10 +188,12 @@ def tile_list_sage_gelu_kernel(
         quantize(c_mx[1], c_woven[1])
         quantize(x_mx[1], x_woven[1])
 
-        def w4_pass(m, h, sums, start, stop):
+        halves = [slice(h * N, (h + 1) * N) for h in range(HALVES)]
+
+        def w4_pass(m, h, start, stop):
             first = m * P % CHUNK
             nc.tensor.matmul_mx(
-                out=sums,
+                out=banks[m][:, halves[h]],
                 lhsT=w4[m * P // CHUNK][:, 2 * first : 2 * (first + P)].bitcast(FP4X4),
                 lhsT_scale=w4_plane[:, m * P : (m + 1) * P],
                 rhs=x_mx[h][0].bitcast(FP8X4),
@@ -196,10 +202,10 @@ def tile_list_sage_gelu_kernel(
                 stop=stop,
             )
 
-        def w8_pass(m, cols, sums, start, stop):
+        def w8_pass(m, cols, start, stop):
             first = m * P % CHUNK
             nc.tensor.matmul_mx(
-                out=sums,
+                out=banks[m][:, cols],
                 lhsT=w8[m * P // CHUNK][:, first : first + P].bitcast(FP8X4),
                 lhsT_scale=w8_plane[W8_PLANE_ROW:P, m * P : (m + 1) * P],
                 rhs=c_codes[:, cols].bitcast(FP8X4),
@@ -208,28 +214,33 @@ def tile_list_sage_gelu_kernel(
                 stop=stop,
             )
 
-        out_view = out.rearrange("(m p) j -> p m j", p=P)
-
         def gelu(res, m, cols):
             nc.scalar.activation(res, banks[m][:, cols], GELU, bias=bias[:, BIAS_STEP * m : BIAS_STEP * m + 1])
 
-        halves = [slice(h * N, (h + 1) * N) for h in range(HALVES)]
-        for m in range(AHEAD):
-            w4_pass(m, 0, banks[m][:, halves[0]], True, False)
-        for h in range(HALVES):
+        out_view = out.rearrange("(m p) j -> p m j", p=P)
+
+        def early_tiles(h, passes):
             for first in range(0, EARLY, TOGETHER):
                 res = held([P, TOGETHER, N], F32, "res%d_%d" % (first, h))
                 for m in range(first, first + TOGETHER):
-                    opened = h == 0 and m < AHEAD
-                    w8_pass(m, halves[h], banks[m][:, halves[h]], not opened, opened)
-                    if not opened:
-                        w4_pass(m, h, banks[m][:, halves[h]], False, True)
+                    passes(m)
                     gelu(res[:, m - first, :], m, halves[h])
                 nc.sync.dma_start(out_view[:, first : first + TOGETHER, halves[h]], res[:])
+
+        def second_half(m):
+            w8_pass(m, halves[1], True, False)
+            w4_pass(m, 1, False, True)
+
+        for m in range(EARLY):
+            w4_pass(m, 0, True, False)
+        early_tiles(0, lambda m: w8_pass(m, halves[0], False, True))
+        for m in range(EARLY, TILES):
+            w8_pass(m, halves[0], True, False)
+        early_tiles(1, second_half)
         for m in range(EARLY, TILES):
             res = held([P, S], F32, "res%d" % m)
-            w8_pass(m, slice(0, S), banks[m][:, 0:S], True, False)
+            w8_pass(m, halves[1], False, False)
             for h in range(HALVES):
-                w4_pass(m, h, banks[m][:, halves[h]], False, h == HALVES - 1)
+                w4_pass(m, h, False, h == HALVES - 1)
             gelu(res[:], m, slice(0, S))
             nc.sync.dma_start(out_view[:, m, :], res[:])

@@ -26,15 +26,18 @@ LIST_ROWS = 16
 QUADRANT = 32
 SCALE_ROWS = 4
 W8_PLANE_ROW = 4
-CHUNKS = 2
-CHUNK = M // CHUNKS
+FIRST_TILES = 3
+CHUNK_TILES = (range(0, FIRST_TILES), range(FIRST_TILES, TILES))
 PIECES = ((640, 384), (512, 320, 192))
 VECTOR_SHARES = ((416, 256), (336, 128, 192))
-EARLY = 4
-TOGETHER = 2
+EARLY = 6
+STORES = (((0,), (1, 2), (3,), (4, 5)), ((3, 4, 5), (0, 1), (2,)))
+AHEAD = (0, EARLY, EARLY + 1)
 BIAS_STEP = QUADRANT // TILES
-HIGH_BLOCK = ((4, 5), (6, 5))
-BLOCKS = 7
+LEAD = 16
+HIGH_AT = ((G * S, G * S + 3 * N - LEAD), (G * S + N, G * S + 2 * N))
+C_AT = G * S + 5 * N
+ROOM = C_AT + PACK * S
 WARM_PASSES = 3
 WARM_ROWS = 32
 
@@ -53,31 +56,29 @@ def tile_list_sage_gelu_kernel(
         offsets = pool.tile([P, G * S // LIST_ROWS], U16, name="offsets")
         x_raw = [held([P, PAIR * T], F32, "x_raw%d" % u) for u in range(PACK // PAIR)]
         pairs = [held([P, T * PAIR], BF16, "pairs%d" % u) for u in range(PACK // PAIR)]
-        staged = held([P, BLOCKS * N], U32, "staged")
-        c_room = held([P, N + PACK * S], F32, "c_room")
-        c_raw = c_room[:, N:].rearrange("p (i j) -> p i j", i=PACK)
-        x_woven = [held([P, N * PACK], BF16, "x_woven0")[:], c_room[:, 0 : 2 * N].bitcast(BF16)]
+        room = held([P, ROOM], F32, "room")
+        staged = room[:].bitcast(U32)
+        c_raw = room[:, C_AT:].rearrange("p (i j) -> p i j", i=PACK)
+        x_woven = [held([P, N * PACK], BF16, "x_woven0")[:], room[:, C_AT - N : C_AT + N].bitcast(BF16)]
         c_woven = [held([P, N * PACK], BF16, "c_woven%d" % h)[:] for h in range(HALVES)]
-        w8 = [held([P, CHUNK], U32, "w8_%d" % a) for a in range(CHUNKS)]
-        w4 = [held([P, 2 * CHUNK], U8, "w4_%d" % a) for a in range(CHUNKS)]
+        w8 = [held([P, P * len(tiles)], U32, "w8_%d" % tiles.start) for tiles in CHUNK_TILES]
+        w4 = held([P, 2 * M], U8, "w4")
         w4_plane = held([P, M], U8, "w4_plane")
         w8_plane = held([P, M], U8, "w8_plane")
         bias_rows = held([P, QUADRANT], F32, "bias_rows")
         bias = held([P, QUADRANT], F32, "bias")
         x_mx = [(held([P, N], U32, "x_codes%d" % h)[:], held([P, N], U8, "x_scale%d" % h)[:]) for h in range(HALVES)]
-        c_codes = held([P, S], U32, "c_codes")
-        c_scale = held([P, S], U8, "c_scale")
-        c_mx = [(c_codes[:, h * N : (h + 1) * N], c_scale[:, h * N : (h + 1) * N]) for h in range(HALVES)]
+        c_mx = [(held([P, N], U32, "c_codes%d" % h)[:], held([P, N], U8, "c_scale%d" % h)[:]) for h in range(HALVES)]
         warm = held([P, 1], F32, "warm")
-        idle = held([P, (PACK + 1) * BANK], U8, "idle")
-        idle_codes, idle_scale = idle[:, 0 : PACK * BANK].bitcast(U32), idle[:, PACK * BANK :]
+        idle = held([P, (PACK + 1) * BANK + PACK], U8, "idle")
+        idle_codes, idle_scale = idle[:, 0 : PACK * BANK].bitcast(U32), idle[:, PACK * BANK : (PACK + 1) * BANK]
         banks = [psum.tile([P, BANK], F32, name="bank%d" % m) for m in range(TILES)]
 
         nc.vector.memset(bias_rows[:], 0.0)
         nc.vector.memset(w8_plane[:].bitcast(U32), 0)
         nc.vector.memset(w4_plane[:].bitcast(U32), 0)
         nc.vector.memset(idle[:].bitcast(U32), 0)
-        nc.scalar.activation(warm[:], idle_codes[:, BANK - 1 : BANK].bitcast(F32), GELU)
+        nc.scalar.activation(warm[:], idle[:, (PACK + 1) * BANK :].bitcast(F32), GELU)
 
         def load_scales(engine, plane, first_row, src):
             rows = src[0].rearrange("(q r) n -> r q n", r=SCALE_ROWS)
@@ -99,19 +100,11 @@ def tile_list_sage_gelu_kernel(
         nc.sync.dma_start(bias_rows[0:P:BIAS_STEP, :], b.rearrange("(m q a) -> q m a", m=TILES, a=QUADRANT))
         load_pair(1)
         nc.sync.dma_start(c_raw, c.rearrange("(p i) j -> p i j", i=PACK))
+        nc.sync.dma_start(w4[:].bitcast(I32), w4_words[0].bitcast(I32))
         load_scales(nc.sync, w4_plane, 0, w4_scales)
         w8_bytes = w8_words[0].rearrange("p n t -> p (n t)")
-
-        def load_w4(a):
-            nc.sync.dma_start(w4[a][:].bitcast(I32), w4_words[0][:, 2 * CHUNK * a : 2 * CHUNK * (a + 1)].bitcast(I32))
-
-        def load_w8(a):
-            nc.sync.dma_start(w8[a][:].bitcast(I32), w8_bytes[:, 4 * CHUNK * a : 4 * CHUNK * (a + 1)].bitcast(I32))
-
-        load_w4(0)
-        load_w8(0)
-        load_w8(1)
-        load_w4(1)
+        for a, tiles in enumerate(CHUNK_TILES):
+            nc.sync.dma_start(w8[a][:].bitcast(I32), w8_bytes[:, 4 * P * tiles.start : 4 * P * tiles.stop].bitcast(I32))
 
         def pair_up(copy, u, first, count):
             copy(
@@ -128,27 +121,25 @@ def tile_list_sage_gelu_kernel(
 
         def gather_high(h, g):
             first = (g * S + h * N) // LIST_ROWS
-            place = HIGH_BLOCK[h][g] * N
+            place = HIGH_AT[h][g]
             nc.vector.tensor_copy(
                 staged[:, place : place + N],
                 pairs[1][:].bitcast(U32).indirect(offsets[:, first : first + N // LIST_ROWS]),
             )
 
-        blocks = staged[:].bitcast(BF16).rearrange("p (k j e) -> p k j e", j=N, e=PAIR)
-
-        def maximum(h):
+        def maximum(h, nodes):
             sides = []
             for g in range(G):
-                low, high = HALVES * g + h, HIGH_BLOCK[h][g]
-                sides.append(blocks[:, low : high + 1 : high - low].rearrange("p u j e -> p j u e"))
-            nc.vector.tensor_max(
-                x_woven[h].rearrange("p (j u e) -> p j u e", u=PACK // PAIR, e=PAIR), sides[0], sides[1]
-            )
+                low, high = g * S + h * N, HIGH_AT[h][g]
+                both = room[:, low : 2 * high - low].bitcast(BF16)
+                sides.append(both.rearrange("p (u j e) -> p j u e", u=PACK // PAIR, e=PAIR)[:, nodes])
+            woven = x_woven[h].rearrange("p (j u e) -> p j u e", u=PACK // PAIR, e=PAIR)
+            nc.vector.tensor_max(woven[:, nodes], sides[0], sides[1])
 
         def weave(h):
             nc.scalar.copy(
-                c_woven[h].rearrange("p (j i) -> p j i", i=PACK),
-                c_raw[:, :, h * N : (h + 1) * N].rearrange("p i j -> p j i"),
+                c_woven[h].rearrange("p (a j i) -> p a i j", j=PACK, i=PACK),
+                c_raw[:, :, h * N : (h + 1) * N].rearrange("p i (a j) -> p a i j", j=PACK),
             )
 
         def quantize(mx, values):
@@ -179,22 +170,30 @@ def tile_list_sage_gelu_kernel(
         weave(1)
         gather_high(0, 0)
         gather_high(0, 1)
-        maximum(0)
+        maximum(0, slice(0, LEAD))
+        maximum(0, slice(LEAD, N))
         gather_high(1, 0)
         quantize(x_mx[0], x_woven[0])
         gather_high(1, 1)
         quantize(c_mx[0], c_woven[0])
-        maximum(1)
+        maximum(1, slice(0, N))
         quantize(c_mx[1], c_woven[1])
         quantize(x_mx[1], x_woven[1])
 
         halves = [slice(h * N, (h + 1) * N) for h in range(HALVES)]
 
+        def place(m):
+            a = 0 if m < FIRST_TILES else 1
+            return a, (m - CHUNK_TILES[a].start) * P
+
+        def sums(m, cols):
+            second = m < EARLY and cols == halves[1]
+            return banks[(m + FIRST_TILES) % EARLY if second else m][:, cols]
+
         def w4_pass(m, h, start, stop):
-            first = m * P % CHUNK
             nc.tensor.matmul_mx(
-                out=banks[m][:, halves[h]],
-                lhsT=w4[m * P // CHUNK][:, 2 * first : 2 * (first + P)].bitcast(FP4X4),
+                out=sums(m, halves[h]),
+                lhsT=w4[:, 2 * P * m : 2 * P * (m + 1)].bitcast(FP4X4),
                 lhsT_scale=w4_plane[:, m * P : (m + 1) * P],
                 rhs=x_mx[h][0].bitcast(FP8X4),
                 rhs_scale=x_mx[h][1],
@@ -202,45 +201,49 @@ def tile_list_sage_gelu_kernel(
                 stop=stop,
             )
 
-        def w8_pass(m, cols, start, stop):
-            first = m * P % CHUNK
+        def w8_pass(m, h, start, stop):
+            a, first = place(m)
             nc.tensor.matmul_mx(
-                out=banks[m][:, cols],
-                lhsT=w8[m * P // CHUNK][:, first : first + P].bitcast(FP8X4),
+                out=sums(m, halves[h]),
+                lhsT=w8[a][:, first : first + P].bitcast(FP8X4),
                 lhsT_scale=w8_plane[W8_PLANE_ROW:P, m * P : (m + 1) * P],
-                rhs=c_codes[:, cols].bitcast(FP8X4),
-                rhs_scale=c_scale[:, cols],
+                rhs=c_mx[h][0].bitcast(FP8X4),
+                rhs_scale=c_mx[h][1],
                 start=start,
                 stop=stop,
             )
 
         def gelu(res, m, cols):
-            nc.scalar.activation(res, banks[m][:, cols], GELU, bias=bias[:, BIAS_STEP * m : BIAS_STEP * m + 1])
+            nc.scalar.activation(res, sums(m, cols), GELU, bias=bias[:, BIAS_STEP * m : BIAS_STEP * m + 1])
 
         out_view = out.rearrange("(m p) j -> p m j", p=P)
 
-        def early_tiles(h, passes):
-            for first in range(0, EARLY, TOGETHER):
-                res = held([P, TOGETHER, N], F32, "res%d_%d" % (first, h))
-                for m in range(first, first + TOGETHER):
-                    passes(m)
-                    gelu(res[:, m - first, :], m, halves[h])
-                nc.sync.dma_start(out_view[:, first : first + TOGETHER, halves[h]], res[:])
+        def finish(h, tiles, passes):
+            res = held([P, len(tiles), N], F32, "res%d_%d" % (tiles[0], h))
+            for m in tiles:
+                passes(m)
+                gelu(res[:, m - tiles[0], :], m, halves[h])
+            nc.sync.dma_start(out_view[:, tiles[0] : tiles[-1] + 1, halves[h]], res[:])
+
+        def first_half(m):
+            w8_pass(m, 0, m not in AHEAD, m in AHEAD)
+            if m not in AHEAD:
+                w4_pass(m, 0, False, True)
 
         def second_half(m):
-            w8_pass(m, halves[1], True, False)
+            w8_pass(m, 1, True, False)
             w4_pass(m, 1, False, True)
 
-        for m in range(EARLY):
+        for m in AHEAD:
             w4_pass(m, 0, True, False)
-        early_tiles(0, lambda m: w8_pass(m, halves[0], False, True))
-        for m in range(EARLY, TILES):
-            w8_pass(m, halves[0], True, False)
-        early_tiles(1, second_half)
+        for tiles in STORES[0]:
+            finish(0, tiles, first_half)
         for m in range(EARLY, TILES):
             res = held([P, S], F32, "res%d" % m)
-            w8_pass(m, halves[1], False, False)
             for h in range(HALVES):
-                w4_pass(m, h, False, h == HALVES - 1)
+                w8_pass(m, h, False, False)
+            w4_pass(m, 1, False, True)
             gelu(res[:], m, slice(0, S))
             nc.sync.dma_start(out_view[:, m, :], res[:])
+        for tiles in STORES[1]:
+            finish(1, tiles, second_half)

@@ -25,14 +25,15 @@ BANK = 512
 LIST_ROWS = 16
 QUADRANT = 32
 SCALE_ROWS = 4
-W8_PLANE_ROW = 4
-FIRST_TILES = 3
+W8_PLANES = 4
+W8_PLANE = M // W8_PLANES
+FIRST_TILES = 4
 CHUNK_TILES = (range(0, FIRST_TILES), range(FIRST_TILES, TILES))
 PIECES = ((640, 384), (512, 320, 192))
 VECTOR_SHARES = ((416, 256), (336, 128, 192))
-EARLY = 6
-STORES = (((0,), (1, 2), (3,), (4, 5)), ((3, 4, 5), (0, 1), (2,)))
-AHEAD = (0, EARLY, EARLY + 1)
+EARLY = 4
+STORES = (((0,), (1,), (2, 3)), ((0, 1, 2), (3,)))
+AHEAD = (0, EARLY)
 BIAS_STEP = QUADRANT // TILES
 LEAD = 16
 HIGH_AT = ((G * S, G * S + 3 * N - LEAD), (G * S + N, G * S + 2 * N))
@@ -64,7 +65,7 @@ def tile_list_sage_gelu_kernel(
         w8 = [held([P, P * len(tiles)], U32, "w8_%d" % tiles.start) for tiles in CHUNK_TILES]
         w4 = held([P, 2 * M], U8, "w4")
         w4_plane = held([P, M], U8, "w4_plane")
-        w8_plane = held([P, M], U8, "w8_plane")
+        w8_plane = held([P, W8_PLANE], U8, "w8_plane")
         bias_rows = held([P, QUADRANT], F32, "bias_rows")
         bias = held([P, QUADRANT], F32, "bias")
         x_mx = [(held([P, N], U32, "x_codes%d" % h)[:], held([P, N], U8, "x_scale%d" % h)[:]) for h in range(HALVES)]
@@ -80,12 +81,12 @@ def tile_list_sage_gelu_kernel(
         nc.vector.memset(idle[:].bitcast(U32), 0)
         nc.scalar.activation(warm[:], idle[:, (PACK + 1) * BANK :].bitcast(F32), GELU)
 
-        def load_scales(engine, plane, first_row, src):
-            rows = src[0].rearrange("(q r) n -> r q n", r=SCALE_ROWS)
-            for r in range(SCALE_ROWS):
-                engine.dma_start(plane[first_row + r : P : QUADRANT, :].bitcast(I32), rows[r].bitcast(I32))
-
-        load_scales(nc.gpsimd, w8_plane, W8_PLANE_ROW, w8_scales)
+        for first in range(0, P, QUADRANT):
+            rows = w8_scales[0][first // QUADRANT * SCALE_ROWS : (first // QUADRANT + 1) * SCALE_ROWS, :]
+            nc.gpsimd.dma_start(
+                w8_plane[first : first + W8_PLANES * SCALE_ROWS, :].bitcast(I32),
+                rows.bitcast(I32).rearrange("r (a n) -> a r n", a=W8_PLANES),
+            )
 
         x_view = xT.rearrange("(p i) t -> p (i t)", i=PACK)
 
@@ -101,7 +102,9 @@ def tile_list_sage_gelu_kernel(
         load_pair(1)
         nc.sync.dma_start(c_raw, c.rearrange("(p i) j -> p i j", i=PACK))
         nc.sync.dma_start(w4[:].bitcast(I32), w4_words[0].bitcast(I32))
-        load_scales(nc.sync, w4_plane, 0, w4_scales)
+        w4_rows = w4_scales[0].rearrange("(q r) n -> r q n", r=SCALE_ROWS)
+        for r in range(SCALE_ROWS):
+            nc.sync.dma_start(w4_plane[r:P:QUADRANT, :].bitcast(I32), w4_rows[r].bitcast(I32))
         w8_bytes = w8_words[0].rearrange("p n t -> p (n t)")
         for a, tiles in enumerate(CHUNK_TILES):
             nc.sync.dma_start(w8[a][:].bitcast(I32), w8_bytes[:, 4 * P * tiles.start : 4 * P * tiles.stop].bitcast(I32))
@@ -188,7 +191,7 @@ def tile_list_sage_gelu_kernel(
 
         def sums(m, cols):
             second = m < EARLY and cols == halves[1]
-            return banks[(m + FIRST_TILES) % EARLY if second else m][:, cols]
+            return banks[m + EARLY - 1 if second else m][:, cols]
 
         def w4_pass(m, h, start, stop):
             nc.tensor.matmul_mx(
@@ -206,7 +209,7 @@ def tile_list_sage_gelu_kernel(
             nc.tensor.matmul_mx(
                 out=sums(m, halves[h]),
                 lhsT=w8[a][:, first : first + P].bitcast(FP8X4),
-                lhsT_scale=w8_plane[W8_PLANE_ROW:P, m * P : (m + 1) * P],
+                lhsT_scale=w8_plane[m * P // W8_PLANE * SCALE_ROWS : P, m * P % W8_PLANE : m * P % W8_PLANE + P],
                 rhs=c_mx[h][0].bitcast(FP8X4),
                 rhs_scale=c_mx[h][1],
                 start=start,
@@ -240,8 +243,10 @@ def tile_list_sage_gelu_kernel(
             finish(0, tiles, first_half)
         for m in range(EARLY, TILES):
             res = held([P, S], F32, "res%d" % m)
-            for h in range(HALVES):
-                w8_pass(m, h, False, False)
+            w8_pass(m, 0, m not in AHEAD, False)
+            if m not in AHEAD:
+                w4_pass(m, 0, False, False)
+            w8_pass(m, 1, False, False)
             w4_pass(m, 1, False, True)
             gelu(res[:], m, slice(0, S))
             nc.sync.dma_start(out_view[:, m, :], res[:])

@@ -31,9 +31,13 @@ FIRST_TILES = 4
 CHUNK_TILES = (range(0, FIRST_TILES), range(FIRST_TILES, TILES))
 PIECES = ((640, 384), (512, 320, 192))
 VECTOR_SHARES = ((416, 256), (336, 128, 192))
-EARLY = 4
-STORES = (((0,), (1,), (2, 3)), ((0, 1, 2), (3,)))
-AHEAD = (0, EARLY)
+EARLY = 3
+STORES = (
+    [((m,), (0,)) for m in range(EARLY)]
+    + [((m,), (0, 1)) for m in range(EARLY, TILES)]
+    + [(tuple(range(EARLY)), (1,))]
+)
+AHEAD = 2
 BIAS_STEP = QUADRANT // TILES
 LEAD = 16
 HIGH_AT = ((G * S, G * S + 3 * N - LEAD), (G * S + N, G * S + 2 * N))
@@ -67,7 +71,8 @@ def tile_list_sage_gelu_kernel(
         w4_plane = held([P, M], U8, "w4_plane")
         w8_plane = held([P, W8_PLANE], U8, "w8_plane")
         bias_rows = held([P, QUADRANT], F32, "bias_rows")
-        bias = held([P, QUADRANT], F32, "bias")
+        last_of_scalar = PIECES[1][0] + VECTOR_SHARES[1][1]
+        bias = x_raw[1][:, last_of_scalar : last_of_scalar + QUADRANT]
         x_mx = [(held([P, N], U32, "x_codes%d" % h)[:], held([P, N], U8, "x_scale%d" % h)[:]) for h in range(HALVES)]
         c_mx = [(held([P, N], U32, "c_codes%d" % h)[:], held([P, N], U8, "c_scale%d" % h)[:]) for h in range(HALVES)]
         warm = held([P, 1], F32, "warm")
@@ -150,13 +155,13 @@ def tile_list_sage_gelu_kernel(
 
         pair_up_pieces(0)
         nc.vector.tensor_copy(staged[:, 0 : G * S], pairs[0][:].bitcast(U32).indirect(offsets[:]))
-        nc.vector.transpose(bias[:], bias_rows[:])
         pair_up_pieces(1)
+        nc.vector.transpose(bias, bias_rows[:])
 
-        last_of_scalar = PAIR * (PIECES[1][0] + VECTOR_SHARES[1][1])
+        first_of_scalar = PAIR * VECTOR_SHARES[1][0]
         quantize(
             (idle_codes[:, 0:WARM_ROWS], idle_scale[:, 0:WARM_ROWS]),
-            pairs[1][:, last_of_scalar : last_of_scalar + PACK * WARM_ROWS],
+            pairs[1][:, first_of_scalar : first_of_scalar + PACK * WARM_ROWS],
         )
         for warm_pass in range(WARM_PASSES):
             nc.tensor.matmul_mx(
@@ -189,13 +194,16 @@ def tile_list_sage_gelu_kernel(
             a = 0 if m < FIRST_TILES else 1
             return a, (m - CHUNK_TILES[a].start) * P
 
-        def sums(m, cols):
-            second = m < EARLY and cols == halves[1]
-            return banks[m + EARLY - 1 if second else m][:, cols]
+        order = [(m, 0) for m in range(EARLY)]
+        order = order + [(m, h) for m in range(EARLY, TILES) for h in range(HALVES)]
+        order = order + [(m, 1) for m in range(EARLY)]
+
+        def sums(m, h):
+            return banks[order.index((m, h)) % TILES][:, 0:N]
 
         def w4_pass(m, h, start, stop):
             nc.tensor.matmul_mx(
-                out=sums(m, halves[h]),
+                out=sums(m, h),
                 lhsT=w4[:, 2 * P * m : 2 * P * (m + 1)].bitcast(FP4X4),
                 lhsT_scale=w4_plane[:, m * P : (m + 1) * P],
                 rhs=x_mx[h][0].bitcast(FP8X4),
@@ -207,7 +215,7 @@ def tile_list_sage_gelu_kernel(
         def w8_pass(m, h, start, stop):
             a, first = place(m)
             nc.tensor.matmul_mx(
-                out=sums(m, halves[h]),
+                out=sums(m, h),
                 lhsT=w8[a][:, first : first + P].bitcast(FP8X4),
                 lhsT_scale=w8_plane[m * P // W8_PLANE * SCALE_ROWS : P, m * P % W8_PLANE : m * P % W8_PLANE + P],
                 rhs=c_mx[h][0].bitcast(FP8X4),
@@ -216,39 +224,26 @@ def tile_list_sage_gelu_kernel(
                 stop=stop,
             )
 
-        def gelu(res, m, cols):
-            nc.scalar.activation(res, sums(m, cols), GELU, bias=bias[:, BIAS_STEP * m : BIAS_STEP * m + 1])
-
         out_view = out.rearrange("(m p) j -> p m j", p=P)
-
-        def finish(h, tiles, passes):
-            res = held([P, len(tiles), N], F32, "res%d_%d" % (tiles[0], h))
+        res = {}
+        for i, (tiles, parts) in enumerate(STORES):
+            staged_out = held([P, len(tiles), len(parts) * N], F32, "res%d" % i)
             for m in tiles:
-                passes(m)
-                gelu(res[:, m - tiles[0], :], m, halves[h])
-            nc.sync.dma_start(out_view[:, tiles[0] : tiles[-1] + 1, halves[h]], res[:])
+                for h in parts:
+                    res[(m, h)] = (staged_out, staged_out[:, m - tiles[0], (h - parts[0]) * N : (h - parts[0] + 1) * N])
 
-        def first_half(m):
-            w8_pass(m, 0, m not in AHEAD, m in AHEAD)
-            if m not in AHEAD:
-                w4_pass(m, 0, False, True)
-
-        def second_half(m):
-            w8_pass(m, 1, True, False)
-            w4_pass(m, 1, False, True)
-
-        for m in AHEAD:
-            w4_pass(m, 0, True, False)
-        for tiles in STORES[0]:
-            finish(0, tiles, first_half)
-        for m in range(EARLY, TILES):
-            res = held([P, S], F32, "res%d" % m)
-            w8_pass(m, 0, m not in AHEAD, False)
-            if m not in AHEAD:
-                w4_pass(m, 0, False, False)
-            w8_pass(m, 1, False, False)
-            w4_pass(m, 1, False, True)
-            gelu(res[:], m, slice(0, S))
-            nc.sync.dma_start(out_view[:, m, :], res[:])
-        for tiles in STORES[1]:
-            finish(1, tiles, second_half)
+        for m, h in order[:AHEAD]:
+            w4_pass(m, h, True, False)
+        for i, (m, h) in enumerate(order):
+            if i < AHEAD:
+                w8_pass(m, h, False, True)
+            else:
+                w8_pass(m, h, True, False)
+                w4_pass(m, h, False, True)
+            nc.scalar.activation(
+                res[(m, h)][1], sums(m, h), GELU, bias=bias[:, BIAS_STEP * m : BIAS_STEP * m + 1]
+            )
+            for tiles, parts in STORES:
+                if (m, h) == (tiles[-1], parts[-1]):
+                    rows, cols = slice(tiles[0], m + 1), slice(parts[0] * N, (h + 1) * N)
+                    nc.sync.dma_start(out_view[:, rows, cols], res[(m, h)][0][:])

@@ -33,7 +33,7 @@ PIECES = ((640, 384), (512, 320, 192))
 VECTOR_SHARES = ((416, 256), (336, 128, 192))
 EARLY = 3
 STORES = (
-    [((m,), (0,)) for m in range(EARLY)]
+    [((0,), (0,)), (tuple(range(1, EARLY)), (0,))]
     + [((m,), (0, 1)) for m in range(EARLY, TILES)]
     + [(tuple(range(EARLY)), (1,))]
 )
@@ -67,7 +67,7 @@ def tile_list_sage_gelu_kernel(
         x_woven = [held([P, N * PACK], BF16, "x_woven0")[:], room[:, C_AT - N : C_AT + N].bitcast(BF16)]
         c_woven = [held([P, N * PACK], BF16, "c_woven%d" % h)[:] for h in range(HALVES)]
         w8 = [held([P, P * len(tiles)], U32, "w8_%d" % tiles.start) for tiles in CHUNK_TILES]
-        w4 = held([P, 2 * M], U8, "w4")
+        w4 = [held([P, 2 * P * len(tiles)], U8, "w4_%d" % tiles.start) for tiles in CHUNK_TILES]
         w4_plane = held([P, M], U8, "w4_plane")
         w8_plane = held([P, W8_PLANE], U8, "w8_plane")
         bias_rows = held([P, QUADRANT], F32, "bias_rows")
@@ -86,11 +86,11 @@ def tile_list_sage_gelu_kernel(
         nc.vector.memset(idle[:].bitcast(U32), 0)
         nc.scalar.activation(warm[:], idle[:, (PACK + 1) * BANK :].bitcast(F32), GELU)
 
-        for first in range(0, P, QUADRANT):
-            rows = w8_scales[0][first // QUADRANT * SCALE_ROWS : (first // QUADRANT + 1) * SCALE_ROWS, :]
+        for q in range(P // QUADRANT):
+            w8_rows = w8_scales[0][q * SCALE_ROWS : (q + 1) * SCALE_ROWS, :]
             nc.gpsimd.dma_start(
-                w8_plane[first : first + W8_PLANES * SCALE_ROWS, :].bitcast(I32),
-                rows.bitcast(I32).rearrange("r (a n) -> a r n", a=W8_PLANES),
+                w8_plane[q * QUADRANT : q * QUADRANT + W8_PLANES * SCALE_ROWS, :].bitcast(I32),
+                w8_rows.bitcast(I32).rearrange("r (a n) -> a r n", a=W8_PLANES),
             )
 
         x_view = xT.rearrange("(p i) t -> p (i t)", i=PACK)
@@ -103,16 +103,28 @@ def tile_list_sage_gelu_kernel(
 
         load_pair(0)
         nc.sync.dma_start(offsets[:], offs)
-        nc.sync.dma_start(bias_rows[0:P:BIAS_STEP, :], b.rearrange("(m q a) -> q m a", m=TILES, a=QUADRANT))
+        nc.scalar.dma_start(bias_rows[0:P:BIAS_STEP, :], b.rearrange("(m q a) -> q m a", m=TILES, a=QUADRANT))
         load_pair(1)
         nc.sync.dma_start(c_raw, c.rearrange("(p i) j -> p i j", i=PACK))
-        nc.sync.dma_start(w4[:].bitcast(I32), w4_words[0].bitcast(I32))
+        w8_bytes = w8_words[0].rearrange("p n t -> p (n t)")
+
+        def load_w4(a):
+            tiles = CHUNK_TILES[a]
+            words = w4_words[0][:, 2 * P * tiles.start : 2 * P * tiles.stop]
+            nc.sync.dma_start(w4[a][:].bitcast(I32), words.bitcast(I32))
+
+        def load_w8(a):
+            tiles = CHUNK_TILES[a]
+            words = w8_bytes[:, PACK * P * tiles.start : PACK * P * tiles.stop]
+            nc.sync.dma_start(w8[a][:].bitcast(I32), words.bitcast(I32))
+
+        load_w4(0)
         w4_rows = w4_scales[0].rearrange("(q r) n -> r q n", r=SCALE_ROWS)
         for r in range(SCALE_ROWS):
             nc.sync.dma_start(w4_plane[r:P:QUADRANT, :].bitcast(I32), w4_rows[r].bitcast(I32))
-        w8_bytes = w8_words[0].rearrange("p n t -> p (n t)")
-        for a, tiles in enumerate(CHUNK_TILES):
-            nc.sync.dma_start(w8[a][:].bitcast(I32), w8_bytes[:, 4 * P * tiles.start : 4 * P * tiles.stop].bitcast(I32))
+        load_w8(0)
+        load_w8(1)
+        load_w4(1)
 
         def pair_up(copy, u, first, count):
             copy(
@@ -129,9 +141,8 @@ def tile_list_sage_gelu_kernel(
 
         def gather_high(h, g):
             first = (g * S + h * N) // LIST_ROWS
-            place = HIGH_AT[h][g]
             nc.vector.tensor_copy(
-                staged[:, place : place + N],
+                staged[:, HIGH_AT[h][g] : HIGH_AT[h][g] + N],
                 pairs[1][:].bitcast(U32).indirect(offsets[:, first : first + N // LIST_ROWS]),
             )
 
@@ -188,23 +199,21 @@ def tile_list_sage_gelu_kernel(
         quantize(c_mx[1], c_woven[1])
         quantize(x_mx[1], x_woven[1])
 
-        halves = [slice(h * N, (h + 1) * N) for h in range(HALVES)]
-
         def place(m):
             a = 0 if m < FIRST_TILES else 1
             return a, (m - CHUNK_TILES[a].start) * P
 
-        order = [(m, 0) for m in range(EARLY)]
-        order = order + [(m, h) for m in range(EARLY, TILES) for h in range(HALVES)]
-        order = order + [(m, 1) for m in range(EARLY)]
+        order = [(m, 0) for m in range(FIRST_TILES)] + [(EARLY, 1)] + [(m, 1) for m in range(EARLY)]
+        order = order + [(m, h) for m in CHUNK_TILES[1] for h in range(HALVES)]
 
         def sums(m, h):
             return banks[order.index((m, h)) % TILES][:, 0:N]
 
         def w4_pass(m, h, start, stop):
+            a, first = place(m)
             nc.tensor.matmul_mx(
                 out=sums(m, h),
-                lhsT=w4[:, 2 * P * m : 2 * P * (m + 1)].bitcast(FP4X4),
+                lhsT=w4[a][:, 2 * first : 2 * (first + P)].bitcast(FP4X4),
                 lhsT_scale=w4_plane[:, m * P : (m + 1) * P],
                 rhs=x_mx[h][0].bitcast(FP8X4),
                 rhs_scale=x_mx[h][1],
@@ -214,10 +223,11 @@ def tile_list_sage_gelu_kernel(
 
         def w8_pass(m, h, start, stop):
             a, first = place(m)
+            plane, column = divmod(m * P, W8_PLANE)
             nc.tensor.matmul_mx(
                 out=sums(m, h),
                 lhsT=w8[a][:, first : first + P].bitcast(FP8X4),
-                lhsT_scale=w8_plane[m * P // W8_PLANE * SCALE_ROWS : P, m * P % W8_PLANE : m * P % W8_PLANE + P],
+                lhsT_scale=w8_plane[plane * SCALE_ROWS : P, column : column + P],
                 rhs=c_mx[h][0].bitcast(FP8X4),
                 rhs_scale=c_mx[h][1],
                 start=start,
@@ -225,25 +235,29 @@ def tile_list_sage_gelu_kernel(
             )
 
         out_view = out.rearrange("(m p) j -> p m j", p=P)
-        res = {}
-        for i, (tiles, parts) in enumerate(STORES):
-            staged_out = held([P, len(tiles), len(parts) * N], F32, "res%d" % i)
-            for m in tiles:
-                for h in parts:
-                    res[(m, h)] = (staged_out, staged_out[:, m - tiles[0], (h - parts[0]) * N : (h - parts[0] + 1) * N])
+        results = [held([P, len(tiles), len(parts) * N], F32, "res%d" % i) for i, (tiles, parts) in enumerate(STORES)]
 
-        for m, h in order[:AHEAD]:
-            w4_pass(m, h, True, False)
-        for i, (m, h) in enumerate(order):
-            if i < AHEAD:
-                w8_pass(m, h, False, True)
-            else:
+        def finish(m, h):
+            for res, (tiles, parts) in zip(results, STORES):
+                if m in tiles and h in parts:
+                    part = slice((h - parts[0]) * N, (h - parts[0] + 1) * N)
+                    column = bias[:, BIAS_STEP * m : BIAS_STEP * m + 1]
+                    nc.scalar.activation(res[:, m - tiles[0], part], sums(m, h), GELU, bias=column)
+                    if (m, h) == (tiles[-1], parts[-1]):
+                        nc.sync.dma_start(out_view[:, tiles[0] : m + 1, parts[0] * N : (h + 1) * N], res[:])
+
+        ahead = [order[h * FIRST_TILES : h * FIRST_TILES + AHEAD] for h in range(HALVES)]
+        for m, h in order:
+            early, late = (w4_pass, w8_pass) if h == 0 else (w8_pass, w4_pass)
+            if (m, h) == ahead[h][0]:
+                for opened, half in ahead[h]:
+                    early(opened, half, True, False)
+            if (m, h) in ahead[h]:
+                late(m, h, False, True)
+            elif m < FIRST_TILES:
                 w8_pass(m, h, True, False)
                 w4_pass(m, h, False, True)
-            nc.scalar.activation(
-                res[(m, h)][1], sums(m, h), GELU, bias=bias[:, BIAS_STEP * m : BIAS_STEP * m + 1]
-            )
-            for tiles, parts in STORES:
-                if (m, h) == (tiles[-1], parts[-1]):
-                    rows, cols = slice(tiles[0], m + 1), slice(parts[0] * N, (h + 1) * N)
-                    nc.sync.dma_start(out_view[:, rows, cols], res[(m, h)][0][:])
+            else:
+                w4_pass(m, h, True, False)
+                w8_pass(m, h, False, True)
+            finish(m, h)

@@ -17,7 +17,6 @@ GELU = mybir.ActivationFunctionType.Gelu_apprx_tanh
 
 P = 128
 PACK = 4
-PAIR = 2
 N = 128
 HALVES = S // N
 TILES = M // P
@@ -29,20 +28,15 @@ W8_PLANES = 4
 W8_PLANE = M // W8_PLANES
 FIRST_TILES = 4
 CHUNK_TILES = (range(0, FIRST_TILES), range(FIRST_TILES, TILES))
-PIECES = ((640, 384), (512, 320, 192))
-VECTOR_SHARES = ((416, 256), (336, 128, 192))
-EARLY = 3
-STORES = (
-    [((0,), (0,)), (tuple(range(1, EARLY)), (0,))]
-    + [((m,), (0, 1)) for m in range(EARLY, TILES)]
-    + [(tuple(range(EARLY)), (1,))]
+LEAD = 16
+PICKS = 6 * N
+HIGH_AT = (
+    ((N, 2 * N), (3 * N, 4 * N)),
+    ((LEAD, 5 * N), (3 * N, PICKS)),
 )
+STORES = (((0,), (1, 2), (3, 4), (5, 6, 7)), ((0, 1), (2, 3, 4), (5, 6), (7,)))
 AHEAD = 2
 BIAS_STEP = QUADRANT // TILES
-LEAD = 16
-HIGH_AT = ((G * S, G * S + 3 * N - LEAD), (G * S + N, G * S + 2 * N))
-C_AT = G * S + 5 * N
-ROOM = C_AT + PACK * S
 WARM_PASSES = 3
 WARM_ROWS = 32
 
@@ -59,20 +53,20 @@ def tile_list_sage_gelu_kernel(
             return pool.tile(shape, dtype, name=name, align_bytes=64)
 
         offsets = pool.tile([P, G * S // LIST_ROWS], U16, name="offsets")
-        x_raw = [held([P, PAIR * T], F32, "x_raw%d" % u) for u in range(PACK // PAIR)]
-        pairs = [held([P, T * PAIR], BF16, "pairs%d" % u) for u in range(PACK // PAIR)]
-        room = held([P, ROOM], F32, "room")
-        staged = room[:].bitcast(U32)
-        c_raw = room[:, C_AT:].rearrange("p (i j) -> p i j", i=PACK)
-        x_woven = [held([P, N * PACK], BF16, "x_woven0")[:], room[:, C_AT - N : C_AT + N].bitcast(BF16)]
-        c_woven = [held([P, N * PACK], BF16, "c_woven%d" % h)[:] for h in range(HALVES)]
+        planes = [held([P, T], F32, "plane%d" % i) for i in range(PACK)]
+        low = held([P, 2, G * S], BF16, "low")
+        low_max = held([P, 2, S], BF16, "low_max")
+        room = held([P, PICKS // 2 + PACK * S], F32, "room")
+        high = room[:].bitcast(BF16)
+        c_raw = room[:, PICKS // 2 :].rearrange("p (i j) -> p i j", i=PACK)
+        x_woven = [held([P, N * PACK], BF16, "x_woven%d" % h) for h in range(HALVES)]
+        c_woven = [held([P, N * PACK], BF16, "c_woven%d" % h) for h in range(HALVES)]
         w8 = [held([P, P * len(tiles)], U32, "w8_%d" % tiles.start) for tiles in CHUNK_TILES]
         w4 = [held([P, 2 * P * len(tiles)], U8, "w4_%d" % tiles.start) for tiles in CHUNK_TILES]
         w4_plane = held([P, M], U8, "w4_plane")
         w8_plane = held([P, W8_PLANE], U8, "w8_plane")
         bias_rows = held([P, QUADRANT], F32, "bias_rows")
-        last_of_scalar = PIECES[1][0] + VECTOR_SHARES[1][1]
-        bias = x_raw[1][:, last_of_scalar : last_of_scalar + QUADRANT]
+        bias = c_raw[:, 1, 0:QUADRANT]
         x_mx = [(held([P, N], U32, "x_codes%d" % h)[:], held([P, N], U8, "x_scale%d" % h)[:]) for h in range(HALVES)]
         c_mx = [(held([P, N], U32, "c_codes%d" % h)[:], held([P, N], U8, "c_scale%d" % h)[:]) for h in range(HALVES)]
         warm = held([P, 1], F32, "warm")
@@ -93,18 +87,12 @@ def tile_list_sage_gelu_kernel(
                 w8_rows.bitcast(I32).rearrange("r (a n) -> a r n", a=W8_PLANES),
             )
 
-        x_view = xT.rearrange("(p i) t -> p (i t)", i=PACK)
-
-        def load_pair(u):
-            for a, width in enumerate(PIECES[u]):
-                last = T + sum(PIECES[u][: a + 1])
-                first = last - width if a > 0 else 0
-                nc.sync.dma_start(x_raw[u][:, first:last], x_view[:, u * PAIR * T + first : u * PAIR * T + last])
-
-        load_pair(0)
+        x_view = xT.rearrange("(p i) t -> p i t", i=PACK)
+        nc.sync.dma_start(planes[0][:], x_view[:, 0, :])
         nc.sync.dma_start(offsets[:], offs)
         nc.scalar.dma_start(bias_rows[0:P:BIAS_STEP, :], b.rearrange("(m q a) -> q m a", m=TILES, a=QUADRANT))
-        load_pair(1)
+        for i in range(1, PACK):
+            nc.sync.dma_start(planes[i][:], x_view[:, i, :])
         nc.sync.dma_start(c_raw, c.rearrange("(p i) j -> p i j", i=PACK))
         w8_bytes = w8_words[0].rearrange("p n t -> p (n t)")
 
@@ -126,54 +114,47 @@ def tile_list_sage_gelu_kernel(
         load_w8(1)
         load_w4(1)
 
-        def pair_up(copy, u, first, count):
-            copy(
-                pairs[u][:, PAIR * first : PAIR * (first + count)].rearrange("p (t e) -> p t e", e=PAIR),
-                x_raw[u][:].rearrange("p (e t) -> p t e", e=PAIR)[:, first : first + count, :],
-            )
-
-        def pair_up_pieces(u):
-            for a, width in enumerate(PIECES[u]):
-                first, share = sum(PIECES[u][:a]), VECTOR_SHARES[u][a]
-                pair_up(nc.vector.tensor_copy, u, first, share)
-                if share < width:
-                    pair_up(nc.scalar.copy, u, first + share, width - share)
-
-        def gather_high(h, g):
-            first = (g * S + h * N) // LIST_ROWS
-            nc.vector.tensor_copy(
-                staged[:, HIGH_AT[h][g] : HIGH_AT[h][g] + N],
-                pairs[1][:].bitcast(U32).indirect(offsets[:, first : first + N // LIST_ROWS]),
-            )
-
-        def maximum(h, nodes):
-            sides = []
-            for g in range(G):
-                low, high = g * S + h * N, HIGH_AT[h][g]
-                both = room[:, low : 2 * high - low].bitcast(BF16)
-                sides.append(both.rearrange("p (u j e) -> p j u e", u=PACK // PAIR, e=PAIR)[:, nodes])
-            woven = x_woven[h].rearrange("p (j u e) -> p j u e", u=PACK // PAIR, e=PAIR)
-            nc.vector.tensor_max(woven[:, nodes], sides[0], sides[1])
-
-        def weave(h):
-            nc.scalar.copy(
-                c_woven[h].rearrange("p (a j i) -> p a i j", j=PACK, i=PACK),
-                c_raw[:, :, h * N : (h + 1) * N].rearrange("p i (a j) -> p a i j", j=PACK),
-            )
+        def gather(into, i, first, count):
+            listed = offsets[:, first // LIST_ROWS : (first + count) // LIST_ROWS]
+            nc.vector.tensor_copy(into, planes[i][:].indirect(listed))
 
         def quantize(mx, values):
             nc.vector.quantize_mx(out=mx[0].bitcast(FP8X4), scales=mx[1], in_=values)
 
-        pair_up_pieces(0)
-        nc.vector.tensor_copy(staged[:, 0 : G * S], pairs[0][:].bitcast(U32).indirect(offsets[:]))
-        pair_up_pieces(1)
-        nc.vector.transpose(bias, bias_rows[:])
+        def woven(h):
+            return x_woven[h][:].rearrange("p (j i) -> p j i", i=PACK)
 
-        first_of_scalar = PAIR * VECTOR_SHARES[1][0]
-        quantize(
-            (idle_codes[:, 0:WARM_ROWS], idle_scale[:, 0:WARM_ROWS]),
-            pairs[1][:, first_of_scalar : first_of_scalar + PACK * WARM_ROWS],
-        )
+        def low_maximum(h):
+            nodes = slice(h * N, (h + 1) * N)
+            sides = low[:].rearrange("p e (g j) -> p g e j", g=G)
+            nc.vector.tensor_max(low_max[:, :, nodes], sides[:, 0, :, nodes], sides[:, 1, :, nodes])
+            nc.scalar.copy(woven(h)[:, :, 0:2], low_max[:, :, nodes].rearrange("p e j -> p j e"))
+
+        def gather_high(e, h, g, first, count):
+            at = HIGH_AT[h][g][e] + first
+            gather(high[:, at : at + count], 2 + e, g * S + h * N + first, count)
+
+        def high_maximum(h, first, count):
+            sides = []
+            for low_at, high_at in HIGH_AT[h]:
+                both = high[:, low_at : 2 * high_at - low_at].rearrange("p (e j) -> p j e", e=2)
+                sides.append(both[:, first : first + count, :])
+            nc.vector.tensor_max(woven(h)[:, first : first + count, 2:4], sides[0], sides[1])
+
+        def weave(h):
+            nc.scalar.copy(
+                c_woven[h][:].rearrange("p (a j i) -> p a i j", j=PACK, i=PACK),
+                c_raw[:, :, h * N : (h + 1) * N].rearrange("p i (a j) -> p a i j", j=PACK),
+            )
+
+        gather(low[:, 0, :], 0, 0, G * S)
+        gather(low[:, 1, 0 : S + N], 1, 0, S + N)
+        gather(low[:, 1, S + N :], 1, S + N, N)
+        low_maximum(0)
+        low_maximum(1)
+        gather_high(0, 0, 0, 0, N)
+        gather_high(0, 0, 1, 0, N)
+        quantize((idle_codes[:, 0:WARM_ROWS], idle_scale[:, 0:WARM_ROWS]), high[:, N : N + PACK * WARM_ROWS])
         for warm_pass in range(WARM_PASSES):
             nc.tensor.matmul_mx(
                 out=banks[TILES - 1][0:WARM_ROWS, :],
@@ -184,30 +165,29 @@ def tile_list_sage_gelu_kernel(
                 start=True,
                 stop=True,
             )
-
         weave(0)
         weave(1)
-        gather_high(0, 0)
-        gather_high(0, 1)
-        maximum(0, slice(0, LEAD))
-        maximum(0, slice(LEAD, N))
-        gather_high(1, 0)
-        quantize(x_mx[0], x_woven[0])
-        gather_high(1, 1)
-        quantize(c_mx[0], c_woven[0])
-        maximum(1, slice(0, N))
-        quantize(c_mx[1], c_woven[1])
-        quantize(x_mx[1], x_woven[1])
+        gather_high(1, 0, 0, 0, N)
+        gather_high(1, 0, 1, 0, N)
+        gather_high(1, 1, 0, 0, N)
+        high_maximum(0, 0, LEAD)
+        high_maximum(0, LEAD, N - LEAD)
+        gather_high(0, 1, 0, 0, N)
+        quantize(x_mx[0], x_woven[0][:])
+        gather_high(0, 1, 1, 0, N)
+        quantize(c_mx[0], c_woven[0][:])
+        gather_high(1, 1, 1, 0, N)
+        nc.vector.transpose(bias, bias_rows[:])
+        high_maximum(1, 0, N)
+        quantize(c_mx[1], c_woven[1][:])
+        quantize(x_mx[1], x_woven[1][:])
 
         def place(m):
             a = 0 if m < FIRST_TILES else 1
             return a, (m - CHUNK_TILES[a].start) * P
 
-        order = [(m, 0) for m in range(FIRST_TILES)] + [(EARLY, 1)] + [(m, 1) for m in range(EARLY)]
-        order = order + [(m, h) for m in CHUNK_TILES[1] for h in range(HALVES)]
-
         def sums(m, h):
-            return banks[order.index((m, h)) % TILES][:, 0:N]
+            return banks[(m + h * FIRST_TILES) % TILES][:, 0:N]
 
         def w4_pass(m, h, start, stop):
             a, first = place(m)
@@ -235,29 +215,18 @@ def tile_list_sage_gelu_kernel(
             )
 
         out_view = out.rearrange("(m p) j -> p m j", p=P)
-        results = [held([P, len(tiles), len(parts) * N], F32, "res%d" % i) for i, (tiles, parts) in enumerate(STORES)]
-
-        def finish(m, h):
-            for res, (tiles, parts) in zip(results, STORES):
-                if m in tiles and h in parts:
-                    part = slice((h - parts[0]) * N, (h - parts[0] + 1) * N)
-                    column = bias[:, BIAS_STEP * m : BIAS_STEP * m + 1]
-                    nc.scalar.activation(res[:, m - tiles[0], part], sums(m, h), GELU, bias=column)
-                    if (m, h) == (tiles[-1], parts[-1]):
-                        nc.sync.dma_start(out_view[:, tiles[0] : m + 1, parts[0] * N : (h + 1) * N], res[:])
-
-        ahead = [order[h * FIRST_TILES : h * FIRST_TILES + AHEAD] for h in range(HALVES)]
-        for m, h in order:
+        for h in range(HALVES):
             early, late = (w4_pass, w8_pass) if h == 0 else (w8_pass, w4_pass)
-            if (m, h) == ahead[h][0]:
-                for opened, half in ahead[h]:
-                    early(opened, half, True, False)
-            if (m, h) in ahead[h]:
-                late(m, h, False, True)
-            elif m < FIRST_TILES:
-                w8_pass(m, h, True, False)
-                w4_pass(m, h, False, True)
-            else:
-                w4_pass(m, h, True, False)
-                w8_pass(m, h, False, True)
-            finish(m, h)
+            for m in range(AHEAD):
+                early(m, h, True, False)
+            for tiles in STORES[h]:
+                res = held([P, len(tiles), N], F32, "res%d_%d" % (h, tiles[0]))
+                for m in tiles:
+                    if m >= FIRST_TILES:
+                        early, late = w4_pass, w8_pass
+                    if m >= AHEAD:
+                        early(m, h, True, False)
+                    late(m, h, False, True)
+                    column = bias[:, BIAS_STEP * m : BIAS_STEP * m + 1]
+                    nc.scalar.activation(res[:, m - tiles[0], :], sums(m, h), GELU, bias=column)
+                nc.sync.dma_start(out_view[:, tiles[0] : tiles[-1] + 1, h * N : (h + 1) * N], res[:])

@@ -29,12 +29,19 @@ W8_PLANE = M // W8_PLANES
 FIRST_TILES = 4
 CHUNK_TILES = (range(0, FIRST_TILES), range(FIRST_TILES, TILES))
 LEAD = 16
+PART = 64
 PICKS = 6 * N
 HIGH_AT = (
     ((N, 2 * N), (3 * N, 4 * N)),
-    ((LEAD, 5 * N), (3 * N, PICKS)),
+    ((LEAD, 5 * N), (PICKS, PICKS + N)),
 )
-STORES = (((0,), (1, 2), (3, 4), (5, 6, 7)), ((0, 1), (2, 3, 4), (5, 6), (7,)))
+EARLY = 6
+STORES = (
+    [((0,), (0,)), ((1,), (0,)), ((2, 3), (0,)), ((4, 5), (0,))]
+    + [((m,), (0, 1)) for m in range(EARLY, TILES)]
+    + [((m, m + 1), (1,)) for m in range(0, EARLY, 2)]
+)
+SECOND = (6, 7, 4, 5, 0, 1, 2, 3)
 AHEAD = 2
 BIAS_STEP = QUADRANT // TILES
 WARM_PASSES = 3
@@ -111,8 +118,8 @@ def tile_list_sage_gelu_kernel(
         for r in range(SCALE_ROWS):
             nc.sync.dma_start(w4_plane[r:P:QUADRANT, :].bitcast(I32), w4_rows[r].bitcast(I32))
         load_w8(0)
-        load_w8(1)
         load_w4(1)
+        load_w8(1)
 
         def gather(into, i, first, count):
             listed = offsets[:, first // LIST_ROWS : (first + count) // LIST_ROWS]
@@ -174,11 +181,13 @@ def tile_list_sage_gelu_kernel(
         high_maximum(0, LEAD, N - LEAD)
         gather_high(0, 1, 0, 0, N)
         quantize(x_mx[0], x_woven[0][:])
-        gather_high(0, 1, 1, 0, N)
         quantize(c_mx[0], c_woven[0][:])
-        gather_high(1, 1, 1, 0, N)
         nc.vector.transpose(bias, bias_rows[:])
-        high_maximum(1, 0, N)
+        for first in range(0, N, PART):
+            gather_high(0, 1, 1, first, PART)
+            gather_high(1, 1, 1, first, PART)
+        for first in range(0, N, PART):
+            high_maximum(1, first, PART)
         quantize(c_mx[1], c_woven[1][:])
         quantize(x_mx[1], x_woven[1][:])
 
@@ -215,18 +224,23 @@ def tile_list_sage_gelu_kernel(
             )
 
         out_view = out.rearrange("(m p) j -> p m j", p=P)
-        for h in range(HALVES):
-            early, late = (w4_pass, w8_pass) if h == 0 else (w8_pass, w4_pass)
-            for m in range(AHEAD):
-                early(m, h, True, False)
-            for tiles in STORES[h]:
-                res = held([P, len(tiles), N], F32, "res%d_%d" % (h, tiles[0]))
-                for m in tiles:
-                    if m >= FIRST_TILES:
-                        early, late = w4_pass, w8_pass
-                    if m >= AHEAD:
-                        early(m, h, True, False)
-                    late(m, h, False, True)
+        results = [held([P, len(tiles), len(parts) * N], F32, "res%d" % i) for i, (tiles, parts) in enumerate(STORES)]
+
+        def finish(m, h):
+            for res, (tiles, parts) in zip(results, STORES):
+                if m in tiles and h in parts:
+                    part = slice((h - parts[0]) * N, (h - parts[0] + 1) * N)
                     column = bias[:, BIAS_STEP * m : BIAS_STEP * m + 1]
-                    nc.scalar.activation(res[:, m - tiles[0], :], sums(m, h), GELU, bias=column)
-                nc.sync.dma_start(out_view[:, tiles[0] : tiles[-1] + 1, h * N : (h + 1) * N], res[:])
+                    nc.scalar.activation(res[:, m - tiles[0], part], sums(m, h), GELU, bias=column)
+                    if (m, h) == (tiles[-1], parts[-1]):
+                        nc.sync.dma_start(out_view[:, tiles[0] : m + 1, parts[0] * N : (h + 1) * N], res[:])
+
+        for h, tiles in enumerate((range(TILES), SECOND)):
+            early, late = (w4_pass, w8_pass) if h == 0 else (w8_pass, w4_pass)
+            for m in tiles[:AHEAD]:
+                early(m, h, True, False)
+            for m in tiles:
+                if m not in tiles[:AHEAD]:
+                    early(m, h, True, False)
+                late(m, h, False, True)
+                finish(m, h)

@@ -159,9 +159,9 @@ def tile_list_sage_gelu_kernel(
         gather(low[:, 1, S + N :], 1, S + N, N)
         low_maximum(0)
         low_maximum(1)
+        quantize((idle_codes[:, 0:WARM_ROWS], idle_scale[:, 0:WARM_ROWS]), low_max[:, 0, 0 : PACK * WARM_ROWS])
         gather_high(0, 0, 0, 0, N)
         gather_high(0, 0, 1, 0, N)
-        quantize((idle_codes[:, 0:WARM_ROWS], idle_scale[:, 0:WARM_ROWS]), high[:, N : N + PACK * WARM_ROWS])
         for warm_pass in range(WARM_PASSES):
             nc.tensor.matmul_mx(
                 out=banks[TILES - 1][0:WARM_ROWS, :],

@@ -35,13 +35,15 @@ HIGH_AT = (
     ((N, 2 * N), (3 * N, 4 * N)),
     ((LEAD, 5 * N), (PICKS, PICKS + N)),
 )
-EARLY = 6
+EARLY = 7
 STORES = (
-    [((0,), (0,)), ((1,), (0,)), ((2, 3), (0,)), ((4, 5), (0,))]
-    + [((m,), (0, 1)) for m in range(EARLY, TILES)]
-    + [((m, m + 1), (1,)) for m in range(0, EARLY, 2)]
+    [((0,), (0,))]
+    + [((m, m + 1), (0,)) for m in range(1, EARLY, 2)]
+    + [((EARLY,), (0, 1))]
+    + [((m, m + 1), (1,)) for m in range(1, EARLY, 2)]
+    + [((0,), (1,))]
 )
-SECOND = (6, 7, 4, 5, 0, 1, 2, 3)
+SECOND = (7, 5, 6, 4, 3, 1, 2, 0)
 AHEAD = 2
 BIAS_STEP = QUADRANT // TILES
 WARM_PASSES = 3
@@ -73,7 +75,7 @@ def tile_list_sage_gelu_kernel(
         w4_plane = held([P, M], U8, "w4_plane")
         w8_plane = held([P, W8_PLANE], U8, "w8_plane")
         bias_rows = held([P, QUADRANT], F32, "bias_rows")
-        bias = c_raw[:, 1, 0:QUADRANT]
+        bias = room[:, N - QUADRANT : N]
         x_mx = [(held([P, N], U32, "x_codes%d" % h)[:], held([P, N], U8, "x_scale%d" % h)[:]) for h in range(HALVES)]
         c_mx = [(held([P, N], U32, "c_codes%d" % h)[:], held([P, N], U8, "c_scale%d" % h)[:]) for h in range(HALVES)]
         warm = held([P, 1], F32, "warm")
@@ -181,8 +183,8 @@ def tile_list_sage_gelu_kernel(
         high_maximum(0, LEAD, N - LEAD)
         gather_high(0, 1, 0, 0, N)
         quantize(x_mx[0], x_woven[0][:])
-        quantize(c_mx[0], c_woven[0][:])
         nc.vector.transpose(bias, bias_rows[:])
+        quantize(c_mx[0], c_woven[0][:])
         for first in range(0, N, PART):
             gather_high(0, 1, 1, first, PART)
             gather_high(1, 1, 1, first, PART)
@@ -226,14 +228,18 @@ def tile_list_sage_gelu_kernel(
         out_view = out.rearrange("(m p) j -> p m j", p=P)
         results = [held([P, len(tiles), len(parts) * N], F32, "res%d" % i) for i, (tiles, parts) in enumerate(STORES)]
 
+        done = set()
+
         def finish(m, h):
             for res, (tiles, parts) in zip(results, STORES):
                 if m in tiles and h in parts:
                     part = slice((h - parts[0]) * N, (h - parts[0] + 1) * N)
                     column = bias[:, BIAS_STEP * m : BIAS_STEP * m + 1]
                     nc.scalar.activation(res[:, m - tiles[0], part], sums(m, h), GELU, bias=column)
-                    if (m, h) == (tiles[-1], parts[-1]):
-                        nc.sync.dma_start(out_view[:, tiles[0] : m + 1, parts[0] * N : (h + 1) * N], res[:])
+                    done.add((m, h))
+                    if all((t, part) in done for t in tiles for part in parts):
+                        rows = out_view[:, tiles[0] : tiles[-1] + 1, parts[0] * N : (parts[-1] + 1) * N]
+                        nc.sync.dma_start(rows, res[:])
 
         for h, tiles in enumerate((range(TILES), SECOND)):
             early, late = (w4_pass, w8_pass) if h == 0 else (w8_pass, w4_pass)

@@ -84,9 +84,9 @@ def tile_list_sage_gelu_kernel(
         banks = [psum.tile([P, BANK], F32, name="bank%d" % m) for m in range(TILES)]
 
         nc.vector.memset(bias_rows[:], 0.0)
-        nc.vector.memset(w8_plane[:].bitcast(U32), 0)
-        nc.vector.memset(w4_plane[:].bitcast(U32), 0)
         nc.vector.memset(idle[:].bitcast(U32), 0)
+        nc.vector.memset(w4_plane[:].bitcast(U32), 0)
+        nc.vector.memset(w8_plane[:].bitcast(U32), 0)
         nc.scalar.activation(warm[:], idle[:, (PACK + 1) * BANK :].bitcast(F32), GELU)
 
         for q in range(P // QUADRANT):

@@ -26,7 +26,7 @@ QUADRANT = 32
 SCALE_ROWS = 4
 W8_PLANES = 4
 W8_PLANE = M // W8_PLANES
-FIRST_TILES = 4
+FIRST_TILES = 5
 CHUNK_TILES = (range(0, FIRST_TILES), range(FIRST_TILES, TILES))
 LEAD = 16
 PART = 64
@@ -44,6 +44,7 @@ STORES = (
     + [((0,), (1,))]
 )
 SECOND = (7, 5, 6, 4, 3, 1, 2, 0)
+SECOND_BANKS = (0, 1, 2, 5, 6, 7, 0, 1)
 AHEAD = 2
 BIAS_STEP = QUADRANT // TILES
 WARM_PASSES = 3
@@ -185,8 +186,8 @@ def tile_list_sage_gelu_kernel(
         quantize(x_mx[0], x_woven[0][:])
         nc.vector.transpose(bias, bias_rows[:])
         quantize(c_mx[0], c_woven[0][:])
+        gather_high(0, 1, 1, 0, N)
         for first in range(0, N, PART):
-            gather_high(0, 1, 1, first, PART)
             gather_high(1, 1, 1, first, PART)
         for first in range(0, N, PART):
             high_maximum(1, first, PART)
@@ -198,7 +199,7 @@ def tile_list_sage_gelu_kernel(
             return a, (m - CHUNK_TILES[a].start) * P
 
         def sums(m, h):
-            return banks[(m + h * FIRST_TILES) % TILES][:, 0:N]
+            return banks[SECOND_BANKS[SECOND.index(m)] if h else m][:, 0:N]
 
         def w4_pass(m, h, start, stop):
             a, first = place(m)

@@ -26,15 +26,18 @@ QUADRANT = 32
 SCALE_ROWS = 4
 W8_PLANES = 4
 W8_PLANE = M // W8_PLANES
-FIRST_TILES = 5
-CHUNK_TILES = (range(0, FIRST_TILES), range(FIRST_TILES, TILES))
+
+W4_LOADS = (range(0, 3), range(3, TILES))
+W8_LOADS = (range(0, 5), range(5, TILES))
+
 LEAD = 16
-PART = 64
 PICKS = 6 * N
 HIGH_AT = (
     ((N, 2 * N), (3 * N, 4 * N)),
     ((LEAD, 5 * N), (PICKS, PICKS + N)),
 )
+PART = 64
+
 EARLY = 7
 STORES = (
     [((0,), (0,))]
@@ -45,7 +48,8 @@ STORES = (
 )
 SECOND = (7, 5, 6, 4, 3, 1, 2, 0)
 SECOND_BANKS = (0, 1, 2, 5, 6, 7, 0, 1)
-AHEAD = 2
+AHEAD = (2, 1)
+
 BIAS_STEP = QUADRANT // TILES
 WARM_PASSES = 3
 WARM_ROWS = 32
@@ -71,8 +75,8 @@ def tile_list_sage_gelu_kernel(
         c_raw = room[:, PICKS // 2 :].rearrange("p (i j) -> p i j", i=PACK)
         x_woven = [held([P, N * PACK], BF16, "x_woven%d" % h) for h in range(HALVES)]
         c_woven = [held([P, N * PACK], BF16, "c_woven%d" % h) for h in range(HALVES)]
-        w8 = [held([P, P * len(tiles)], U32, "w8_%d" % tiles.start) for tiles in CHUNK_TILES]
-        w4 = [held([P, 2 * P * len(tiles)], U8, "w4_%d" % tiles.start) for tiles in CHUNK_TILES]
+        w8 = [held([P, P * len(tiles)], U32, "w8_%d" % tiles.start) for tiles in W8_LOADS]
+        w4 = [held([P, 2 * P * len(tiles)], U8, "w4_%d" % tiles.start) for tiles in W4_LOADS]
         w4_plane = held([P, M], U8, "w4_plane")
         w8_plane = held([P, W8_PLANE], U8, "w8_plane")
         bias_rows = held([P, QUADRANT], F32, "bias_rows")
@@ -107,12 +111,12 @@ def tile_list_sage_gelu_kernel(
         w8_bytes = w8_words[0].rearrange("p n t -> p (n t)")
 
         def load_w4(a):
-            tiles = CHUNK_TILES[a]
+            tiles = W4_LOADS[a]
             words = w4_words[0][:, 2 * P * tiles.start : 2 * P * tiles.stop]
             nc.sync.dma_start(w4[a][:].bitcast(I32), words.bitcast(I32))
 
         def load_w8(a):
-            tiles = CHUNK_TILES[a]
+            tiles = W8_LOADS[a]
             words = w8_bytes[:, PACK * P * tiles.start : PACK * P * tiles.stop]
             nc.sync.dma_start(w8[a][:].bitcast(I32), words.bitcast(I32))
 
@@ -128,8 +132,13 @@ def tile_list_sage_gelu_kernel(
             listed = offsets[:, first // LIST_ROWS : (first + count) // LIST_ROWS]
             nc.vector.tensor_copy(into, planes[i][:].indirect(listed))
 
-        def quantize(mx, values):
-            nc.vector.quantize_mx(out=mx[0].bitcast(FP8X4), scales=mx[1], in_=values)
+        def quantize(mx, values, first, count):
+            nodes = slice(first, first + count)
+            nc.vector.quantize_mx(
+                out=mx[0][:, nodes].bitcast(FP8X4),
+                scales=mx[1][:, nodes],
+                in_=values[:, PACK * first : PACK * (first + count)],
+            )
 
         def woven(h):
             return x_woven[h][:].rearrange("p (j i) -> p j i", i=PACK)
@@ -146,8 +155,8 @@ def tile_list_sage_gelu_kernel(
 
         def high_maximum(h, first, count):
             sides = []
-            for low_at, high_at in HIGH_AT[h]:
-                both = high[:, low_at : 2 * high_at - low_at].rearrange("p (e j) -> p j e", e=2)
+            for plane2_at, plane3_at in HIGH_AT[h]:
+                both = high[:, plane2_at : 2 * plane3_at - plane2_at].rearrange("p (e j) -> p j e", e=2)
                 sides.append(both[:, first : first + count, :])
             nc.vector.tensor_max(woven(h)[:, first : first + count, 2:4], sides[0], sides[1])
 
@@ -162,7 +171,7 @@ def tile_list_sage_gelu_kernel(
         gather(low[:, 1, S + N :], 1, S + N, N)
         low_maximum(0)
         low_maximum(1)
-        quantize((idle_codes[:, 0:WARM_ROWS], idle_scale[:, 0:WARM_ROWS]), low_max[:, 0, 0 : PACK * WARM_ROWS])
+        quantize((idle_codes, idle_scale), low_max[:, 0, :], 0, WARM_ROWS)
         gather_high(0, 0, 0, 0, N)
         gather_high(0, 0, 1, 0, N)
         for warm_pass in range(WARM_PASSES):
@@ -183,26 +192,27 @@ def tile_list_sage_gelu_kernel(
         high_maximum(0, 0, LEAD)
         high_maximum(0, LEAD, N - LEAD)
         gather_high(0, 1, 0, 0, N)
-        quantize(x_mx[0], x_woven[0][:])
+        quantize(x_mx[0], x_woven[0], 0, N)
         nc.vector.transpose(bias, bias_rows[:])
-        quantize(c_mx[0], c_woven[0][:])
+        quantize(c_mx[0], c_woven[0], 0, N)
         gather_high(0, 1, 1, 0, N)
         for first in range(0, N, PART):
             gather_high(1, 1, 1, first, PART)
         for first in range(0, N, PART):
             high_maximum(1, first, PART)
-        quantize(c_mx[1], c_woven[1][:])
-        quantize(x_mx[1], x_woven[1][:])
+        quantize(x_mx[1], x_woven[1], 0, PART)
+        quantize(c_mx[1], c_woven[1], 0, N)
+        quantize(x_mx[1], x_woven[1], PART, PART)
 
-        def place(m):
-            a = 0 if m < FIRST_TILES else 1
-            return a, (m - CHUNK_TILES[a].start) * P
+        def place(m, loads):
+            a = 0 if m in loads[0] else 1
+            return a, (m - loads[a].start) * P
 
         def sums(m, h):
             return banks[SECOND_BANKS[SECOND.index(m)] if h else m][:, 0:N]
 
         def w4_pass(m, h, start, stop):
-            a, first = place(m)
+            a, first = place(m, W4_LOADS)
             nc.tensor.matmul_mx(
                 out=sums(m, h),
                 lhsT=w4[a][:, 2 * first : 2 * (first + P)].bitcast(FP4X4),
@@ -214,7 +224,7 @@ def tile_list_sage_gelu_kernel(
             )
 
         def w8_pass(m, h, start, stop):
-            a, first = place(m)
+            a, first = place(m, W8_LOADS)
             plane, column = divmod(m * P, W8_PLANE)
             nc.tensor.matmul_mx(
                 out=sums(m, h),
@@ -234,20 +244,20 @@ def tile_list_sage_gelu_kernel(
         def finish(m, h):
             for res, (tiles, parts) in zip(results, STORES):
                 if m in tiles and h in parts:
-                    part = slice((h - parts[0]) * N, (h - parts[0] + 1) * N)
-                    column = bias[:, BIAS_STEP * m : BIAS_STEP * m + 1]
-                    nc.scalar.activation(res[:, m - tiles[0], part], sums(m, h), GELU, bias=column)
+                    columns = slice((h - parts[0]) * N, (h - parts[0] + 1) * N)
+                    bias_column = bias[:, BIAS_STEP * m : BIAS_STEP * m + 1]
+                    nc.scalar.activation(res[:, m - tiles[0], columns], sums(m, h), GELU, bias=bias_column)
                     done.add((m, h))
-                    if all((t, part) in done for t in tiles for part in parts):
+                    if all((tile, half) in done for tile in tiles for half in parts):
                         rows = out_view[:, tiles[0] : tiles[-1] + 1, parts[0] * N : (parts[-1] + 1) * N]
                         nc.sync.dma_start(rows, res[:])
 
         for h, tiles in enumerate((range(TILES), SECOND)):
             early, late = (w4_pass, w8_pass) if h == 0 else (w8_pass, w4_pass)
-            for m in tiles[:AHEAD]:
+            for m in tiles[: AHEAD[h]]:
                 early(m, h, True, False)
             for m in tiles:
-                if m not in tiles[:AHEAD]:
+                if m not in tiles[: AHEAD[h]]:
                     early(m, h, True, False)
                 late(m, h, False, True)
                 finish(m, h)

from contextlib import ExitStack

import concourse.mybir as mybir

G, K, M, T, S = 2, 512, 1024, 1024, 256
FLOPS = 2 * 2 * K * M * S

F32 = mybir.dt.float32
BF16 = mybir.dt.bfloat16
I32 = mybir.dt.int32
U32 = mybir.dt.uint32
U16 = mybir.dt.uint16
U8 = mybir.dt.uint8
FP8X4 = mybir.dt.float8_e4m3fn_x4
FP4X4 = mybir.dt.float4_e2m1fn_x4
GELU = mybir.ActivationFunctionType.Gelu_apprx_tanh

P = 128
PACK = 4
N = 128
HALVES = S // N
TILES = M // P
BANK = 512
LIST_ROWS = 16
QUADRANT = 32
SCALE_ROWS = 4
W8_PLANES = 4
W8_PLANE = M // W8_PLANES

W4_LOADS = (range(0, 3), range(3, TILES))
W8_LOADS = (range(0, 5), range(5, TILES))

LEAD = 16
PICKS = 6 * N
HIGH_AT = (
    ((N, 2 * N), (3 * N, 4 * N)),
    ((LEAD, 5 * N), (PICKS, PICKS + N)),
)
PART = 64

EARLY = 7
STORES = (
    [((0,), (0,))]
    + [((m, m + 1), (0,)) for m in range(1, EARLY, 2)]
    + [((EARLY,), (0, 1))]
    + [((m, m + 1), (1,)) for m in range(1, EARLY, 2)]
    + [((0,), (1,))]
)
SECOND = (7, 5, 6, 4, 3, 1, 2, 0)
SECOND_BANKS = (0, 1, 2, 5, 6, 7, 0, 1)
AHEAD = (2, 1)

BIAS_STEP = QUADRANT // TILES
WARM_PASSES = 3
WARM_ROWS = 32


def tile_list_sage_gelu_kernel(
    tc, xT, c, w4_words, w4_scales, w8_words, w8_scales, b, offs, out
):
    nc = tc.nc
    with ExitStack() as ctx:
        pool = ctx.enter_context(tc.tile_pool(name="held", bufs=1))
        psum = ctx.enter_context(tc.psum_pool(name="psum", bufs=1))

        def held(shape, dtype, name):
            return pool.tile(shape, dtype, name=name, align_bytes=64)

        offsets = pool.tile([P, G * S // LIST_ROWS], U16, name="offsets")
        planes = [held([P, T], F32, "plane%d" % i) for i in range(PACK)]
        low = held([P, 2, G * S], BF16, "low")
        low_max = held([P, 2, S], BF16, "low_max")
        room = held([P, PICKS // 2 + PACK * S], F32, "room")
        high = room[:].bitcast(BF16)
        c_raw = room[:, PICKS // 2 :].rearrange("p (i j) -> p i j", i=PACK)
        x_woven = [held([P, N * PACK], BF16, "x_woven%d" % h) for h in range(HALVES)]
        c_woven = [held([P, N * PACK], BF16, "c_woven%d" % h) for h in range(HALVES)]
        w8 = [held([P, P * len(tiles)], U32, "w8_%d" % tiles.start) for tiles in W8_LOADS]
        w4 = [held([P, 2 * P * len(tiles)], U8, "w4_%d" % tiles.start) for tiles in W4_LOADS]
        w4_plane = held([P, M], U8, "w4_plane")
        w8_plane = held([P, W8_PLANE], U8, "w8_plane")
        bias_rows = held([P, QUADRANT], F32, "bias_rows")
        bias = room[:, N - QUADRANT : N]
        x_mx = [(held([P, N], U32, "x_codes%d" % h)[:], held([P, N], U8, "x_scale%d" % h)[:]) for h in range(HALVES)]
        c_mx = [(held([P, N], U32, "c_codes%d" % h)[:], held([P, N], U8, "c_scale%d" % h)[:]) for h in range(HALVES)]
        warm = held([P, 1], F32, "warm")
        idle = held([P, (PACK + 1) * BANK + PACK], U8, "idle")
        idle_codes, idle_scale = idle[:, 0 : PACK * BANK].bitcast(U32), idle[:, PACK * BANK : (PACK + 1) * BANK]
        banks = [psum.tile([P, BANK], F32, name="bank%d" % m) for m in range(TILES)]

        nc.vector.memset(bias_rows[:], 0.0)
        nc.vector.memset(idle[:].bitcast(U32), 0)
        nc.vector.memset(w4_plane[:].bitcast(U32), 0)
        nc.vector.memset(w8_plane[:].bitcast(U32), 0)
        nc.scalar.activation(warm[:], idle[:, (PACK + 1) * BANK :].bitcast(F32), GELU)

        for q in range(P // QUADRANT):
            w8_rows = w8_scales[0][q * SCALE_ROWS : (q + 1) * SCALE_ROWS, :]
            nc.gpsimd.dma_start(
                w8_plane[q * QUADRANT : q * QUADRANT + W8_PLANES * SCALE_ROWS, :].bitcast(I32),
                w8_rows.bitcast(I32).rearrange("r (a n) -> a r n", a=W8_PLANES),
            )

        x_view = xT.rearrange("(p i) t -> p i t", i=PACK)
        nc.sync.dma_start(planes[0][:], x_view[:, 0, :])
        nc.sync.dma_start(offsets[:], offs)
        nc.scalar.dma_start(bias_rows[0:P:BIAS_STEP, :], b.rearrange("(m q a) -> q m a", m=TILES, a=QUADRANT))
        for i in range(1, PACK):
            nc.sync.dma_start(planes[i][:], x_view[:, i, :])
        nc.sync.dma_start(c_raw, c.rearrange("(p i) j -> p i j", i=PACK))
        w8_bytes = w8_words[0].rearrange("p n t -> p (n t)")

        def load_w4(a):
            tiles = W4_LOADS[a]
            words = w4_words[0][:, 2 * P * tiles.start : 2 * P * tiles.stop]
            nc.sync.dma_start(w4[a][:].bitcast(I32), words.bitcast(I32))

        def load_w8(a):
            tiles = W8_LOADS[a]
            words = w8_bytes[:, PACK * P * tiles.start : PACK * P * tiles.stop]
            nc.sync.dma_start(w8[a][:].bitcast(I32), words.bitcast(I32))

        load_w4(0)
        w4_rows = w4_scales[0].rearrange("(q r) n -> r q n", r=SCALE_ROWS)
        for r in range(SCALE_ROWS):
            nc.sync.dma_start(w4_plane[r:P:QUADRANT, :].bitcast(I32), w4_rows[r].bitcast(I32))
        load_w8(0)
        load_w4(1)
        load_w8(1)

        def gather(into, i, first, count):
            listed = offsets[:, first // LIST_ROWS : (first + count) // LIST_ROWS]
            nc.vector.tensor_copy(into, planes[i][:].indirect(listed))

        def quantize(mx, values, first, count):
            nodes = slice(first, first + count)
            nc.vector.quantize_mx(
                out=mx[0][:, nodes].bitcast(FP8X4),
                scales=mx[1][:, nodes],
                in_=values[:, PACK * first : PACK * (first + count)],
            )

        def woven(h):
            return x_woven[h][:].rearrange("p (j i) -> p j i", i=PACK)

        def low_maximum(h):
            nodes = slice(h * N, (h + 1) * N)
            sides = low[:].rearrange("p e (g j) -> p g e j", g=G)
            nc.vector.tensor_max(low_max[:, :, nodes], sides[:, 0, :, nodes], sides[:, 1, :, nodes])
            nc.scalar.copy(woven(h)[:, :, 0:2], low_max[:, :, nodes].rearrange("p e j -> p j e"))

        def gather_high(e, h, g, first, count):
            at = HIGH_AT[h][g][e] + first
            gather(high[:, at : at + count], 2 + e, g * S + h * N + first, count)

        def high_maximum(h, first, count):
            sides = []
            for plane2_at, plane3_at in HIGH_AT[h]:
                both = high[:, plane2_at : 2 * plane3_at - plane2_at].rearrange("p (e j) -> p j e", e=2)
                sides.append(both[:, first : first + count, :])
            nc.vector.tensor_max(woven(h)[:, first : first + count, 2:4], sides[0], sides[1])

        def weave(h):
            nc.scalar.copy(
                c_woven[h][:].rearrange("p (a j i) -> p a i j", j=PACK, i=PACK),
                c_raw[:, :, h * N : (h + 1) * N].rearrange("p i (a j) -> p a i j", j=PACK),
            )

        gather(low[:, 0, :], 0, 0, G * S)
        gather(low[:, 1, 0 : S + N], 1, 0, S + N)
        gather(low[:, 1, S + N :], 1, S + N, N)
        low_maximum(0)
        low_maximum(1)
        quantize((idle_codes, idle_scale), low_max[:, 0, :], 0, WARM_ROWS)
        gather_high(0, 0, 0, 0, N)
        gather_high(0, 0, 1, 0, N)
        for warm_pass in range(WARM_PASSES):
            nc.tensor.matmul_mx(
                out=banks[TILES - 1][0:WARM_ROWS, :],
                lhsT=idle_codes[:, 0:WARM_ROWS].bitcast(FP8X4),
                lhsT_scale=idle_scale[:, 0:WARM_ROWS],
                rhs=idle_codes.bitcast(FP8X4),
                rhs_scale=idle_scale,
                start=True,
                stop=True,
            )
        weave(0)
        weave(1)
        gather_high(1, 0, 0, 0, N)
        gather_high(1, 0, 1, 0, N)
        gather_high(1, 1, 0, 0, N)
        high_maximum(0, 0, LEAD)
        high_maximum(0, LEAD, N - LEAD)
        gather_high(0, 1, 0, 0, N)
        quantize(x_mx[0], x_woven[0], 0, N)
        nc.vector.transpose(bias, bias_rows[:])
        quantize(c_mx[0], c_woven[0], 0, N)
        gather_high(0, 1, 1, 0, N)
        for first in range(0, N, PART):
            gather_high(1, 1, 1, first, PART)
        for first in range(0, N, PART):
            high_maximum(1, first, PART)
        quantize(x_mx[1], x_woven[1], 0, PART)
        quantize(c_mx[1], c_woven[1], 0, N)
        quantize(x_mx[1], x_woven[1], PART, PART)

        def place(m, loads):
            a = 0 if m in loads[0] else 1
            return a, (m - loads[a].start) * P

        def sums(m, h):
            return banks[SECOND_BANKS[SECOND.index(m)] if h else m][:, 0:N]

        def w4_pass(m, h, start, stop):
            a, first = place(m, W4_LOADS)
            nc.tensor.matmul_mx(
                out=sums(m, h),
                lhsT=w4[a][:, 2 * first : 2 * (first + P)].bitcast(FP4X4),
                lhsT_scale=w4_plane[:, m * P : (m + 1) * P],
                rhs=x_mx[h][0].bitcast(FP8X4),
                rhs_scale=x_mx[h][1],
                start=start,
                stop=stop,
            )

        def w8_pass(m, h, start, stop):
            a, first = place(m, W8_LOADS)
            plane, column = divmod(m * P, W8_PLANE)
            nc.tensor.matmul_mx(
                out=sums(m, h),
                lhsT=w8[a][:, first : first + P].bitcast(FP8X4),
                lhsT_scale=w8_plane[plane * SCALE_ROWS : P, column : column + P],
                rhs=c_mx[h][0].bitcast(FP8X4),
                rhs_scale=c_mx[h][1],
                start=start,
                stop=stop,
            )

        out_view = out.rearrange("(m p) j -> p m j", p=P)
        results = [held([P, len(tiles), len(parts) * N], F32, "res%d" % i) for i, (tiles, parts) in enumerate(STORES)]

        done = set()

        def finish(m, h):
            for res, (tiles, parts) in zip(results, STORES):
                if m in tiles and h in parts:
                    columns = slice((h - parts[0]) * N, (h - parts[0] + 1) * N)
                    bias_column = bias[:, BIAS_STEP * m : BIAS_STEP * m + 1]
                    nc.scalar.activation(res[:, m - tiles[0], columns], sums(m, h), GELU, bias=bias_column)
                    done.add((m, h))
                    if all((tile, half) in done for tile in tiles for half in parts):
                        rows = out_view[:, tiles[0] : tiles[-1] + 1, parts[0] * N : (parts[-1] + 1) * N]
                        nc.sync.dma_start(rows, res[:])

        for h, tiles in enumerate((range(TILES), SECOND)):
            early, late = (w4_pass, w8_pass) if h == 0 else (w8_pass, w4_pass)
            for m in tiles[: AHEAD[h]]:
                early(m, h, True, False)
            for m in tiles:
                if m not in tiles[: AHEAD[h]]:
                    early(m, h, True, False)
                late(m, h, False, True)
                finish(m, h)
